import numpy as np
import ml_dtypes


def mxq(x, axis, fmt="e4m3"):
    dtype, down = {"e4m3": (ml_dtypes.float8_e4m3fn, 7), "e5m2": (ml_dtypes.float8_e5m2, 14)}[fmt]
    v = np.moveaxis(np.asarray(x, np.float32).astype(ml_dtypes.bfloat16).astype(np.float64), axis, -1)
    blocks = v.reshape(v.shape[:-1] + (-1, 32))
    amax = np.abs(blocks).max(-1, keepdims=True)
    byte = np.maximum(np.where(amax > 0, np.frexp(amax)[1] - 1 + 127, 0) - down, 1)
    scale = np.exp2(byte - 127.0)
    codes = (blocks / scale).astype(np.float32).astype(dtype).astype(np.float64)
    return np.moveaxis((codes * scale).reshape(v.shape), -1, axis)


WIDE = False


def mx_kscale(k):
    if not WIDE:
        return np.ones(k)
    levels = np.array([18, -18])
    if k % 512:
        return np.exp2(np.random.permutation(np.resize(levels, k // 32))).repeat(32)
    a = np.empty((k // 512, 16))
    for p in range(k // 512):
        a[p, :8] = np.random.permutation(np.resize(levels, 8))
        for g in range(8):
            far = levels[np.abs(levels - a[p, g]) >= 10]
            a[p, g + 8] = far[np.random.randint(len(far))]
    return np.exp2(a.ravel()).repeat(32)


def f64(x):
    return np.asarray(x).astype(np.float64)


def striped(idx):
    return np.tile(np.asarray(idx).reshape(-1, 16).T, (8, 1)).astype(np.uint16)


def unstriped(offs):
    return offs[:16].T.reshape(-1).astype(np.int64)


def setup_inputs():
    n = np.random.standard_normal
    uni = np.random.uniform
    idx = np.random.permutation(1024)[:512]
    jdx = np.random.permutation(1024)[:512]
    f_f = mx_kscale(512)
    f_r = mx_kscale(512)
    return {
        "V": (n((512, 512)) / np.sqrt(512) * f_f[:, None]).astype(np.float32),
        "dz": (n((512, 512)) / f_f[:, None]).astype(np.float32),
        "xT": (n((512, 512)) * f_r[None, :]).astype(np.float32),
        "G": (n((512, 512)) / np.sqrt(512) / f_r[:, None]).astype(np.float32),
        "mT": (n((512, 1024))).astype(np.float32),
        "wT": (n((512, 1024))).astype(np.float32),
        "offs": striped(idx),
        "joffs": striped(jdx),
    }


def reference(V, dz, xT, G, mT, wT, offs, joffs):
    idx = unstriped(offs)
    jdx = unstriped(joffs)
    da = mxq(f64(V), 0, "e4m3").T @ mxq(f64(dz), 0, "e5m2")
    db = mxq(f64(xT), 1, "e4m3") @ mxq(f64(G), 0, "e5m2")
    pa = np.zeros((512, 1024))
    pa[:, jdx] = da
    pb = np.zeros((512, 1024))
    pb[:, idx] = db
    out_0 = 0.9 * f64(mT) + pa + pb
    out_1 = f64(wT) - 0.1 * out_0
    return out_0, out_1

@@ -1,0 +1,246 @@
+from contextlib import ExitStack
+
+import concourse.mybir as mybir
+from concourse.masks import make_identity
+
+F32 = mybir.dt.float32
+BF16 = mybir.dt.bfloat16
+U32 = mybir.dt.uint32
+U16 = mybir.dt.uint16
+U8 = mybir.dt.uint8
+E4M3 = mybir.dt.float8_e4m3fn_x4
+E5M2 = mybir.dt.float8_e5m2_x4
+COPY = mybir.ActivationFunctionType.Copy
+MULT = mybir.AluOpType.mult
+ADD = mybir.AluOpType.add
+
+P = 128
+PACK = 4
+K = 512
+D = 512
+SLOTS = 512
+TOKENS = 1024
+HALF = 512
+BLOCKS = D // P
+DECAY = 0.9
+RATE = 0.1
+
+FLOPS = 2 * 2 * K * D * SLOTS
+
+
+def tile_attend_gtied_mom_kernel(tc, V, dz, xT, G, mT, wT, offs, joffs, out_0, out_1):
+    nc = tc.nc
+    with ExitStack() as ctx:
+        keep = ctx.enter_context(tc.tile_pool(name="keep", bufs=1))
+        ring = ctx.enter_context(tc.tile_pool(name="ring", bufs=2))
+        psum = ctx.enter_context(tc.psum_pool(name="psum", bufs=1))
+
+        def load_k_first(src, c0, c1, name):
+            raw = keep.tile([P, PACK, c1 - c0], F32, name=name, tag=name, align_bytes=64)
+            nc.sync.dma_start(out=raw[:], in_=src.rearrange("(p j) n -> p j n", j=PACK)[:, :, c0:c1])
+            return raw
+
+        def load_rows(src, b, name):
+            raw = keep.tile([P, src.shape[1]], F32, name=name, tag=name, align_bytes=64)
+            nc.sync.dma_start(out=raw[:], in_=src[b * P:(b + 1) * P, :])
+            return raw
+
+        def load_list(src, name):
+            lst = keep.tile([P, SLOTS // 16], U16, name=name)
+            nc.sync.dma_start(lst[:], src)
+            return lst
+
+        dz_a = load_k_first(dz, 0, 256, "dz_a")
+        v_0 = load_k_first(V, 0, 128, "v_0")
+        dz_b = load_k_first(dz, 256, 512, "dz_b")
+        v_1 = load_k_first(V, 128, 256, "v_1")
+        j_list = load_list(joffs, "j_list")
+        x_rows = [load_rows(xT, 0, "x_0")]
+        g_a = load_k_first(G, 0, 256, "g_a")
+        g_b = load_k_first(G, 256, 512, "g_b")
+        x_rows.append(load_rows(xT, 1, "x_1"))
+        i_list = load_list(offs, "i_list")
+        x_rows.extend([load_rows(xT, b, "x_%d" % b) for b in range(2, 4)])
+        v_23 = load_k_first(V, 256, 512, "v_23")
+        m_rows = []
+        w_rows = []
+        for b in range(BLOCKS):
+            m_rows.append(load_rows(mT, b, "m_%d" % b))
+            w_rows.append(load_rows(wT, b, "w_%d" % b))
+
+        ident = keep.tile([P, P], F32, name="ident")
+        make_identity(nc, ident[:])
+        pa_win = [keep.tile([P, TOKENS], F32, name="pa_win_%d" % n) for n in range(2)]
+        pb_win = [keep.tile([P, TOKENS], F32, name="pb_win_%d" % n) for n in range(2)]
+        for win in pa_win:
+            nc.vector.memset(win[:], 0.0)
+        for win in pb_win:
+            nc.gpsimd.memset(win[:], 0.0)
+
+        def mx_operand(name, width, tag):
+            codes = keep.tile([P, width], U32, name=name + "_codes", tag=tag, align_bytes=64)
+            scales = keep.tile([P, width], U8, name=name + "_scales", align_bytes=64)
+            return codes, scales
+
+        v_mx, dz_mx, x_mx = [mx_operand(n, 512, n + "_codes") for n in ("v", "dz", "x")]
+
+        def weave(raw, on_vector, name, tag):
+            width = raw.shape[2]
+            woven = keep.tile([P, width, PACK], BF16, name=name, tag=tag, align_bytes=64)
+            dst = woven[:].rearrange("p (c i) t -> p c t i", i=4)
+            src = raw[:].rearrange("p t (c i) -> p c t i", i=4)
+            if on_vector:
+                nc.vector.tensor_copy(out=dst, in_=src)
+            else:
+                nc.scalar.activation(out=dst, in_=src, func=COPY)
+            return woven
+
+        def quantise(woven, operand, c0, fmt):
+            codes, scales = operand
+            cols = slice(c0, c0 + woven.shape[1])
+            nc.vector.quantize_mx(
+                out=codes[:, cols].bitcast(fmt),
+                scales=scales[:, cols],
+                in_=woven[:].rearrange("p n t -> p (n t)"),
+            )
+
+        def bank_pair(tag):
+            return psum.tile([P, 2, HALF], F32, name=tag, tag=tag)
+
+        def mx_bank(tag):
+            return psum.tile([P, SLOTS], F32, name=tag, tag=tag)[:]
+
+        def round_x(b, tag):
+            pairs = keep.tile([P, 2, P, 2], BF16, name="x_pairs_%d" % b, tag=tag, align_bytes=64)
+            nc.scalar.copy(out=pairs[:], in_=x_rows[b][:].rearrange("d (p u e) -> d u p e", u=2, e=2))
+            return pairs[:].rearrange("d u p e -> d (u p e)").bitcast(F32)
+
+        def turn_x(b, words, bank):
+            for u in range(2):
+                nc.tensor.transpose(bank[:, u * P:(u + 1) * P], words[:, u * P:(u + 1) * P], ident[:])
+            woven = keep.tile([P, P, PACK], BF16, name="x_woven_%d" % b, align_bytes=64)
+            nc.scalar.copy(
+                out=woven[:].rearrange("p d t -> p (d t)").bitcast(F32).rearrange("p (d u) -> p d u", u=2),
+                in_=bank[:, 0:2 * P].rearrange("p (u d) -> p d u", u=2),
+            )
+            return woven
+
+        def product(stationary, moving, b, name, bank, on_vector=False, tag=None):
+            cols = slice(b * P, (b + 1) * P)
+            nc.tensor.matmul_mx(
+                out=bank,
+                lhsT=stationary[0][:, cols].bitcast(E4M3),
+                lhsT_scale=stationary[1][:, cols],
+                rhs=moving[0][:].bitcast(E5M2),
+                rhs_scale=moving[1][:],
+                start=True,
+                stop=True,
+            )
+            grad = keep.tile([P, SLOTS], F32, name=name, tag=tag or name, align_bytes=64)
+            if on_vector:
+                nc.vector.tensor_scalar(out=grad[:], in0=bank, scalar1=1.0 / DECAY, scalar2=None, op0=MULT)
+            else:
+                nc.scalar.activation(out=grad[:], in_=bank, func=COPY, scale=1.0 / DECAY)
+            return grad
+
+        def scatter(win, lst, grad):
+            nc.vector.tensor_copy(win[:].indirect(lst[:]), grad[:])
+
+        def turned_sum(addends):
+            turned = bank_pair("turned")
+            back = bank_pair("back")
+            for a, src in enumerate(addends):
+                for n in range(TOKENS // P):
+                    h, c = divmod(n, 4)
+                    nc.tensor.matmul(
+                        turned[:, h, c * P:(c + 1) * P],
+                        lhsT=src[:, n * P:(n + 1) * P],
+                        rhs=ident[:],
+                        is_transpose=True,
+                        start=(a == 0 and c == 0),
+                        stop=(a == len(addends) - 1 and c == 3),
+                    )
+            scaled = []
+            for h in range(2):
+                half = ring.tile([P, HALF], F32, name="scaled", tag="scaled")
+                nc.scalar.activation(out=half[:], in_=turned[:, h, :], func=COPY, scale=DECAY)
+                scaled.append(half)
+            for h in range(2):
+                for c in range(4):
+                    nc.tensor.transpose(back[:, h, c * P:(c + 1) * P], scaled[h][:, c * P:(c + 1) * P], ident[:])
+            return back
+
+        def finish(b):
+            rows = slice(b * P, (b + 1) * P)
+            back = turned_sum([m_rows[b], pa_win[b % 2], pb_win[b % 2]])
+            new_m = keep.tile([P, TOKENS], F32, name="new_m_%d" % b)
+            new_w = keep.tile([P, TOKENS], F32, name="new_w_%d" % b)
+            for h in range(2):
+                cols = slice(h * HALF, (h + 1) * HALF)
+                step = ring.tile([P, HALF], F32, name="step", tag="step")
+                nc.scalar.copy(out=new_m[:, cols], in_=back[:, h, :])
+                nc.scalar.activation(out=step[:], in_=back[:, h, :], func=COPY, scale=-RATE)
+                nc.gpsimd.tensor_tensor(out=new_w[:, cols], in0=w_rows[b][:, cols], in1=step[:], op=ADD)
+            nc.sync.dma_start(out=out_0[rows, :], in_=new_m[:])
+            nc.sync.dma_start(out=out_1[rows, :], in_=new_w[:])
+
+        def finish_last(b, back):
+            rows = slice(b * P, (b + 1) * P)
+            new_m = keep.tile([P, TOKENS], F32, name="new_m_%d" % b)
+            new_w = keep.tile([P, TOKENS], F32, name="new_w_%d" % b)
+            for h in range(2):
+                cols = slice(h * HALF, (h + 1) * HALF)
+                nc.vector.scalar_tensor_tensor(
+                    out=new_m[:, cols], in0=pb_win[b % 2][:, cols], scalar=DECAY, in1=back[:, h, :], op0=MULT, op1=ADD
+                )
+                nc.sync.dma_start(out=out_0[rows, cols], in_=new_m[:, cols])
+            for h in range(2):
+                cols = slice(h * HALF, (h + 1) * HALF)
+                nc.vector.scalar_tensor_tensor(
+                    out=new_w[:, cols], in0=new_m[:, cols], scalar=-RATE, in1=w_rows[b][:, cols], op0=MULT, op1=ADD
+                )
+                nc.sync.dma_start(out=out_1[rows, cols], in_=new_w[:, cols])
+
+        quantise(weave(dz_a, True, "dz_a_woven", "head_woven"), dz_mx, 0, E5M2)
+        quantise(weave(v_0, False, "v_0_woven", "v_0_woven"), v_mx, 0, E4M3)
+        quantise(weave(dz_b, True, "dz_b_woven", "head_woven"), dz_mx, 256, E5M2)
+        v_1_woven = weave(v_1, True, "v_1_woven", "head_woven")
+        da_0 = product(v_mx, dz_mx, 0, "da_0", mx_bank("mx_a"), on_vector=True)
+        quantise(v_1_woven, v_mx, 128, E4M3)
+        scatter(pa_win[0], j_list, da_0)
+
+        g_mx = mx_operand("g", 512, "da_0")
+        x_0_words = round_x(0, "x_pairs_0")
+        g_a_woven = weave(g_a, False, "g_a_woven", "g_a_woven")
+        x_0_woven = turn_x(0, x_0_words, mx_bank("mx_b"))
+        g_b_woven = weave(g_b, False, "g_b_woven", "g_a")
+        quantise(g_a_woven, g_mx, 0, E5M2)
+        quantise(x_0_woven, x_mx, 0, E4M3)
+        quantise(g_b_woven, g_mx, 256, E5M2)
+        da_1 = product(v_mx, dz_mx, 1, "da_1", mx_bank("mx_b"), tag="g_b")
+        scatter(pa_win[1], j_list, da_1)
+
+        quantise(turn_x(1, round_x(1, "x_pairs_1"), mx_bank("mx_a")), x_mx, P, E4M3)
+        db_0 = product(x_mx, g_mx, 0, "db_0", mx_bank("mx_a"))
+        scatter(pb_win[0], i_list, db_0)
+
+        x_2_words = round_x(2, "x_1")
+        x_3_words = round_x(3, "x_2")
+        quantise(turn_x(2, x_2_words, bank_pair("turned")[:, 0, :]), x_mx, 2 * P, E4M3)
+        quantise(turn_x(3, x_3_words, mx_bank("mx_c")), x_mx, 3 * P, E4M3)
+        quantise(weave(v_23, False, "v_23_woven", "x_3"), v_mx, 256, E4M3)
+        db_1 = product(x_mx, g_mx, 1, "db_1", mx_bank("mx_c"), tag="v_23")
+        scatter(pb_win[1], i_list, db_1)
+        da_2 = product(v_mx, dz_mx, 2, "da_2", mx_bank("mx_a"))
+        db_2 = product(x_mx, g_mx, 2, "db_2", mx_bank("mx_c"))
+        finish(0)
+        da_3 = product(v_mx, dz_mx, 3, "da_3", mx_bank("mx_a"))
+        db_3 = product(x_mx, g_mx, 3, "db_3", mx_bank("mx_c"))
+        scatter(pa_win[0], j_list, da_2)
+        scatter(pb_win[0], i_list, db_2)
+        finish(1)
+        scatter(pa_win[1], j_list, da_3)
+        finish(2)
+        partial = turned_sum([m_rows[3], pa_win[1]])
+        scatter(pb_win[1], i_list, db_3)
+        finish_last(3, partial)

@@ -32,7 +32,6 @@ def tile_attend_gtied_mom_kernel(tc, V, dz, xT, G, mT, wT, offs, joffs, out_0, o
     nc = tc.nc
     with ExitStack() as ctx:
         keep = ctx.enter_context(tc.tile_pool(name="keep", bufs=1))
-        ring = ctx.enter_context(tc.tile_pool(name="ring", bufs=2))
         psum = ctx.enter_context(tc.psum_pool(name="psum", bufs=1))
 
         def load_k_first(src, c0, c1, name):
@@ -50,11 +49,11 @@ def tile_attend_gtied_mom_kernel(tc, V, dz, xT, G, mT, wT, offs, joffs, out_0, o
             nc.sync.dma_start(lst[:], src)
             return lst
 
-        dz_a = load_k_first(dz, 0, 256, "dz_a")
         v_0 = load_k_first(V, 0, 128, "v_0")
+        dz_a = load_k_first(dz, 0, 256, "dz_a")
         dz_b = load_k_first(dz, 256, 512, "dz_b")
-        v_1 = load_k_first(V, 128, 256, "v_1")
         j_list = load_list(joffs, "j_list")
+        v_1 = load_k_first(V, 128, 256, "v_1")
         x_rows = [load_rows(xT, 0, "x_0")]
         g_a = load_k_first(G, 0, 256, "g_a")
         g_b = load_k_first(G, 256, 512, "g_b")
@@ -82,7 +81,13 @@ def tile_attend_gtied_mom_kernel(tc, V, dz, xT, G, mT, wT, offs, joffs, out_0, o
             scales = keep.tile([P, width], U8, name=name + "_scales", align_bytes=64)
             return codes, scales
 
-        v_mx, dz_mx, x_mx = [mx_operand(n, 512, n + "_codes") for n in ("v", "dz", "x")]
+        v_mx, x_mx = [mx_operand(n, 512, n + "_codes") for n in ("v", "x")]
+        v_0_mx = mx_operand("v_0", P, "v_0_codes")
+        dz_padded = mx_operand("dz", 768, "dz_codes")
+        for part in dz_padded:
+            nc.vector.memset(part[:, 0:256], 0)
+        dz_early = [part[:, 0:512] for part in dz_padded]
+        dz_mx = [part[:, 256:768] for part in dz_padded]
 
         def weave(raw, on_vector, name, tag):
             width = raw.shape[2]
@@ -125,28 +130,34 @@ def tile_attend_gtied_mom_kernel(tc, V, dz, xT, G, mT, wT, offs, joffs, out_0, o
             )
             return woven
 
-        def product(stationary, moving, b, name, bank, on_vector=False, tag=None):
+        def multiply(stationary, moving, b, bank):
             cols = slice(b * P, (b + 1) * P)
             nc.tensor.matmul_mx(
                 out=bank,
                 lhsT=stationary[0][:, cols].bitcast(E4M3),
                 lhsT_scale=stationary[1][:, cols],
-                rhs=moving[0][:].bitcast(E5M2),
-                rhs_scale=moving[1][:],
+                rhs=moving[0].bitcast(E5M2),
+                rhs_scale=moving[1],
                 start=True,
                 stop=True,
             )
-            grad = keep.tile([P, SLOTS], F32, name=name, tag=tag or name, align_bytes=64)
+            return bank
+
+        def drain(sums, name, tag, on_vector=False, scale=1.0 / DECAY):
+            grad = keep.tile([P, sums.shape[1]], F32, name=name, tag=tag, align_bytes=64)
             if on_vector:
-                nc.vector.tensor_scalar(out=grad[:], in0=bank, scalar1=1.0 / DECAY, scalar2=None, op0=MULT)
+                nc.vector.tensor_scalar(out=grad[:], in0=sums, scalar1=scale, scalar2=None, op0=MULT)
             else:
-                nc.scalar.activation(out=grad[:], in_=bank, func=COPY, scale=1.0 / DECAY)
+                nc.scalar.activation(out=grad[:], in_=sums, func=COPY, scale=scale)
             return grad
 
-        def scatter(win, lst, grad):
-            nc.vector.tensor_copy(win[:].indirect(lst[:]), grad[:])
+        def product(stationary, moving, b, name, bank, tag=None):
+            return drain(multiply(stationary, moving, b, bank), name, tag or name)
 
-        def turned_sum(addends):
+        def scatter(win, lst, grad):
+            nc.vector.tensor_copy(win[:].indirect(lst), grad[:])
+
+        def turned_sum(b, addends):
             turned = bank_pair("turned")
             back = bank_pair("back")
             for a, src in enumerate(addends):
@@ -162,7 +173,7 @@ def tile_attend_gtied_mom_kernel(tc, V, dz, xT, G, mT, wT, offs, joffs, out_0, o
                     )
             scaled = []
             for h in range(2):
-                half = ring.tile([P, HALF], F32, name="scaled", tag="scaled")
+                half = keep.tile([P, HALF], F32, name="scaled_%d_%d" % (b, h), tag="scaled_%d_%d" % (b, h), align_bytes=64)
                 nc.scalar.activation(out=half[:], in_=turned[:, h, :], func=COPY, scale=DECAY)
                 scaled.append(half)
             for h in range(2):
@@ -170,77 +181,94 @@ def tile_attend_gtied_mom_kernel(tc, V, dz, xT, G, mT, wT, offs, joffs, out_0, o
                     nc.tensor.transpose(back[:, h, c * P:(c + 1) * P], scaled[h][:, c * P:(c + 1) * P], ident[:])
             return back
 
-        def finish(b):
+        def add_early(b, tag):
+            both = keep.tile([P, TOKENS], F32, name="m_pa_%d" % b, tag=tag, align_bytes=64)
+            for h in range(2):
+                cols = slice(h * HALF, (h + 1) * HALF)
+                nc.gpsimd.tensor_tensor(out=both[:, cols], in0=m_rows[b][:, cols], in1=pa_win[b % 2][:, cols], op=ADD)
+            return both
+
+        def finish(b, back):
             rows = slice(b * P, (b + 1) * P)
-            back = turned_sum([m_rows[b], pa_win[b % 2], pb_win[b % 2]])
             new_m = keep.tile([P, TOKENS], F32, name="new_m_%d" % b)
             new_w = keep.tile([P, TOKENS], F32, name="new_w_%d" % b)
             for h in range(2):
                 cols = slice(h * HALF, (h + 1) * HALF)
-                step = ring.tile([P, HALF], F32, name="step", tag="step")
+                step = keep.tile([P, HALF], F32, name="step_%d_%d" % (b, h), tag="step_%d_%d" % (b, h), align_bytes=64)
                 nc.scalar.copy(out=new_m[:, cols], in_=back[:, h, :])
                 nc.scalar.activation(out=step[:], in_=back[:, h, :], func=COPY, scale=-RATE)
                 nc.gpsimd.tensor_tensor(out=new_w[:, cols], in0=w_rows[b][:, cols], in1=step[:], op=ADD)
             nc.sync.dma_start(out=out_0[rows, :], in_=new_m[:])
             nc.sync.dma_start(out=out_1[rows, :], in_=new_w[:])
 
-        def finish_last(b, back):
+        def finish_last(b, partial):
             rows = slice(b * P, (b + 1) * P)
-            new_m = keep.tile([P, TOKENS], F32, name="new_m_%d" % b)
+            new_m = keep.tile([P, TOKENS], F32, name="new_m_%d" % b, tag="step_2_1", align_bytes=64)
             new_w = keep.tile([P, TOKENS], F32, name="new_w_%d" % b)
             for h in range(2):
                 cols = slice(h * HALF, (h + 1) * HALF)
-                nc.vector.scalar_tensor_tensor(
-                    out=new_m[:, cols], in0=pb_win[b % 2][:, cols], scalar=DECAY, in1=back[:, h, :], op0=MULT, op1=ADD
-                )
+                nc.vector.tensor_tensor(out=new_m[:, cols], in0=pb_win[b % 2][:, cols], in1=partial[:, cols], op=ADD)
                 nc.sync.dma_start(out=out_0[rows, cols], in_=new_m[:, cols])
-            for h in range(2):
-                cols = slice(h * HALF, (h + 1) * HALF)
+            for cols in (slice(0, 512), slice(512, 768), slice(768, 1024)):
                 nc.vector.scalar_tensor_tensor(
                     out=new_w[:, cols], in0=new_m[:, cols], scalar=-RATE, in1=w_rows[b][:, cols], op0=MULT, op1=ADD
                 )
                 nc.sync.dma_start(out=out_1[rows, cols], in_=new_w[:, cols])
 
-        quantise(weave(dz_a, True, "dz_a_woven", "head_woven"), dz_mx, 0, E5M2)
-        quantise(weave(v_0, False, "v_0_woven", "v_0_woven"), v_mx, 0, E4M3)
-        quantise(weave(dz_b, True, "dz_b_woven", "head_woven"), dz_mx, 256, E5M2)
-        v_1_woven = weave(v_1, True, "v_1_woven", "head_woven")
-        da_0 = product(v_mx, dz_mx, 0, "da_0", mx_bank("mx_a"), on_vector=True)
-        quantise(v_1_woven, v_mx, 128, E4M3)
-        scatter(pa_win[0], j_list, da_0)
+        quantise(weave(v_0, False, "v_0_woven", "v_0_woven"), v_0_mx, 0, E4M3)
+        quantise(weave(dz_a, True, "dz_a_woven", "head_woven"), dz_padded, 256, E5M2)
+        early = multiply(v_0_mx, dz_early, 0, mx_bank("mx_d"))
+        dz_b_woven = weave(dz_b, True, "dz_b_woven", "head_woven")
+        da_0a = drain(early[:, 256:512], "da_0a", "da_0a", on_vector=True)
+        quantise(dz_b_woven, dz_padded, 512, E5M2)
+        scatter(pa_win[0], j_list[:, 0:16], da_0a)
+        da_0b = drain(multiply(v_0_mx, dz_mx, 0, mx_bank("mx_a"))[:, 256:512], "da_0b", "da_0b")
+        quantise(weave(v_1, False, "v_1_woven", "v_1_woven"), v_mx, 128, E4M3)
+        scatter(pa_win[0], j_list[:, 16:32], da_0b)
+        sums_1 = multiply(v_mx, dz_mx, 1, mx_bank("mx_d"))
+        scatter(pa_win[1], j_list[:, 0:16], drain(sums_1[:, 0:256], "da_1a", "da_1a"))
 
-        g_mx = mx_operand("g", 512, "da_0")
+        g_tiles = mx_operand("g", 512, "da_0b")
+        g_mx = [part[:] for part in g_tiles]
         x_0_words = round_x(0, "x_pairs_0")
-        g_a_woven = weave(g_a, False, "g_a_woven", "g_a_woven")
+        g_a_woven = weave(g_a, False, "g_a_woven", "v_0_codes")
         x_0_woven = turn_x(0, x_0_words, mx_bank("mx_b"))
         g_b_woven = weave(g_b, False, "g_b_woven", "g_a")
-        quantise(g_a_woven, g_mx, 0, E5M2)
-        quantise(x_0_woven, x_mx, 0, E4M3)
-        quantise(g_b_woven, g_mx, 256, E5M2)
-        da_1 = product(v_mx, dz_mx, 1, "da_1", mx_bank("mx_b"), tag="g_b")
-        scatter(pa_win[1], j_list, da_1)
+        quantise(g_a_woven, g_tiles, 0, E5M2)
+        x_0_mx = mx_operand("x_0", P, "x_0_codes")
+        quantise(x_0_woven, x_0_mx, 0, E4M3)
+        quantise(g_b_woven, g_tiles, 256, E5M2)
+        scatter(pa_win[1], j_list[:, 16:32], drain(sums_1[:, 256:512], "da_1b", "g_b"))
 
-        quantise(turn_x(1, round_x(1, "x_pairs_1"), mx_bank("mx_a")), x_mx, P, E4M3)
-        db_0 = product(x_mx, g_mx, 0, "db_0", mx_bank("mx_a"))
-        scatter(pb_win[0], i_list, db_0)
+        x_1_words = round_x(1, "x_pairs_1")
+        sums_0 = multiply(x_0_mx, g_mx, 0, mx_bank("mx_b"))
+        scatter(pb_win[0], i_list[:, 0:16], drain(sums_0[:, 0:256], "db_0a", "db_0a"))
+        quantise(turn_x(1, x_1_words, mx_bank("mx_a")), x_mx, P, E4M3)
+        scatter(pb_win[0], i_list[:, 16:32], drain(sums_0[:, 256:512], "db_0b", "x_pairs_1"))
 
-        x_2_words = round_x(2, "x_1")
+        x_2_words = round_x(2, "x_0_codes")
         x_3_words = round_x(3, "x_2")
         quantise(turn_x(2, x_2_words, bank_pair("turned")[:, 0, :]), x_mx, 2 * P, E4M3)
         quantise(turn_x(3, x_3_words, mx_bank("mx_c")), x_mx, 3 * P, E4M3)
         quantise(weave(v_23, False, "v_23_woven", "x_3"), v_mx, 256, E4M3)
         db_1 = product(x_mx, g_mx, 1, "db_1", mx_bank("mx_c"), tag="v_23")
-        scatter(pb_win[1], i_list, db_1)
+        scatter(pb_win[1], i_list[:], db_1)
+        m_pa_1 = add_early(1, "x_3")
+        sum_0 = turned_sum(0, [m_rows[0], pa_win[0], pb_win[0]])
         da_2 = product(v_mx, dz_mx, 2, "da_2", mx_bank("mx_a"))
-        db_2 = product(x_mx, g_mx, 2, "db_2", mx_bank("mx_c"))
-        finish(0)
-        da_3 = product(v_mx, dz_mx, 3, "da_3", mx_bank("mx_a"))
-        db_3 = product(x_mx, g_mx, 3, "db_3", mx_bank("mx_c"))
-        scatter(pa_win[0], j_list, da_2)
-        scatter(pb_win[0], i_list, db_2)
-        finish(1)
-        scatter(pa_win[1], j_list, da_3)
-        finish(2)
-        partial = turned_sum([m_rows[3], pa_win[1]])
-        scatter(pb_win[1], i_list, db_3)
+        finish(0, sum_0)
+        db_2 = product(x_mx, g_mx, 2, "db_2", mx_bank("mx_a"))
+        da_3 = drain(multiply(v_mx, dz_mx, 3, mx_bank("mx_c")), "da_3", "scaled_0_1", scale=1.0)
+        db_3 = drain(multiply(x_mx, g_mx, 3, mx_bank("mx_c")), "db_3", "db_3", scale=1.0)
+        scatter(pa_win[0], j_list[:], da_2)
+        scatter(pb_win[0], i_list[:], db_2)
+        m_pa_2 = add_early(2, "step_0_1")
+        finish(1, turned_sum(1, [m_pa_1, pb_win[1]]))
+        scatter(pa_win[1], j_list[:], da_3)
+        partial = keep.tile([P, TOKENS], F32, name="partial")
+        nc.vector.scalar_tensor_tensor(
+            out=partial[:], in0=m_rows[3][:], scalar=DECAY, in1=pa_win[1][:], op0=MULT, op1=ADD
+        )
+        finish(2, turned_sum(2, [m_pa_2, pb_win[0]]))
+        scatter(pb_win[1], i_list[:], db_3)
         finish_last(3, partial)

@@ -89,12 +89,12 @@ def tile_attend_gtied_mom_kernel(tc, V, dz, xT, G, mT, wT, offs, joffs, out_0, o
         dz_early = [part[:, 0:512] for part in dz_padded]
         dz_mx = [part[:, 256:768] for part in dz_padded]
 
-        def weave(raw, on_vector, name, tag):
+        def weave(raw, engine, name, tag):
             width = raw.shape[2]
             woven = keep.tile([P, width, PACK], BF16, name=name, tag=tag, align_bytes=64)
             dst = woven[:].rearrange("p (c i) t -> p c t i", i=4)
             src = raw[:].rearrange("p t (c i) -> p c t i", i=4)
-            if on_vector:
+            if engine == "vector":
                 nc.vector.tensor_copy(out=dst, in_=src)
             else:
                 nc.scalar.activation(out=dst, in_=src, func=COPY)
@@ -123,7 +123,7 @@ def tile_attend_gtied_mom_kernel(tc, V, dz, xT, G, mT, wT, offs, joffs, out_0, o
         def turn_x(b, words, bank):
             for u in range(2):
                 nc.tensor.transpose(bank[:, u * P:(u + 1) * P], words[:, u * P:(u + 1) * P], ident[:])
-            woven = keep.tile([P, P, PACK], BF16, name="x_woven_%d" % b, align_bytes=64)
+            woven = keep.tile([P, P, PACK], BF16, name="x_woven_%d" % b, tag="x_woven_%d" % b, align_bytes=64)
             nc.scalar.copy(
                 out=woven[:].rearrange("p d t -> p (d t)").bitcast(F32).rearrange("p (d u) -> p d u", u=2),
                 in_=bank[:, 0:2 * P].rearrange("p (u d) -> p d u", u=2),
@@ -157,26 +157,26 @@ def tile_attend_gtied_mom_kernel(tc, V, dz, xT, G, mT, wT, offs, joffs, out_0, o
         def scatter(win, lst, grad):
             nc.vector.tensor_copy(win[:].indirect(lst), grad[:])
 
-        def turned_sum(b, addends):
+        def turned_sum(b, addends, halves, scale):
             turned = bank_pair("turned")
             back = bank_pair("back")
             for a, src in enumerate(addends):
-                for n in range(TOKENS // P):
-                    h, c = divmod(n, 4)
-                    nc.tensor.matmul(
-                        turned[:, h, c * P:(c + 1) * P],
-                        lhsT=src[:, n * P:(n + 1) * P],
-                        rhs=ident[:],
-                        is_transpose=True,
-                        start=(a == 0 and c == 0),
-                        stop=(a == len(addends) - 1 and c == 3),
-                    )
-            scaled = []
-            for h in range(2):
-                half = keep.tile([P, HALF], F32, name="scaled_%d_%d" % (b, h), tag="scaled_%d_%d" % (b, h), align_bytes=64)
-                nc.scalar.activation(out=half[:], in_=turned[:, h, :], func=COPY, scale=DECAY)
-                scaled.append(half)
-            for h in range(2):
+                for h in halves:
+                    for c in range(4):
+                        nc.tensor.matmul(
+                            turned[:, h, c * P:(c + 1) * P],
+                            lhsT=src[:, h * HALF + c * P:h * HALF + (c + 1) * P],
+                            rhs=ident[:],
+                            is_transpose=True,
+                            start=(a == 0 and c == 0),
+                            stop=(a == len(addends) - 1 and c == 3),
+                        )
+            scaled = {}
+            for h in halves:
+                tag = "scaled_%d_%d" % (b, h)
+                scaled[h] = keep.tile([P, HALF], F32, name=tag, tag=tag, align_bytes=64)
+                nc.scalar.activation(out=scaled[h][:], in_=turned[:, h, :], func=COPY, scale=scale)
+            for h in halves:
                 for c in range(4):
                     nc.tensor.transpose(back[:, h, c * P:(c + 1) * P], scaled[h][:, c * P:(c + 1) * P], ident[:])
             return back
@@ -195,8 +195,8 @@ def tile_attend_gtied_mom_kernel(tc, V, dz, xT, G, mT, wT, offs, joffs, out_0, o
             for h in range(2):
                 cols = slice(h * HALF, (h + 1) * HALF)
                 step = keep.tile([P, HALF], F32, name="step_%d_%d" % (b, h), tag="step_%d_%d" % (b, h), align_bytes=64)
-                nc.scalar.copy(out=new_m[:, cols], in_=back[:, h, :])
                 nc.scalar.activation(out=step[:], in_=back[:, h, :], func=COPY, scale=-RATE)
+                nc.scalar.copy(out=new_m[:, cols], in_=back[:, h, :])
                 nc.gpsimd.tensor_tensor(out=new_w[:, cols], in0=w_rows[b][:, cols], in1=step[:], op=ADD)
             nc.sync.dma_start(out=out_0[rows, :], in_=new_m[:])
             nc.sync.dma_start(out=out_1[rows, :], in_=new_w[:])
@@ -207,7 +207,7 @@ def tile_attend_gtied_mom_kernel(tc, V, dz, xT, G, mT, wT, offs, joffs, out_0, o
             new_w = keep.tile([P, TOKENS], F32, name="new_w_%d" % b)
             for h in range(2):
                 cols = slice(h * HALF, (h + 1) * HALF)
-                nc.vector.tensor_tensor(out=new_m[:, cols], in0=pb_win[b % 2][:, cols], in1=partial[:, cols], op=ADD)
+                nc.vector.tensor_tensor(out=new_m[:, cols], in0=pb_win[b % 2][:, cols], in1=partial[h], op=ADD)
                 nc.sync.dma_start(out=out_0[rows, cols], in_=new_m[:, cols])
             for cols in (slice(0, 512), slice(512, 768), slice(768, 1024)):
                 nc.vector.scalar_tensor_tensor(
@@ -215,15 +215,15 @@ def tile_attend_gtied_mom_kernel(tc, V, dz, xT, G, mT, wT, offs, joffs, out_0, o
                 )
                 nc.sync.dma_start(out=out_1[rows, cols], in_=new_w[:, cols])
 
-        quantise(weave(v_0, False, "v_0_woven", "v_0_woven"), v_0_mx, 0, E4M3)
-        quantise(weave(dz_a, True, "dz_a_woven", "head_woven"), dz_padded, 256, E5M2)
+        quantise(weave(v_0, "scalar", "v_0_woven", "v_0_woven"), v_0_mx, 0, E4M3)
+        quantise(weave(dz_a, "vector", "dz_a_woven", "head_woven"), dz_padded, 256, E5M2)
         early = multiply(v_0_mx, dz_early, 0, mx_bank("mx_d"))
-        dz_b_woven = weave(dz_b, True, "dz_b_woven", "head_woven")
+        dz_b_woven = weave(dz_b, "vector", "dz_b_woven", "head_woven")
         da_0a = drain(early[:, 256:512], "da_0a", "da_0a", on_vector=True)
         quantise(dz_b_woven, dz_padded, 512, E5M2)
         scatter(pa_win[0], j_list[:, 0:16], da_0a)
         da_0b = drain(multiply(v_0_mx, dz_mx, 0, mx_bank("mx_a"))[:, 256:512], "da_0b", "da_0b")
-        quantise(weave(v_1, False, "v_1_woven", "v_1_woven"), v_mx, 128, E4M3)
+        quantise(weave(v_1, "scalar", "v_1_woven", "v_1_woven"), v_mx, 128, E4M3)
         scatter(pa_win[0], j_list[:, 16:32], da_0b)
         sums_1 = multiply(v_mx, dz_mx, 1, mx_bank("mx_d"))
         scatter(pa_win[1], j_list[:, 0:16], drain(sums_1[:, 0:256], "da_1a", "da_1a"))
@@ -231,9 +231,9 @@ def tile_attend_gtied_mom_kernel(tc, V, dz, xT, G, mT, wT, offs, joffs, out_0, o
         g_tiles = mx_operand("g", 512, "da_0b")
         g_mx = [part[:] for part in g_tiles]
         x_0_words = round_x(0, "x_pairs_0")
-        g_a_woven = weave(g_a, False, "g_a_woven", "v_0_codes")
+        g_a_woven = weave(g_a, "scalar", "g_a_woven", "v_0_codes")
         x_0_woven = turn_x(0, x_0_words, mx_bank("mx_b"))
-        g_b_woven = weave(g_b, False, "g_b_woven", "g_a")
+        g_b_woven = weave(g_b, "scalar", "g_b_woven", "g_a")
         quantise(g_a_woven, g_tiles, 0, E5M2)
         x_0_mx = mx_operand("x_0", P, "x_0_codes")
         quantise(x_0_woven, x_0_mx, 0, E4M3)
@@ -250,11 +250,11 @@ def tile_attend_gtied_mom_kernel(tc, V, dz, xT, G, mT, wT, offs, joffs, out_0, o
         x_3_words = round_x(3, "x_2")
         quantise(turn_x(2, x_2_words, bank_pair("turned")[:, 0, :]), x_mx, 2 * P, E4M3)
         quantise(turn_x(3, x_3_words, mx_bank("mx_c")), x_mx, 3 * P, E4M3)
-        quantise(weave(v_23, False, "v_23_woven", "x_3"), v_mx, 256, E4M3)
+        quantise(weave(v_23, "scalar", "v_23_woven", "x_3"), v_mx, 256, E4M3)
         db_1 = product(x_mx, g_mx, 1, "db_1", mx_bank("mx_c"), tag="v_23")
         scatter(pb_win[1], i_list[:], db_1)
         m_pa_1 = add_early(1, "x_3")
-        sum_0 = turned_sum(0, [m_rows[0], pa_win[0], pb_win[0]])
+        sum_0 = turned_sum(0, [m_rows[0], pa_win[0], pb_win[0]], (0, 1), DECAY)
         da_2 = product(v_mx, dz_mx, 2, "da_2", mx_bank("mx_a"))
         finish(0, sum_0)
         db_2 = product(x_mx, g_mx, 2, "db_2", mx_bank("mx_a"))
@@ -263,12 +263,15 @@ def tile_attend_gtied_mom_kernel(tc, V, dz, xT, G, mT, wT, offs, joffs, out_0, o
         scatter(pa_win[0], j_list[:], da_2)
         scatter(pb_win[0], i_list[:], db_2)
         m_pa_2 = add_early(2, "step_0_1")
-        finish(1, turned_sum(1, [m_pa_1, pb_win[1]]))
+        finish(1, turned_sum(1, [m_pa_1, pb_win[1]], (0, 1), DECAY))
         scatter(pa_win[1], j_list[:], da_3)
-        partial = keep.tile([P, TOKENS], F32, name="partial")
+        low = keep.tile([P, HALF], F32, name="low")
         nc.vector.scalar_tensor_tensor(
-            out=partial[:], in0=m_rows[3][:], scalar=DECAY, in1=pa_win[1][:], op0=MULT, op1=ADD
+            out=low[:], in0=m_rows[3][:, 0:HALF], scalar=DECAY, in1=pa_win[1][:, 0:HALF], op0=MULT, op1=ADD
         )
-        finish(2, turned_sum(2, [m_pa_2, pb_win[0]]))
+        decayed = keep.tile([P, TOKENS], F32, name="decayed", tag="scaled_1_1", align_bytes=64)
+        nc.scalar.activation(out=decayed[:, HALF:], in_=m_rows[3][:, HALF:], func=COPY, scale=DECAY)
+        finish(2, turned_sum(2, [m_pa_2, pb_win[0]], (0, 1), DECAY))
+        high = turned_sum(3, [decayed, pa_win[1]], (1,), 1.0)[:, 1, :]
         scatter(pb_win[1], i_list[:], db_3)
-        finish_last(3, partial)
+        finish_last(3, [low[:], high])

@@ -20,7 +20,7 @@ K = 512
 D = 512
 SLOTS = 512
 TOKENS = 1024
-HALF = 512
+HALF = 256
 BLOCKS = D // P
 DECAY = 0.9
 RATE = 0.1
@@ -49,49 +49,46 @@ def tile_attend_gtied_mom_kernel(tc, V, dz, xT, G, mT, wT, offs, joffs, out_0, o
             nc.sync.dma_start(lst[:], src)
             return lst
 
-        v_0 = load_k_first(V, 0, 128, "v_0")
+        x_rows, m_rows, w_rows = {}, {}, {}
+        v_01 = load_k_first(V, 0, 256, "v_01")
         dz_a = load_k_first(dz, 0, 256, "dz_a")
-        dz_b = load_k_first(dz, 256, 512, "dz_b")
         j_list = load_list(joffs, "j_list")
-        v_1 = load_k_first(V, 128, 256, "v_1")
-        x_rows = [load_rows(xT, 0, "x_0")]
+        dz_b = load_k_first(dz, 256, 512, "dz_b")
+        x_rows[0] = load_rows(xT, 0, "x_0")
         g_a = load_k_first(G, 0, 256, "g_a")
         g_b = load_k_first(G, 256, 512, "g_b")
-        x_rows.append(load_rows(xT, 1, "x_1"))
         i_list = load_list(offs, "i_list")
-        x_rows.extend([load_rows(xT, b, "x_%d" % b) for b in range(2, 4)])
+        x_rows[1] = load_rows(xT, 1, "x_1")
         v_23 = load_k_first(V, 256, 512, "v_23")
-        m_rows = []
-        w_rows = []
-        for b in range(BLOCKS):
-            m_rows.append(load_rows(mT, b, "m_%d" % b))
-            w_rows.append(load_rows(wT, b, "w_%d" % b))
+        for b in (0, 1):
+            m_rows[b] = load_rows(mT, b, "m_%d" % b)
+        for b in (2, 3):
+            x_rows[b] = load_rows(xT, b, "x_%d" % b)
+        for b in (0, 1):
+            w_rows[b] = load_rows(wT, b, "w_%d" % b)
+        for b in (2, 3):
+            m_rows[b] = load_rows(mT, b, "m_%d" % b)
+        for b in (2, 3):
+            w_rows[b] = load_rows(wT, b, "w_%d" % b)
 
         ident = keep.tile([P, P], F32, name="ident")
         make_identity(nc, ident[:])
         pa_win = [keep.tile([P, TOKENS], F32, name="pa_win_%d" % n) for n in range(2)]
         pb_win = [keep.tile([P, TOKENS], F32, name="pb_win_%d" % n) for n in range(2)]
-        for win in pa_win:
-            nc.vector.memset(win[:], 0.0)
-        for win in pb_win:
-            nc.gpsimd.memset(win[:], 0.0)
+        for n in range(2):
+            nc.vector.memset(pa_win[n][:], 0.0)
+            nc.gpsimd.memset(pb_win[n][:], 0.0)
 
-        def mx_operand(name, width, tag):
-            codes = keep.tile([P, width], U32, name=name + "_codes", tag=tag, align_bytes=64)
-            scales = keep.tile([P, width], U8, name=name + "_scales", align_bytes=64)
+        def mx_operand(name):
+            codes = keep.tile([P, SLOTS], U32, name=name + "_codes", align_bytes=64)
+            scales = keep.tile([P, SLOTS], U8, name=name + "_scales", align_bytes=64)
             return codes, scales
 
-        v_mx, x_mx = [mx_operand(n, 512, n + "_codes") for n in ("v", "x")]
-        v_0_mx = mx_operand("v_0", P, "v_0_codes")
-        dz_padded = mx_operand("dz", 768, "dz_codes")
-        for part in dz_padded:
-            nc.vector.memset(part[:, 0:256], 0)
-        dz_early = [part[:, 0:512] for part in dz_padded]
-        dz_mx = [part[:, 256:768] for part in dz_padded]
+        v_mx, x_mx, dz_mx, g_mx = [mx_operand(n) for n in ("v", "x", "dz", "g")]
 
-        def weave(raw, engine, name, tag):
+        def weave(raw, engine, name):
             width = raw.shape[2]
-            woven = keep.tile([P, width, PACK], BF16, name=name, tag=tag, align_bytes=64)
+            woven = keep.tile([P, width, PACK], BF16, name=name, align_bytes=64)
             dst = woven[:].rearrange("p (c i) t -> p c t i", i=4)
             src = raw[:].rearrange("p t (c i) -> p c t i", i=4)
             if engine == "vector":
@@ -109,169 +106,118 @@ def tile_attend_gtied_mom_kernel(tc, V, dz, xT, G, mT, wT, offs, joffs, out_0, o
                 in_=woven[:].rearrange("p n t -> p (n t)"),
             )
 
-        def bank_pair(tag):
-            return psum.tile([P, 2, HALF], F32, name=tag, tag=tag)
+        def bank(tag):
+            return psum.tile([P, SLOTS], F32, name=tag, tag=tag)
 
-        def mx_bank(tag):
-            return psum.tile([P, SLOTS], F32, name=tag, tag=tag)[:]
+        def turn_x(b, tag):
+            turned = bank(tag)
+            rows = x_rows[b][:].rearrange("d (p t) -> d t p", t=PACK)
+            for t in range(PACK):
+                nc.tensor.transpose(turned[:, t * P:(t + 1) * P], rows[:, t, :], ident[:])
+            woven = keep.tile([P, P, PACK], BF16, name="x_woven_%d" % b, align_bytes=64)
+            nc.vector.tensor_copy(out=woven[:], in_=turned[:].rearrange("p (t d) -> p d t", t=PACK))
+            quantise(woven, x_mx, b * P, E4M3)
 
-        def round_x(b, tag):
-            pairs = keep.tile([P, 2, P, 2], BF16, name="x_pairs_%d" % b, tag=tag, align_bytes=64)
-            nc.scalar.copy(out=pairs[:], in_=x_rows[b][:].rearrange("d (p u e) -> d u p e", u=2, e=2))
-            return pairs[:].rearrange("d u p e -> d (u p e)").bitcast(F32)
-
-        def turn_x(b, words, bank):
-            for u in range(2):
-                nc.tensor.transpose(bank[:, u * P:(u + 1) * P], words[:, u * P:(u + 1) * P], ident[:])
-            woven = keep.tile([P, P, PACK], BF16, name="x_woven_%d" % b, tag="x_woven_%d" % b, align_bytes=64)
-            nc.scalar.copy(
-                out=woven[:].rearrange("p d t -> p (d t)").bitcast(F32).rearrange("p (d u) -> p d u", u=2),
-                in_=bank[:, 0:2 * P].rearrange("p (u d) -> p d u", u=2),
-            )
-            return woven
-
-        def multiply(stationary, moving, b, bank):
+        def multiply(stationary, moving, b, sums, c0=0, c1=SLOTS):
             cols = slice(b * P, (b + 1) * P)
             nc.tensor.matmul_mx(
-                out=bank,
+                out=sums[:, c0:c1],
                 lhsT=stationary[0][:, cols].bitcast(E4M3),
                 lhsT_scale=stationary[1][:, cols],
-                rhs=moving[0].bitcast(E5M2),
-                rhs_scale=moving[1],
+                rhs=moving[0][:, c0:c1].bitcast(E5M2),
+                rhs_scale=moving[1][:, c0:c1],
                 start=True,
                 stop=True,
             )
-            return bank
+            return sums[:, c0:c1]
 
-        def drain(sums, name, tag, on_vector=False, scale=1.0 / DECAY):
-            grad = keep.tile([P, sums.shape[1]], F32, name=name, tag=tag, align_bytes=64)
-            if on_vector:
-                nc.vector.tensor_scalar(out=grad[:], in0=sums, scalar1=scale, scalar2=None, op0=MULT)
-            else:
-                nc.scalar.activation(out=grad[:], in_=sums, func=COPY, scale=scale)
+        def drain_a(sums, name, scale=1.0 / DECAY):
+            grad = keep.tile([P, sums.shape[1]], F32, name=name, tag=name, align_bytes=64)
+            nc.scalar.activation(out=grad[:], in_=sums, func=COPY, scale=scale)
             return grad
 
-        def product(stationary, moving, b, name, bank, tag=None):
-            return drain(multiply(stationary, moving, b, bank), name, tag or name)
+        def drain_b(sums, name, tag):
+            grad = keep.tile([P, sums.shape[1]], F32, name=name, tag=tag, align_bytes=64)
+            nc.vector.tensor_copy(out=grad[:], in_=sums)
+            return grad
 
-        def scatter(win, lst, grad):
-            nc.vector.tensor_copy(win[:].indirect(lst), grad[:])
+        def scatter_scalar(win, lst, grad, c0=0):
+            for s in range(0, grad.shape[1], HALF):
+                cols = slice((c0 + s) // 16, (c0 + s + HALF) // 16)
+                nc.scalar.activation(out=win[:].indirect(lst[:, cols]), in_=grad[:, s:s + HALF], func=COPY)
 
-        def turned_sum(b, addends, halves, scale):
-            turned = bank_pair("turned")
-            back = bank_pair("back")
-            for a, src in enumerate(addends):
-                for h in halves:
-                    for c in range(4):
-                        nc.tensor.matmul(
-                            turned[:, h, c * P:(c + 1) * P],
-                            lhsT=src[:, h * HALF + c * P:h * HALF + (c + 1) * P],
-                            rhs=ident[:],
-                            is_transpose=True,
-                            start=(a == 0 and c == 0),
-                            stop=(a == len(addends) - 1 and c == 3),
-                        )
-            scaled = {}
-            for h in halves:
-                tag = "scaled_%d_%d" % (b, h)
-                scaled[h] = keep.tile([P, HALF], F32, name=tag, tag=tag, align_bytes=64)
-                nc.scalar.activation(out=scaled[h][:], in_=turned[:, h, :], func=COPY, scale=scale)
-            for h in halves:
-                for c in range(4):
-                    nc.tensor.transpose(back[:, h, c * P:(c + 1) * P], scaled[h][:, c * P:(c + 1) * P], ident[:])
-            return back
+        def scatter_vector(win, lst, grad):
+            nc.vector.tensor_copy(win[:].indirect(lst[:]), grad[:])
 
         def add_early(b, tag):
             both = keep.tile([P, TOKENS], F32, name="m_pa_%d" % b, tag=tag, align_bytes=64)
             for h in range(2):
-                cols = slice(h * HALF, (h + 1) * HALF)
+                cols = slice(h * 512, (h + 1) * 512)
                 nc.gpsimd.tensor_tensor(out=both[:, cols], in0=m_rows[b][:, cols], in1=pa_win[b % 2][:, cols], op=ADD)
             return both
 
-        def finish(b, back):
+        def momentum(b, both, pieces):
             rows = slice(b * P, (b + 1) * P)
             new_m = keep.tile([P, TOKENS], F32, name="new_m_%d" % b)
-            new_w = keep.tile([P, TOKENS], F32, name="new_w_%d" % b)
-            for h in range(2):
-                cols = slice(h * HALF, (h + 1) * HALF)
-                step = keep.tile([P, HALF], F32, name="step_%d_%d" % (b, h), tag="step_%d_%d" % (b, h), align_bytes=64)
-                nc.scalar.activation(out=step[:], in_=back[:, h, :], func=COPY, scale=-RATE)
-                nc.scalar.copy(out=new_m[:, cols], in_=back[:, h, :])
-                nc.gpsimd.tensor_tensor(out=new_w[:, cols], in0=w_rows[b][:, cols], in1=step[:], op=ADD)
-            nc.sync.dma_start(out=out_0[rows, :], in_=new_m[:])
-            nc.sync.dma_start(out=out_1[rows, :], in_=new_w[:])
-
-        def finish_last(b, partial):
-            rows = slice(b * P, (b + 1) * P)
-            new_m = keep.tile([P, TOKENS], F32, name="new_m_%d" % b, tag="step_2_1", align_bytes=64)
-            new_w = keep.tile([P, TOKENS], F32, name="new_w_%d" % b)
-            for h in range(2):
-                cols = slice(h * HALF, (h + 1) * HALF)
-                nc.vector.tensor_tensor(out=new_m[:, cols], in0=pb_win[b % 2][:, cols], in1=partial[h], op=ADD)
+            for cols in pieces:
+                nc.vector.scalar_tensor_tensor(
+                    out=new_m[:, cols], in0=both[:, cols], scalar=DECAY, in1=pb_win[b % 2][:, cols], op0=MULT, op1=ADD
+                )
                 nc.sync.dma_start(out=out_0[rows, cols], in_=new_m[:, cols])
-            for cols in (slice(0, 512), slice(512, 768), slice(768, 1024)):
+            return new_m
+
+        def table(b, new_m, pieces):
+            rows = slice(b * P, (b + 1) * P)
+            new_w = keep.tile([P, TOKENS], F32, name="new_w_%d" % b)
+            for cols in pieces:
                 nc.vector.scalar_tensor_tensor(
                     out=new_w[:, cols], in0=new_m[:, cols], scalar=-RATE, in1=w_rows[b][:, cols], op0=MULT, op1=ADD
                 )
                 nc.sync.dma_start(out=out_1[rows, cols], in_=new_w[:, cols])
 
-        quantise(weave(v_0, "scalar", "v_0_woven", "v_0_woven"), v_0_mx, 0, E4M3)
-        quantise(weave(dz_a, "vector", "dz_a_woven", "head_woven"), dz_padded, 256, E5M2)
-        early = multiply(v_0_mx, dz_early, 0, mx_bank("mx_d"))
-        dz_b_woven = weave(dz_b, "vector", "dz_b_woven", "head_woven")
-        da_0a = drain(early[:, 256:512], "da_0a", "da_0a", on_vector=True)
-        quantise(dz_b_woven, dz_padded, 512, E5M2)
-        scatter(pa_win[0], j_list[:, 0:16], da_0a)
-        da_0b = drain(multiply(v_0_mx, dz_mx, 0, mx_bank("mx_a"))[:, 256:512], "da_0b", "da_0b")
-        quantise(weave(v_1, "scalar", "v_1_woven", "v_1_woven"), v_mx, 128, E4M3)
-        scatter(pa_win[0], j_list[:, 16:32], da_0b)
-        sums_1 = multiply(v_mx, dz_mx, 1, mx_bank("mx_d"))
-        scatter(pa_win[1], j_list[:, 0:16], drain(sums_1[:, 0:256], "da_1a", "da_1a"))
+        whole = [slice(0, TOKENS)]
+        halves = [slice(0, 512), slice(512, TOKENS)]
 
-        g_tiles = mx_operand("g", 512, "da_0b")
-        g_mx = [part[:] for part in g_tiles]
-        x_0_words = round_x(0, "x_pairs_0")
-        g_a_woven = weave(g_a, "scalar", "g_a_woven", "v_0_codes")
-        x_0_woven = turn_x(0, x_0_words, mx_bank("mx_b"))
-        g_b_woven = weave(g_b, "scalar", "g_b_woven", "g_a")
-        quantise(g_a_woven, g_tiles, 0, E5M2)
-        x_0_mx = mx_operand("x_0", P, "x_0_codes")
-        quantise(x_0_woven, x_0_mx, 0, E4M3)
-        quantise(g_b_woven, g_tiles, 256, E5M2)
-        scatter(pa_win[1], j_list[:, 16:32], drain(sums_1[:, 256:512], "da_1b", "g_b"))
+        v_01_woven = weave(v_01, "scalar", "v_01_woven")
+        dz_a_woven = weave(dz_a, "vector", "dz_a_woven")
+        quantise(v_01_woven, v_mx, 0, E4M3)
+        quantise(dz_a_woven, dz_mx, 0, E5M2)
+        da_0a = drain_a(multiply(v_mx, dz_mx, 0, bank("bank_0"), 0, HALF), "da_0a")
+        scatter_scalar(pa_win[0], j_list, da_0a)
+        quantise(weave(dz_b, "vector", "dz_b_woven"), dz_mx, HALF, E5M2)
+        da_0b = drain_a(multiply(v_mx, dz_mx, 0, bank("bank_1"), HALF, SLOTS), "da_0b")
+        scatter_scalar(pa_win[0], j_list, da_0b, HALF)
+        da_1 = drain_a(multiply(v_mx, dz_mx, 1, bank("bank_2")), "da_1")
+        scatter_scalar(pa_win[1], j_list, da_1)
 
-        x_1_words = round_x(1, "x_pairs_1")
-        sums_0 = multiply(x_0_mx, g_mx, 0, mx_bank("mx_b"))
-        scatter(pb_win[0], i_list[:, 0:16], drain(sums_0[:, 0:256], "db_0a", "db_0a"))
-        quantise(turn_x(1, x_1_words, mx_bank("mx_a")), x_mx, P, E4M3)
-        scatter(pb_win[0], i_list[:, 16:32], drain(sums_0[:, 256:512], "db_0b", "x_pairs_1"))
-
-        x_2_words = round_x(2, "x_0_codes")
-        x_3_words = round_x(3, "x_2")
-        quantise(turn_x(2, x_2_words, bank_pair("turned")[:, 0, :]), x_mx, 2 * P, E4M3)
-        quantise(turn_x(3, x_3_words, mx_bank("mx_c")), x_mx, 3 * P, E4M3)
-        quantise(weave(v_23, "scalar", "v_23_woven", "x_3"), v_mx, 256, E4M3)
-        db_1 = product(x_mx, g_mx, 1, "db_1", mx_bank("mx_c"), tag="v_23")
-        scatter(pb_win[1], i_list[:], db_1)
-        m_pa_1 = add_early(1, "x_3")
-        sum_0 = turned_sum(0, [m_rows[0], pa_win[0], pb_win[0]], (0, 1), DECAY)
-        da_2 = product(v_mx, dz_mx, 2, "da_2", mx_bank("mx_a"))
-        finish(0, sum_0)
-        db_2 = product(x_mx, g_mx, 2, "db_2", mx_bank("mx_a"))
-        da_3 = drain(multiply(v_mx, dz_mx, 3, mx_bank("mx_c")), "da_3", "scaled_0_1", scale=1.0)
-        db_3 = drain(multiply(x_mx, g_mx, 3, mx_bank("mx_c")), "db_3", "db_3", scale=1.0)
-        scatter(pa_win[0], j_list[:], da_2)
-        scatter(pb_win[0], i_list[:], db_2)
-        m_pa_2 = add_early(2, "step_0_1")
-        finish(1, turned_sum(1, [m_pa_1, pb_win[1]], (0, 1), DECAY))
-        scatter(pa_win[1], j_list[:], da_3)
-        low = keep.tile([P, HALF], F32, name="low")
-        nc.vector.scalar_tensor_tensor(
-            out=low[:], in0=m_rows[3][:, 0:HALF], scalar=DECAY, in1=pa_win[1][:, 0:HALF], op0=MULT, op1=ADD
-        )
-        decayed = keep.tile([P, TOKENS], F32, name="decayed", tag="scaled_1_1", align_bytes=64)
-        nc.scalar.activation(out=decayed[:, HALF:], in_=m_rows[3][:, HALF:], func=COPY, scale=DECAY)
-        finish(2, turned_sum(2, [m_pa_2, pb_win[0]], (0, 1), DECAY))
-        high = turned_sum(3, [decayed, pa_win[1]], (1,), 1.0)[:, 1, :]
-        scatter(pb_win[1], i_list[:], db_3)
-        finish_last(3, [low[:], high])
+        turn_x(0, "bank_3")
+        quantise(weave(g_a, "vector", "g_a_woven"), g_mx, 0, E5M2)
+        quantise(weave(g_b, "vector", "g_b_woven"), g_mx, HALF, E5M2)
+        sums_b0 = multiply(x_mx, g_mx, 0, bank("bank_4"))
+        turn_x(1, "bank_5")
+        db_1 = drain_a(multiply(x_mx, g_mx, 1, bank("bank_6")), "db_1", 1.0)
+        scatter_scalar(pb_win[1], i_list, db_1)
+        v_23_woven = weave(v_23, "vector", "v_23_woven")
+        db_0 = drain_b(sums_b0, "db_0", "v_23")
+        quantise(v_23_woven, v_mx, HALF, E4M3)
+        scatter_vector(pb_win[0], i_list, db_0)
+        m_pa_0 = add_early(0, "m_pa_0")
+        m_pa_1 = add_early(1, "m_pa_1")
+        da_2 = drain_a(multiply(v_mx, dz_mx, 2, bank("bank_7")), "da_2")
+        scatter_scalar(pa_win[0], j_list, da_2)
+        da_3 = drain_a(multiply(v_mx, dz_mx, 3, bank("bank_0")), "da_3")
+        scatter_scalar(pa_win[1], j_list, da_3)
+        turn_x(2, "bank_1")
+        turn_x(3, "bank_3")
+        sums_b2 = multiply(x_mx, g_mx, 2, bank("bank_2"))
+        db_3 = drain_a(multiply(x_mx, g_mx, 3, bank("bank_4")), "db_3", 1.0)
+        table(0, momentum(0, m_pa_0, whole), whole)
+        new_m_1 = momentum(1, m_pa_1, whole)
+        db_2 = drain_b(sums_b2, "db_2", "m_pa_1")
+        table(1, new_m_1, whole)
+        scatter_scalar(pb_win[1], i_list, db_3)
+        scatter_vector(pb_win[0], i_list, db_2)
+        m_pa_2 = add_early(2, "w_1")
+        m_pa_3 = add_early(3, "m_2")
+        table(2, momentum(2, m_pa_2, whole), whole)
+        table(3, momentum(3, m_pa_3, halves), halves)

@@ -32,6 +32,7 @@ def tile_attend_gtied_mom_kernel(tc, V, dz, xT, G, mT, wT, offs, joffs, out_0, o
     nc = tc.nc
     with ExitStack() as ctx:
         keep = ctx.enter_context(tc.tile_pool(name="keep", bufs=1))
+        reuse = ctx.enter_context(tc.tile_pool(name="reuse", bufs=1))
         psum = ctx.enter_context(tc.psum_pool(name="psum", bufs=1))
 
         def load_k_first(src, c0, c1, name):
@@ -50,45 +51,45 @@ def tile_attend_gtied_mom_kernel(tc, V, dz, xT, G, mT, wT, offs, joffs, out_0, o
             return lst
 
         x_rows, m_rows, w_rows = {}, {}, {}
-        v_01 = load_k_first(V, 0, 256, "v_01")
+        v_0 = load_k_first(V, 0, 128, "v_0")
         dz_a = load_k_first(dz, 0, 256, "dz_a")
         j_list = load_list(joffs, "j_list")
         dz_b = load_k_first(dz, 256, 512, "dz_b")
-        x_rows[0] = load_rows(xT, 0, "x_0")
+        for b in (0, 1):
+            x_rows[b] = load_rows(xT, b, "x_%d" % b)
+        v_1 = load_k_first(V, 128, 256, "v_1")
         g_a = load_k_first(G, 0, 256, "g_a")
         g_b = load_k_first(G, 256, 512, "g_b")
         i_list = load_list(offs, "i_list")
-        x_rows[1] = load_rows(xT, 1, "x_1")
-        v_23 = load_k_first(V, 256, 512, "v_23")
-        for b in (0, 1):
-            m_rows[b] = load_rows(mT, b, "m_%d" % b)
+        v_23 = reuse.tile([P, PACK, HALF], F32, name="v_23", offset=0, align_bytes=64)
+        nc.sync.dma_start(out=v_23[:], in_=V.rearrange("(p j) n -> p j n", j=PACK)[:, :, HALF:])
         for b in (2, 3):
             x_rows[b] = load_rows(xT, b, "x_%d" % b)
-        for b in (0, 1):
-            w_rows[b] = load_rows(wT, b, "w_%d" % b)
-        for b in (2, 3):
-            m_rows[b] = load_rows(mT, b, "m_%d" % b)
-        for b in (2, 3):
-            w_rows[b] = load_rows(wT, b, "w_%d" % b)
+        for pair in ((0, 1), (2, 3)):
+            for b in pair:
+                m_rows[b] = load_rows(mT, b, "m_%d" % b)
+            for b in pair:
+                w_rows[b] = load_rows(wT, b, "w_%d" % b)
 
         ident = keep.tile([P, P], F32, name="ident")
         make_identity(nc, ident[:])
         pa_win = [keep.tile([P, TOKENS], F32, name="pa_win_%d" % n) for n in range(2)]
         pb_win = [keep.tile([P, TOKENS], F32, name="pb_win_%d" % n) for n in range(2)]
-        for n in range(2):
-            nc.vector.memset(pa_win[n][:], 0.0)
-            nc.gpsimd.memset(pb_win[n][:], 0.0)
+        for win in pa_win:
+            nc.vector.memset(win[:], 0.0)
+        for win in pb_win:
+            nc.gpsimd.memset(win[:], 0.0)
 
-        def mx_operand(name):
-            codes = keep.tile([P, SLOTS], U32, name=name + "_codes", align_bytes=64)
-            scales = keep.tile([P, SLOTS], U8, name=name + "_scales", align_bytes=64)
+        def mx_operand(name, width=SLOTS, tag=None):
+            codes = keep.tile([P, width], U32, name=name + "_codes", tag=tag or name + "_codes", align_bytes=64)
+            scales = keep.tile([P, width], U8, name=name + "_scales", align_bytes=64)
             return codes, scales
 
         v_mx, x_mx, dz_mx, g_mx = [mx_operand(n) for n in ("v", "x", "dz", "g")]
 
         def weave(raw, engine, name):
             width = raw.shape[2]
-            woven = keep.tile([P, width, PACK], BF16, name=name, align_bytes=64)
+            woven = keep.tile([P, width, PACK], BF16, name=name, tag=name, align_bytes=64)
             dst = woven[:].rearrange("p (c i) t -> p c t i", i=4)
             src = raw[:].rearrange("p t (c i) -> p c t i", i=4)
             if engine == "vector":
@@ -109,19 +110,23 @@ def tile_attend_gtied_mom_kernel(tc, V, dz, xT, G, mT, wT, offs, joffs, out_0, o
         def bank(tag):
             return psum.tile([P, SLOTS], F32, name=tag, tag=tag)
 
-        def turn_x(b, tag):
+        def turn_x(b, tag, engine):
             turned = bank(tag)
             rows = x_rows[b][:].rearrange("d (p t) -> d t p", t=PACK)
             for t in range(PACK):
                 nc.tensor.transpose(turned[:, t * P:(t + 1) * P], rows[:, t, :], ident[:])
             woven = keep.tile([P, P, PACK], BF16, name="x_woven_%d" % b, align_bytes=64)
-            nc.vector.tensor_copy(out=woven[:], in_=turned[:].rearrange("p (t d) -> p d t", t=PACK))
-            quantise(woven, x_mx, b * P, E4M3)
+            src = turned[:].rearrange("p (t d) -> p d t", t=PACK)
+            if engine == "vector":
+                nc.vector.tensor_copy(out=woven[:], in_=src)
+            else:
+                nc.scalar.activation(out=woven[:], in_=src, func=COPY)
+            return woven
 
         def multiply(stationary, moving, b, sums, c0=0, c1=SLOTS):
             cols = slice(b * P, (b + 1) * P)
             nc.tensor.matmul_mx(
-                out=sums[:, c0:c1],
+                out=sums,
                 lhsT=stationary[0][:, cols].bitcast(E4M3),
                 lhsT_scale=stationary[1][:, cols],
                 rhs=moving[0][:, c0:c1].bitcast(E5M2),
@@ -129,10 +134,10 @@ def tile_attend_gtied_mom_kernel(tc, V, dz, xT, G, mT, wT, offs, joffs, out_0, o
                 start=True,
                 stop=True,
             )
-            return sums[:, c0:c1]
+            return sums
 
-        def drain_a(sums, name, scale=1.0 / DECAY):
-            grad = keep.tile([P, sums.shape[1]], F32, name=name, tag=name, align_bytes=64)
+        def drain_a(sums, name, scale=1.0 / DECAY, tag=None):
+            grad = keep.tile([P, sums.shape[1]], F32, name=name, tag=tag or name, align_bytes=64)
             nc.scalar.activation(out=grad[:], in_=sums, func=COPY, scale=scale)
             return grad
 
@@ -141,17 +146,20 @@ def tile_attend_gtied_mom_kernel(tc, V, dz, xT, G, mT, wT, offs, joffs, out_0, o
             nc.vector.tensor_copy(out=grad[:], in_=sums)
             return grad
 
-        def scatter_scalar(win, lst, grad, c0=0):
-            for s in range(0, grad.shape[1], HALF):
-                cols = slice((c0 + s) // 16, (c0 + s + HALF) // 16)
-                nc.scalar.activation(out=win[:].indirect(lst[:, cols]), in_=grad[:, s:s + HALF], func=COPY)
+        def scatter_scalar(win, lst, h, grad):
+            cols = slice(h * HALF // 16, (h + 1) * HALF // 16)
+            nc.scalar.activation(out=win[:].indirect(lst[:, cols]), in_=grad, func=COPY)
+
+        def scatter_halves(win, lst, grad):
+            for h in range(2):
+                scatter_scalar(win, lst, h, grad[:, h * HALF:(h + 1) * HALF])
 
         def scatter_vector(win, lst, grad):
-            nc.vector.tensor_copy(win[:].indirect(lst[:]), grad[:])
+            nc.vector.tensor_copy(win[:].indirect(lst[:]), grad)
 
-        def add_early(b, tag):
+        def add_early(b, tag, parts=(0, 1)):
             both = keep.tile([P, TOKENS], F32, name="m_pa_%d" % b, tag=tag, align_bytes=64)
-            for h in range(2):
+            for h in parts:
                 cols = slice(h * 512, (h + 1) * 512)
                 nc.gpsimd.tensor_tensor(out=both[:, cols], in0=m_rows[b][:, cols], in1=pa_win[b % 2][:, cols], op=ADD)
             return both
@@ -178,46 +186,55 @@ def tile_attend_gtied_mom_kernel(tc, V, dz, xT, G, mT, wT, offs, joffs, out_0, o
         whole = [slice(0, TOKENS)]
         halves = [slice(0, 512), slice(512, TOKENS)]
 
-        v_01_woven = weave(v_01, "scalar", "v_01_woven")
-        dz_a_woven = weave(dz_a, "vector", "dz_a_woven")
-        quantise(v_01_woven, v_mx, 0, E4M3)
-        quantise(dz_a_woven, dz_mx, 0, E5M2)
-        da_0a = drain_a(multiply(v_mx, dz_mx, 0, bank("bank_0"), 0, HALF), "da_0a")
-        scatter_scalar(pa_win[0], j_list, da_0a)
+        quantise(weave(v_0, "scalar", "v_0_woven"), v_mx, 0, E4M3)
+        quantise(weave(dz_a, "vector", "dz_a_woven"), dz_mx, 0, E5M2)
+        da_0a = drain_a(multiply(v_mx, dz_mx, 0, bank("bank_0")[:, 0:HALF], 0, HALF), "da_0a")
+        scatter_scalar(pa_win[0], j_list, 0, da_0a[:])
         quantise(weave(dz_b, "vector", "dz_b_woven"), dz_mx, HALF, E5M2)
-        da_0b = drain_a(multiply(v_mx, dz_mx, 0, bank("bank_1"), HALF, SLOTS), "da_0b")
-        scatter_scalar(pa_win[0], j_list, da_0b, HALF)
-        da_1 = drain_a(multiply(v_mx, dz_mx, 1, bank("bank_2")), "da_1")
-        scatter_scalar(pa_win[1], j_list, da_1)
+        da_0b = drain_a(multiply(v_mx, dz_mx, 0, bank("bank_1")[:, 0:HALF], HALF, SLOTS), "da_0b")
+        scatter_scalar(pa_win[0], j_list, 1, da_0b[:])
+        x_0_woven = turn_x(0, "bank_2", "vector")
+        x_1_woven = turn_x(1, "bank_3", "scalar")
+        v_1_woven = weave(v_1, "vector", "v_1_woven")
+        quantise(x_0_woven, x_mx, 0, E4M3)
+        quantise(v_1_woven, v_mx, P, E4M3)
+        scatter_halves(pa_win[1], j_list, drain_a(multiply(v_mx, dz_mx, 1, bank("bank_4")[:]), "da_1", tag="x_1"))
 
-        turn_x(0, "bank_3")
         quantise(weave(g_a, "vector", "g_a_woven"), g_mx, 0, E5M2)
         quantise(weave(g_b, "vector", "g_b_woven"), g_mx, HALF, E5M2)
-        sums_b0 = multiply(x_mx, g_mx, 0, bank("bank_4"))
-        turn_x(1, "bank_5")
-        db_1 = drain_a(multiply(x_mx, g_mx, 1, bank("bank_6")), "db_1", 1.0)
-        scatter_scalar(pb_win[1], i_list, db_1)
+        sums_b0 = multiply(x_mx, g_mx, 0, bank("bank_5")[:])
         v_23_woven = weave(v_23, "vector", "v_23_woven")
-        db_0 = drain_b(sums_b0, "db_0", "v_23")
+        x_1_codes = reuse.tile([P, P], U32, name="x_1_codes", offset=2048, align_bytes=64)
+        x_1_scales = keep.tile([P, P], U8, name="x_1_scales", align_bytes=64)
+        quantise(x_1_woven, (x_1_codes, x_1_scales), 0, E4M3)
+        db_1 = drain_a(multiply((x_1_codes, x_1_scales), g_mx, 0, bank("bank_6")[:]), "db_1", 1.0)
+        db_0 = reuse.tile([P, SLOTS], F32, name="db_0", offset=0, align_bytes=64)
+        nc.vector.tensor_copy(out=db_0[:], in_=sums_b0)
         quantise(v_23_woven, v_mx, HALF, E4M3)
-        scatter_vector(pb_win[0], i_list, db_0)
-        m_pa_0 = add_early(0, "m_pa_0")
+        scatter_vector(pb_win[0], i_list, db_0[:])
+        scatter_vector(pb_win[1], i_list, db_1[:])
+        m_pa_0 = add_early(0, "v_23_woven")
         m_pa_1 = add_early(1, "m_pa_1")
-        da_2 = drain_a(multiply(v_mx, dz_mx, 2, bank("bank_7")), "da_2")
-        scatter_scalar(pa_win[0], j_list, da_2)
-        da_3 = drain_a(multiply(v_mx, dz_mx, 3, bank("bank_0")), "da_3")
-        scatter_scalar(pa_win[1], j_list, da_3)
-        turn_x(2, "bank_1")
-        turn_x(3, "bank_3")
-        sums_b2 = multiply(x_mx, g_mx, 2, bank("bank_2"))
-        db_3 = drain_a(multiply(x_mx, g_mx, 3, bank("bank_4")), "db_3", 1.0)
-        table(0, momentum(0, m_pa_0, whole), whole)
+        x_2_woven = turn_x(2, "bank_1", "scalar")
+        x_3_woven = turn_x(3, "bank_2", "scalar")
+        da_2 = drain_a(multiply(v_mx, dz_mx, 2, bank("bank_7")[:]), "da_2", tag="x_3")
+        da_3 = drain_a(multiply(v_mx, dz_mx, 3, bank("bank_0")[:]), "da_3")
+        scatter_halves(pa_win[0], j_list, da_2)
+        new_m_0 = momentum(0, m_pa_0, whole)
+        quantise(x_2_woven, x_mx, 2 * P, E4M3)
+        quantise(x_3_woven, x_mx, 3 * P, E4M3)
+        sums_b2 = multiply(x_mx, g_mx, 2, bank("bank_3")[:])
+        db_3 = drain_a(multiply(x_mx, g_mx, 3, bank("bank_4")[:]), "db_3", 1.0)
+        scatter_halves(pa_win[1], j_list, da_3)
         new_m_1 = momentum(1, m_pa_1, whole)
         db_2 = drain_b(sums_b2, "db_2", "m_pa_1")
+        table(0, new_m_0, whole)
         table(1, new_m_1, whole)
-        scatter_scalar(pb_win[1], i_list, db_3)
-        scatter_vector(pb_win[0], i_list, db_2)
+        scatter_halves(pb_win[1], i_list, db_3)
+        scatter_vector(pb_win[0], i_list, db_2[:])
         m_pa_2 = add_early(2, "w_1")
-        m_pa_3 = add_early(3, "m_2")
-        table(2, momentum(2, m_pa_2, whole), whole)
+        m_pa_3 = add_early(3, "m_2", (0,))
+        new_m_2 = momentum(2, m_pa_2, whole)
+        nc.vector.tensor_tensor(out=m_pa_3[:, 512:], in0=m_rows[3][:, 512:], in1=pa_win[1][:, 512:], op=ADD)
+        table(2, new_m_2, whole)
         table(3, momentum(3, m_pa_3, halves), halves)

@@ -35,13 +35,16 @@ def tile_attend_gtied_mom_kernel(tc, V, dz, xT, G, mT, wT, offs, joffs, out_0, o
         reuse = ctx.enter_context(tc.tile_pool(name="reuse", bufs=1))
         psum = ctx.enter_context(tc.psum_pool(name="psum", bufs=1))
 
-        def load_k_first(src, c0, c1, name):
-            raw = keep.tile([P, PACK, c1 - c0], F32, name=name, tag=name, align_bytes=64)
-            nc.sync.dma_start(out=raw[:], in_=src.rearrange("(p j) n -> p j n", j=PACK)[:, :, c0:c1])
+        def tile(shape, dtype, name, over=None):
+            return keep.tile(shape, dtype, name=name, tag=over or name, align_bytes=64)
+
+        def load_k_first(src, h, name):
+            raw = tile([P, PACK, HALF], F32, name)
+            nc.sync.dma_start(out=raw[:], in_=src.rearrange("(p j) n -> p j n", j=PACK)[:, :, h * HALF:(h + 1) * HALF])
             return raw
 
         def load_rows(src, b, name):
-            raw = keep.tile([P, src.shape[1]], F32, name=name, tag=name, align_bytes=64)
+            raw = tile([P, src.shape[1]], F32, name)
             nc.sync.dma_start(out=raw[:], in_=src[b * P:(b + 1) * P, :])
             return raw
 
@@ -51,18 +54,16 @@ def tile_attend_gtied_mom_kernel(tc, V, dz, xT, G, mT, wT, offs, joffs, out_0, o
             return lst
 
         x_rows, m_rows, w_rows = {}, {}, {}
-        v_0 = load_k_first(V, 0, 128, "v_0")
-        dz_a = load_k_first(dz, 0, 256, "dz_a")
+        v_01 = load_k_first(V, 0, "v_01")
+        dz_a = load_k_first(dz, 0, "dz_a")
         j_list = load_list(joffs, "j_list")
-        dz_b = load_k_first(dz, 256, 512, "dz_b")
+        dz_b = load_k_first(dz, 1, "dz_b")
         for b in (0, 1):
             x_rows[b] = load_rows(xT, b, "x_%d" % b)
-        v_1 = load_k_first(V, 128, 256, "v_1")
-        g_a = load_k_first(G, 0, 256, "g_a")
-        g_b = load_k_first(G, 256, 512, "g_b")
+        g_a = load_k_first(G, 0, "g_a")
+        g_b = load_k_first(G, 1, "g_b")
         i_list = load_list(offs, "i_list")
-        v_23 = reuse.tile([P, PACK, HALF], F32, name="v_23", offset=0, align_bytes=64)
-        nc.sync.dma_start(out=v_23[:], in_=V.rearrange("(p j) n -> p j n", j=PACK)[:, :, HALF:])
+        v_23 = load_k_first(V, 1, "v_23")
         for b in (2, 3):
             x_rows[b] = load_rows(xT, b, "x_%d" % b)
         for pair in ((0, 1), (2, 3)):
@@ -73,23 +74,23 @@ def tile_attend_gtied_mom_kernel(tc, V, dz, xT, G, mT, wT, offs, joffs, out_0, o
 
         ident = keep.tile([P, P], F32, name="ident")
         make_identity(nc, ident[:])
-        pa_win = [keep.tile([P, TOKENS], F32, name="pa_win_%d" % n) for n in range(2)]
-        pb_win = [keep.tile([P, TOKENS], F32, name="pb_win_%d" % n) for n in range(2)]
-        for win in pa_win:
-            nc.vector.memset(win[:], 0.0)
-        for win in pb_win:
-            nc.gpsimd.memset(win[:], 0.0)
 
-        def mx_operand(name, width=SLOTS, tag=None):
-            codes = keep.tile([P, width], U32, name=name + "_codes", tag=tag or name + "_codes", align_bytes=64)
-            scales = keep.tile([P, width], U8, name=name + "_scales", align_bytes=64)
-            return codes, scales
+        pa_win = [tile([P, TOKENS], F32, "pa_win_%d" % n) for n in range(2)] * 2
+        pb_win = [tile([P, TOKENS], F32, "pb_win_%d" % n) for n in range(2)] * 2
+        for n in range(2):
+            nc.vector.memset(pa_win[n][:], 0.0)
+            nc.gpsimd.memset(pb_win[n][:], 0.0)
 
-        v_mx, x_mx, dz_mx, g_mx = [mx_operand(n) for n in ("v", "x", "dz", "g")]
+        def placed(shape, dtype, name, offset):
+            return reuse.tile(shape, dtype, name=name, offset=offset, align_bytes=64)
 
-        def weave(raw, engine, name):
-            width = raw.shape[2]
-            woven = keep.tile([P, width, PACK], BF16, name=name, tag=name, align_bytes=64)
+        def mx_operand(name, width=SLOTS, over=None):
+            return tile([P, width], U32, name + "_codes", over), tile([P, width], U8, name + "_scales")
+
+        dz_mx, g_mx = [mx_operand(n) for n in ("dz", "g")]
+        v_01_mx, v_23_mx, x_01_mx, x_23_mx = [mx_operand(n, HALF) for n in ("v_01", "v_23", "x_01", "x_23")]
+
+        def weave(raw, engine, woven):
             dst = woven[:].rearrange("p (c i) t -> p c t i", i=4)
             src = raw[:].rearrange("p t (c i) -> p c t i", i=4)
             if engine == "vector":
@@ -107,24 +108,30 @@ def tile_attend_gtied_mom_kernel(tc, V, dz, xT, G, mT, wT, offs, joffs, out_0, o
                 in_=woven[:].rearrange("p n t -> p (n t)"),
             )
 
-        def bank(tag):
-            return psum.tile([P, SLOTS], F32, name=tag, tag=tag)
+        def bank(n, width=SLOTS):
+            return psum.tile([P, SLOTS], F32, name="bank_%d" % n, tag="bank_%d" % n)[:, 0:width]
 
-        def turn_x(b, tag, engine):
-            turned = bank(tag)
-            rows = x_rows[b][:].rearrange("d (p t) -> d t p", t=PACK)
-            for t in range(PACK):
-                nc.tensor.transpose(turned[:, t * P:(t + 1) * P], rows[:, t, :], ident[:])
-            woven = keep.tile([P, P, PACK], BF16, name="x_woven_%d" % b, align_bytes=64)
-            src = turned[:].rearrange("p (t d) -> p d t", t=PACK)
+        def round_x(pair, engine, pairs):
+            for n in range(2):
+                src = x_rows[2 * pair + n][:].rearrange("d (p u e) -> d u p e", u=2, e=2)
+                if engine == "gpsimd":
+                    nc.gpsimd.tensor_scalar(out=pairs[:, n], in0=src, scalar1=1.0, scalar2=0.0, op0=MULT, op1=ADD)
+                else:
+                    nc.vector.tensor_copy(out=pairs[:, n], in_=src)
+
+        def turn_x(pairs, turned, engine, woven):
+            words = pairs[:].rearrange("d n u p e -> d (n u p e)").bitcast(F32)
+            for q in range(4):
+                nc.tensor.transpose(turned[:, q * P:(q + 1) * P], words[:, q * P:(q + 1) * P], ident[:])
+            dst = woven[:].rearrange("p d t -> p (d t)").bitcast(F32).rearrange("p (n d u) -> p n d u", n=2, u=2)
+            src = turned.rearrange("p (n u d) -> p n d u", n=2, u=2)
             if engine == "vector":
-                nc.vector.tensor_copy(out=woven[:], in_=src)
+                nc.vector.tensor_copy(out=dst, in_=src)
             else:
-                nc.scalar.activation(out=woven[:], in_=src, func=COPY)
-            return woven
+                nc.scalar.copy(out=dst, in_=src)
 
-        def multiply(stationary, moving, b, sums, c0=0, c1=SLOTS):
-            cols = slice(b * P, (b + 1) * P)
+        def multiply(stationary, n, moving, sums, c0=0, c1=SLOTS):
+            cols = slice(n * P, (n + 1) * P)
             nc.tensor.matmul_mx(
                 out=sums,
                 lhsT=stationary[0][:, cols].bitcast(E4M3),
@@ -136,105 +143,113 @@ def tile_attend_gtied_mom_kernel(tc, V, dz, xT, G, mT, wT, offs, joffs, out_0, o
             )
             return sums
 
-        def drain_a(sums, name, scale=1.0 / DECAY, tag=None):
-            grad = keep.tile([P, sums.shape[1]], F32, name=name, tag=tag or name, align_bytes=64)
-            nc.scalar.activation(out=grad[:], in_=sums, func=COPY, scale=scale)
-            return grad
-
-        def drain_b(sums, name, tag):
-            grad = keep.tile([P, sums.shape[1]], F32, name=name, tag=tag, align_bytes=64)
-            nc.vector.tensor_copy(out=grad[:], in_=sums)
-            return grad
+        def drain(sums, grad, scale):
+            nc.scalar.activation(out=grad, in_=sums, func=COPY, scale=scale)
 
         def scatter_scalar(win, lst, h, grad):
             cols = slice(h * HALF // 16, (h + 1) * HALF // 16)
             nc.scalar.activation(out=win[:].indirect(lst[:, cols]), in_=grad, func=COPY)
 
-        def scatter_halves(win, lst, grad):
-            for h in range(2):
-                scatter_scalar(win, lst, h, grad[:, h * HALF:(h + 1) * HALF])
-
         def scatter_vector(win, lst, grad):
             nc.vector.tensor_copy(win[:].indirect(lst[:]), grad)
 
-        def add_early(b, tag, parts=(0, 1)):
-            both = keep.tile([P, TOKENS], F32, name="m_pa_%d" % b, tag=tag, align_bytes=64)
-            for h in parts:
-                cols = slice(h * 512, (h + 1) * 512)
-                nc.gpsimd.tensor_tensor(out=both[:, cols], in0=m_rows[b][:, cols], in1=pa_win[b % 2][:, cols], op=ADD)
+        halves = [slice(0, 512), slice(512, TOKENS)]
+
+        def add_early(b, over, parts):
+            both = tile([P, TOKENS], F32, "partial_%d" % b, over)
+            for cols in parts:
+                nc.gpsimd.tensor_tensor(out=both[:, cols], in0=m_rows[b][:, cols], in1=pa_win[b][:, cols], op=ADD)
             return both
 
-        def momentum(b, both, pieces):
-            rows = slice(b * P, (b + 1) * P)
-            new_m = keep.tile([P, TOKENS], F32, name="new_m_%d" % b)
+        def store(dst, b, src, pieces):
+            for cols in pieces:
+                nc.sync.dma_start(out=dst[b * P:(b + 1) * P, cols], in_=src[:, cols])
+
+        def momentum(b, both, new_m, pieces):
             for cols in pieces:
                 nc.vector.scalar_tensor_tensor(
-                    out=new_m[:, cols], in0=both[:, cols], scalar=DECAY, in1=pb_win[b % 2][:, cols], op0=MULT, op1=ADD
+                    out=new_m[:, cols], in0=both[:, cols], scalar=DECAY, in1=pb_win[b][:, cols], op0=MULT, op1=ADD
                 )
-                nc.sync.dma_start(out=out_0[rows, cols], in_=new_m[:, cols])
-            return new_m
 
-        def table(b, new_m, pieces):
-            rows = slice(b * P, (b + 1) * P)
-            new_w = keep.tile([P, TOKENS], F32, name="new_w_%d" % b)
+        def table(b, new_m, new_w, pieces):
             for cols in pieces:
                 nc.vector.scalar_tensor_tensor(
                     out=new_w[:, cols], in0=new_m[:, cols], scalar=-RATE, in1=w_rows[b][:, cols], op0=MULT, op1=ADD
                 )
-                nc.sync.dma_start(out=out_1[rows, cols], in_=new_w[:, cols])
 
-        whole = [slice(0, TOKENS)]
-        halves = [slice(0, 512), slice(512, TOKENS)]
+        def finish(b, both, new_m, pieces=(slice(0, TOKENS),)):
+            new_w = tile([P, TOKENS], F32, "new_w_%d" % b)
+            momentum(b, both, new_m, halves)
+            store(out_0, b, new_m, pieces)
+            table(b, new_m, new_w, halves)
+            store(out_1, b, new_w, pieces)
 
-        quantise(weave(v_0, "scalar", "v_0_woven"), v_mx, 0, E4M3)
-        quantise(weave(dz_a, "vector", "dz_a_woven"), dz_mx, 0, E5M2)
-        da_0a = drain_a(multiply(v_mx, dz_mx, 0, bank("bank_0")[:, 0:HALF], 0, HALF), "da_0a")
-        scatter_scalar(pa_win[0], j_list, 0, da_0a[:])
-        quantise(weave(dz_b, "vector", "dz_b_woven"), dz_mx, HALF, E5M2)
-        da_0b = drain_a(multiply(v_mx, dz_mx, 0, bank("bank_1")[:, 0:HALF], HALF, SLOTS), "da_0b")
-        scatter_scalar(pa_win[0], j_list, 1, da_0b[:])
-        x_0_woven = turn_x(0, "bank_2", "vector")
-        x_1_woven = turn_x(1, "bank_3", "scalar")
-        v_1_woven = weave(v_1, "vector", "v_1_woven")
-        quantise(x_0_woven, x_mx, 0, E4M3)
-        quantise(v_1_woven, v_mx, P, E4M3)
-        scatter_halves(pa_win[1], j_list, drain_a(multiply(v_mx, dz_mx, 1, bank("bank_4")[:]), "da_1", tag="x_1"))
+        def first_pair(h, banks):
+            grads = tile([P, 2, HALF], F32, "da_01_%d" % h)
+            for b in range(2):
+                sums = multiply(v_01_mx, b, dz_mx, bank(banks[b], HALF), h * HALF, (h + 1) * HALF)
+                drain(sums, grads[:, b, :], 1.0 / DECAY)
+            for b in range(2):
+                scatter_scalar(pa_win[b], j_list, h, grads[:, b, :])
 
-        quantise(weave(g_a, "vector", "g_a_woven"), g_mx, 0, E5M2)
-        quantise(weave(g_b, "vector", "g_b_woven"), g_mx, HALF, E5M2)
-        sums_b0 = multiply(x_mx, g_mx, 0, bank("bank_5")[:])
-        v_23_woven = weave(v_23, "vector", "v_23_woven")
-        x_1_codes = reuse.tile([P, P], U32, name="x_1_codes", offset=2048, align_bytes=64)
-        x_1_scales = keep.tile([P, P], U8, name="x_1_scales", align_bytes=64)
-        quantise(x_1_woven, (x_1_codes, x_1_scales), 0, E4M3)
-        db_1 = drain_a(multiply((x_1_codes, x_1_scales), g_mx, 0, bank("bank_6")[:]), "db_1", 1.0)
-        db_0 = reuse.tile([P, SLOTS], F32, name="db_0", offset=0, align_bytes=64)
-        nc.vector.tensor_copy(out=db_0[:], in_=sums_b0)
-        quantise(v_23_woven, v_mx, HALF, E4M3)
-        scatter_vector(pb_win[0], i_list, db_0[:])
-        scatter_vector(pb_win[1], i_list, db_1[:])
-        m_pa_0 = add_early(0, "v_23_woven")
-        m_pa_1 = add_early(1, "m_pa_1")
-        x_2_woven = turn_x(2, "bank_1", "scalar")
-        x_3_woven = turn_x(3, "bank_2", "scalar")
-        da_2 = drain_a(multiply(v_mx, dz_mx, 2, bank("bank_7")[:]), "da_2", tag="x_3")
-        da_3 = drain_a(multiply(v_mx, dz_mx, 3, bank("bank_0")[:]), "da_3")
-        scatter_halves(pa_win[0], j_list, da_2)
-        new_m_0 = momentum(0, m_pa_0, whole)
-        quantise(x_2_woven, x_mx, 2 * P, E4M3)
-        quantise(x_3_woven, x_mx, 3 * P, E4M3)
-        sums_b2 = multiply(x_mx, g_mx, 2, bank("bank_3")[:])
-        db_3 = drain_a(multiply(x_mx, g_mx, 3, bank("bank_4")[:]), "db_3", 1.0)
-        scatter_halves(pa_win[1], j_list, da_3)
-        new_m_1 = momentum(1, m_pa_1, whole)
-        db_2 = drain_b(sums_b2, "db_2", "m_pa_1")
-        table(0, new_m_0, whole)
-        table(1, new_m_1, whole)
-        scatter_halves(pb_win[1], i_list, db_3)
-        scatter_vector(pb_win[0], i_list, db_2[:])
-        m_pa_2 = add_early(2, "w_1")
-        m_pa_3 = add_early(3, "m_2", (0,))
-        new_m_2 = momentum(2, m_pa_2, whole)
-        nc.vector.tensor_tensor(out=m_pa_3[:, 512:], in0=m_rows[3][:, 512:], in1=pa_win[1][:, 512:], op=ADD)
-        table(2, new_m_2, whole)
-        table(3, momentum(3, m_pa_3, halves), halves)
+        half_woven = [P, HALF, PACK]
+        pair_words = [P, 2, 2, P, 2]
+        v_01_woven = weave(v_01, "scalar", tile(half_woven, BF16, "v_01_woven"))
+        dz_a_woven = weave(dz_a, "vector", tile(half_woven, BF16, "dz_a_woven"))
+        quantise(v_01_woven, v_01_mx, 0, E4M3)
+        quantise(dz_a_woven, dz_mx, 0, E5M2)
+        first_pair(0, (0, 1))
+        quantise(weave(dz_b, "vector", tile(half_woven, BF16, "dz_b_woven")), dz_mx, HALF, E5M2)
+        first_pair(1, (2, 3))
+
+        x_01_pairs = placed(pair_words, BF16, "x_01_pairs", 1024)
+        round_x(0, "vector", x_01_pairs)
+        quantise(weave(g_a, "vector", tile(half_woven, BF16, "g_a_woven")), g_mx, 0, E5M2)
+        x_01_woven = tile(half_woven, BF16, "x_01_woven")
+        turn_x(x_01_pairs, bank(4), "vector", x_01_woven)
+        g_b_woven = weave(g_b, "vector", placed(half_woven, BF16, "g_b_woven", 0))
+        quantise(x_01_woven, x_01_mx, 0, E4M3)
+        quantise(g_b_woven, g_mx, HALF, E5M2)
+        sums_b = [multiply(x_01_mx, b, g_mx, bank(5 + b)) for b in range(2)]
+        v_23_woven = weave(v_23, "vector", placed(half_woven, BF16, "v_23_woven", 2048))
+        db_01 = [tile([P, SLOTS], F32, "db_%d" % b) for b in range(2)]
+        nc.vector.tensor_copy(out=db_01[0][:], in_=sums_b[0])
+        drain(sums_b[1], db_01[1][:], 1.0)
+        quantise(v_23_woven, v_23_mx, 0, E4M3)
+        for b in range(2):
+            scatter_vector(pb_win[b], i_list, db_01[b][:])
+        x_23_pairs = placed(pair_words, BF16, "x_23_pairs", 2048)
+        round_x(1, "gpsimd", x_23_pairs)
+        partial_0 = add_early(0, "x_3", halves)
+        partial_1 = add_early(1, None, halves)
+
+        x_23_woven = tile(half_woven, BF16, "x_23_woven")
+        turn_x(x_23_pairs, bank(7), "scalar", x_23_woven)
+        da_23 = placed([P, 2, SLOTS], F32, "da_23", 2048)
+        for n in range(2):
+            drain(multiply(v_23_mx, n, dz_mx, bank(n)), da_23[:, n, :], 1.0 / DECAY)
+        for n in range(2):
+            for h in range(2):
+                scatter_scalar(pa_win[2 + n], j_list, h, da_23[:, n, h * HALF:(h + 1) * HALF])
+        quantise(x_23_woven, x_23_mx, 0, E4M3)
+        finish(0, partial_0, tile([P, TOKENS], F32, "new_m_0", "x_23_woven"))
+        finish(1, partial_1, tile([P, TOKENS], F32, "new_m_1"))
+        db_2 = tile([P, SLOTS], F32, "db_2", "partial_1")
+        nc.vector.tensor_copy(out=db_2[:], in_=multiply(x_23_mx, 0, g_mx, bank(2)))
+        db_3 = tile([P, SLOTS], F32, "db_3")
+        drain(multiply(x_23_mx, 1, g_mx, bank(3)), db_3[:], 1.0)
+        for h in range(2):
+            scatter_scalar(pb_win[3], i_list, h, db_3[:, h * HALF:(h + 1) * HALF])
+        scatter_vector(pb_win[2], i_list, db_2[:])
+        partial_2 = add_early(2, "w_1", halves)
+        partial_3 = add_early(3, "m_2", halves[:1])
+        nc.vector.tensor_tensor(out=partial_3[:, 512:], in0=m_rows[3][:, 512:], in1=pa_win[3][:, 512:], op=ADD)
+        finish(2, partial_2, tile([P, TOKENS], F32, "new_m_2"), halves)
+        new_m = tile([P, TOKENS], F32, "new_m_3")
+        new_w = tile([P, TOKENS], F32, "new_w_3")
+        for cols in halves:
+            momentum(3, partial_3, new_m, [cols])
+            store(out_0, 3, new_m, [cols])
+        for cols in halves:
+            table(3, new_m, new_w, [cols])
+            store(out_1, 3, new_w, [cols])

@@ -75,11 +75,12 @@ def tile_attend_gtied_mom_kernel(tc, V, dz, xT, G, mT, wT, offs, joffs, out_0, o
         ident = keep.tile([P, P], F32, name="ident")
         make_identity(nc, ident[:])
 
-        pa_win = [tile([P, TOKENS], F32, "pa_win_%d" % n) for n in range(2)] * 2
+        pa_win = [tile([P, TOKENS], F32, "pa_win_%d" % b) for b in range(BLOCKS)]
         pb_win = [tile([P, TOKENS], F32, "pb_win_%d" % n) for n in range(2)] * 2
-        for n in range(2):
-            nc.vector.memset(pa_win[n][:], 0.0)
-            nc.gpsimd.memset(pb_win[n][:], 0.0)
+        for win in pa_win:
+            nc.vector.memset(win[:], 0.0)
+        for win in pb_win[:2]:
+            nc.gpsimd.memset(win[:], 0.0)
 
         def placed(shape, dtype, name, offset):
             return reuse.tile(shape, dtype, name=name, offset=offset, align_bytes=64)
@@ -111,13 +112,10 @@ def tile_attend_gtied_mom_kernel(tc, V, dz, xT, G, mT, wT, offs, joffs, out_0, o
         def bank(n, width=SLOTS):
             return psum.tile([P, SLOTS], F32, name="bank_%d" % n, tag="bank_%d" % n)[:, 0:width]
 
-        def round_x(pair, engine, pairs):
+        def round_x(pair, pairs):
             for n in range(2):
                 src = x_rows[2 * pair + n][:].rearrange("d (p u e) -> d u p e", u=2, e=2)
-                if engine == "gpsimd":
-                    nc.gpsimd.tensor_scalar(out=pairs[:, n], in0=src, scalar1=1.0, scalar2=0.0, op0=MULT, op1=ADD)
-                else:
-                    nc.vector.tensor_copy(out=pairs[:, n], in_=src)
+                nc.vector.tensor_copy(out=pairs[:, n], in_=src)
 
         def turn_x(pairs, turned, engine, woven):
             words = pairs[:].rearrange("d n u p e -> d (n u p e)").bitcast(F32)
@@ -155,10 +153,10 @@ def tile_attend_gtied_mom_kernel(tc, V, dz, xT, G, mT, wT, offs, joffs, out_0, o
 
         halves = [slice(0, 512), slice(512, TOKENS)]
 
-        def add_early(b, over, parts):
+        def add_early(b, over=None):
             both = tile([P, TOKENS], F32, "partial_%d" % b, over)
-            for cols in parts:
-                nc.gpsimd.tensor_tensor(out=both[:, cols], in0=m_rows[b][:, cols], in1=pa_win[b][:, cols], op=ADD)
+            for cols in halves:
+                nc.vector.tensor_tensor(out=both[:, cols], in0=m_rows[b][:, cols], in1=pa_win[b][:, cols], op=ADD)
             return both
 
         def store(dst, b, src, pieces):
@@ -203,7 +201,7 @@ def tile_attend_gtied_mom_kernel(tc, V, dz, xT, G, mT, wT, offs, joffs, out_0, o
         first_pair(1, (2, 3))
 
         x_01_pairs = placed(pair_words, BF16, "x_01_pairs", 1024)
-        round_x(0, "vector", x_01_pairs)
+        round_x(0, x_01_pairs)
         quantise(weave(g_a, "vector", tile(half_woven, BF16, "g_a_woven")), g_mx, 0, E5M2)
         x_01_woven = tile(half_woven, BF16, "x_01_woven")
         turn_x(x_01_pairs, bank(4), "vector", x_01_woven)
@@ -212,38 +210,34 @@ def tile_attend_gtied_mom_kernel(tc, V, dz, xT, G, mT, wT, offs, joffs, out_0, o
         quantise(g_b_woven, g_mx, HALF, E5M2)
         sums_b = [multiply(x_01_mx, b, g_mx, bank(5 + b)) for b in range(2)]
         v_23_woven = weave(v_23, "vector", placed(half_woven, BF16, "v_23_woven", 2048))
+        quantise(v_23_woven, v_23_mx, 0, E4M3)
         db_01 = [tile([P, SLOTS], F32, "db_%d" % b) for b in range(2)]
         nc.vector.tensor_copy(out=db_01[0][:], in_=sums_b[0])
         drain(sums_b[1], db_01[1][:], 1.0)
-        quantise(v_23_woven, v_23_mx, 0, E4M3)
+        x_23_pairs = placed(pair_words, BF16, "x_23_pairs", 2048)
+        round_x(1, x_23_pairs)
         for b in range(2):
             scatter_vector(pb_win[b], i_list, db_01[b][:])
-        x_23_pairs = placed(pair_words, BF16, "x_23_pairs", 2048)
-        round_x(1, "gpsimd", x_23_pairs)
-        partial_0 = add_early(0, "x_3", halves)
-        partial_1 = add_early(1, None, halves)
 
         x_23_woven = tile(half_woven, BF16, "x_23_woven")
         turn_x(x_23_pairs, bank(7), "scalar", x_23_woven)
-        da_23 = placed([P, 2, SLOTS], F32, "da_23", 2048)
+        da_23 = placed([P, 2, 2, HALF], F32, "da_23", 2048)
         for n in range(2):
-            drain(multiply(v_23_mx, n, dz_mx, bank(n)), da_23[:, n, :], 1.0 / DECAY)
-        for n in range(2):
-            for h in range(2):
-                scatter_scalar(pa_win[2 + n], j_list, h, da_23[:, n, h * HALF:(h + 1) * HALF])
-        quantise(x_23_woven, x_23_mx, 0, E4M3)
-        finish(0, partial_0, tile([P, TOKENS], F32, "new_m_0", "x_23_woven"))
-        finish(1, partial_1, tile([P, TOKENS], F32, "new_m_1"))
-        db_2 = tile([P, SLOTS], F32, "db_2", "partial_1")
-        nc.vector.tensor_copy(out=db_2[:], in_=multiply(x_23_mx, 0, g_mx, bank(2)))
-        db_3 = tile([P, SLOTS], F32, "db_3")
-        drain(multiply(x_23_mx, 1, g_mx, bank(3)), db_3[:], 1.0)
+            sums = multiply(v_23_mx, n, dz_mx, bank(n))
+            drain(sums.rearrange("p (h c) -> p h c", h=2), da_23[:, :, n, :], 1.0 / DECAY)
         for h in range(2):
-            scatter_scalar(pb_win[3], i_list, h, db_3[:, h * HALF:(h + 1) * HALF])
-        scatter_vector(pb_win[2], i_list, db_2[:])
-        partial_2 = add_early(2, "w_1", halves)
-        partial_3 = add_early(3, "m_2", halves[:1])
-        nc.vector.tensor_tensor(out=partial_3[:, 512:], in0=m_rows[3][:, 512:], in1=pa_win[3][:, 512:], op=ADD)
+            for n in range(2):
+                scatter_scalar(pa_win[2 + n], j_list, h, da_23[:, h, n, :])
+        quantise(x_23_woven, x_23_mx, 0, E4M3)
+        for b in range(2):
+            partial = add_early(b, ("x_23_woven", None)[b])
+            db = tile([P, SLOTS], F32, "db_%d" % (2 + b), "m_%d" % b)
+            nc.vector.tensor_copy(out=db[:], in_=multiply(x_23_mx, b, g_mx, bank(2 + b)))
+            finish(b, partial, tile([P, TOKENS], F32, "new_m_%d" % b))
+            for h in range(2):
+                scatter_scalar(pb_win[2 + b], i_list, h, db[:, h * HALF:(h + 1) * HALF])
+        partial_2 = add_early(2)
+        partial_3 = add_early(3)
         finish(2, partial_2, tile([P, TOKENS], F32, "new_m_2"), halves)
         new_m = tile([P, TOKENS], F32, "new_m_3")
         new_w = tile([P, TOKENS], F32, "new_w_3")

@@ -38,9 +38,9 @@ def tile_attend_gtied_mom_kernel(tc, V, dz, xT, G, mT, wT, offs, joffs, out_0, o
         def tile(shape, dtype, name, over=None):
             return keep.tile(shape, dtype, name=name, tag=over or name, align_bytes=64)
 
-        def load_k_first(src, h, name):
-            raw = tile([P, PACK, HALF], F32, name)
-            nc.sync.dma_start(out=raw[:], in_=src.rearrange("(p j) n -> p j n", j=PACK)[:, :, h * HALF:(h + 1) * HALF])
+        def load_k_first(src, c0, c1, name):
+            raw = tile([P, PACK, c1 - c0], F32, name)
+            nc.sync.dma_start(out=raw[:], in_=src.rearrange("(p j) n -> p j n", j=PACK)[:, :, c0:c1])
             return raw
 
         def load_rows(src, b, name):
@@ -54,33 +54,34 @@ def tile_attend_gtied_mom_kernel(tc, V, dz, xT, G, mT, wT, offs, joffs, out_0, o
             return lst
 
         x_rows, m_rows, w_rows = {}, {}, {}
-        v_01 = load_k_first(V, 0, "v_01")
-        dz_a = load_k_first(dz, 0, "dz_a")
+        v_0 = load_k_first(V, 0, P, "v_0")
+        dz_a = load_k_first(dz, 0, HALF, "dz_a")
+        v_1 = load_k_first(V, P, HALF, "v_1")
         j_list = load_list(joffs, "j_list")
-        dz_b = load_k_first(dz, 1, "dz_b")
+        dz_b = load_k_first(dz, HALF, SLOTS, "dz_b")
         for b in (0, 1):
             x_rows[b] = load_rows(xT, b, "x_%d" % b)
-        g_a = load_k_first(G, 0, "g_a")
-        g_b = load_k_first(G, 1, "g_b")
+        g_a = load_k_first(G, 0, HALF, "g_a")
+        g_b = load_k_first(G, HALF, SLOTS, "g_b")
         i_list = load_list(offs, "i_list")
-        v_23 = load_k_first(V, 1, "v_23")
+        v_23 = load_k_first(V, HALF, SLOTS, "v_23")
         for b in (2, 3):
             x_rows[b] = load_rows(xT, b, "x_%d" % b)
-        for pair in ((0, 1), (2, 3)):
-            for b in pair:
-                m_rows[b] = load_rows(mT, b, "m_%d" % b)
-            for b in pair:
-                w_rows[b] = load_rows(wT, b, "w_%d" % b)
+        for b in range(BLOCKS):
+            m_rows[b] = load_rows(mT, b, "m_%d" % b)
+            w_rows[b] = load_rows(wT, b, "w_%d" % b)
 
         ident = keep.tile([P, P], F32, name="ident")
         make_identity(nc, ident[:])
 
-        pa_win = [tile([P, TOKENS], F32, "pa_win_%d" % b) for b in range(BLOCKS)]
-        pb_win = [tile([P, TOKENS], F32, "pb_win_%d" % n) for n in range(2)] * 2
+        pa_win = [tile([P, TOKENS], F32, "pa_win_%d" % n) for n in range(3)]
+        pb_win = [tile([P, TOKENS], F32, "pb_win_%d" % n) for n in range(3)]
         for win in pa_win:
             nc.vector.memset(win[:], 0.0)
-        for win in pb_win[:2]:
+        for win in pb_win:
             nc.gpsimd.memset(win[:], 0.0)
+        pa_win.append(pa_win[0])
+        pb_win.append(pb_win[0])
 
         def placed(shape, dtype, name, offset):
             return reuse.tile(shape, dtype, name=name, offset=offset, align_bytes=64)
@@ -153,8 +154,7 @@ def tile_attend_gtied_mom_kernel(tc, V, dz, xT, G, mT, wT, offs, joffs, out_0, o
 
         halves = [slice(0, 512), slice(512, TOKENS)]
 
-        def add_early(b, over=None):
-            both = tile([P, TOKENS], F32, "partial_%d" % b, over)
+        def add_early(b, both):
             for cols in halves:
                 nc.vector.tensor_tensor(out=both[:, cols], in0=m_rows[b][:, cols], in1=pa_win[b][:, cols], op=ADD)
             return both
@@ -175,7 +175,9 @@ def tile_attend_gtied_mom_kernel(tc, V, dz, xT, G, mT, wT, offs, joffs, out_0, o
                     out=new_w[:, cols], in0=new_m[:, cols], scalar=-RATE, in1=w_rows[b][:, cols], op0=MULT, op1=ADD
                 )
 
-        def finish(b, both, new_m, pieces=(slice(0, TOKENS),)):
+        def finish(b, both):
+            pieces = [slice(0, TOKENS)]
+            new_m = tile([P, TOKENS], F32, "new_m_%d" % b)
             new_w = tile([P, TOKENS], F32, "new_w_%d" % b)
             momentum(b, both, new_m, halves)
             store(out_0, b, new_m, pieces)
@@ -192,58 +194,61 @@ def tile_attend_gtied_mom_kernel(tc, V, dz, xT, G, mT, wT, offs, joffs, out_0, o
 
         half_woven = [P, HALF, PACK]
         pair_words = [P, 2, 2, P, 2]
-        v_01_woven = weave(v_01, "scalar", tile(half_woven, BF16, "v_01_woven"))
-        dz_a_woven = weave(dz_a, "vector", tile(half_woven, BF16, "dz_a_woven"))
-        quantise(v_01_woven, v_01_mx, 0, E4M3)
-        quantise(dz_a_woven, dz_mx, 0, E5M2)
+        quantise(weave(v_0, "scalar", tile([P, P, PACK], BF16, "v_0_woven")), v_01_mx, 0, E4M3)
+        quantise(weave(dz_a, "vector", tile(half_woven, BF16, "dz_a_woven")), dz_mx, 0, E5M2)
+        quantise(weave(v_1, "scalar", tile([P, P, PACK], BF16, "v_1_woven")), v_01_mx, P, E4M3)
+        dz_b_woven = weave(dz_b, "vector", tile(half_woven, BF16, "dz_b_woven"))
         first_pair(0, (0, 1))
-        quantise(weave(dz_b, "vector", tile(half_woven, BF16, "dz_b_woven")), dz_mx, HALF, E5M2)
+        x_01_pairs = placed(pair_words, BF16, "x_01_pairs", 3072)
+        round_x(0, x_01_pairs)
+        quantise(dz_b_woven, dz_mx, HALF, E5M2)
         first_pair(1, (2, 3))
 
-        x_01_pairs = placed(pair_words, BF16, "x_01_pairs", 1024)
-        round_x(0, x_01_pairs)
         quantise(weave(g_a, "vector", tile(half_woven, BF16, "g_a_woven")), g_mx, 0, E5M2)
         x_01_woven = tile(half_woven, BF16, "x_01_woven")
         turn_x(x_01_pairs, bank(4), "vector", x_01_woven)
-        g_b_woven = weave(g_b, "vector", placed(half_woven, BF16, "g_b_woven", 0))
+        g_b_woven = weave(g_b, "vector", placed(half_woven, BF16, "g_b_woven", 2048))
         quantise(x_01_woven, x_01_mx, 0, E4M3)
         quantise(g_b_woven, g_mx, HALF, E5M2)
         sums_b = [multiply(x_01_mx, b, g_mx, bank(5 + b)) for b in range(2)]
-        v_23_woven = weave(v_23, "vector", placed(half_woven, BF16, "v_23_woven", 2048))
+        v_23_woven = weave(v_23, "vector", placed(half_woven, BF16, "v_23_woven", 4096))
         quantise(v_23_woven, v_23_mx, 0, E4M3)
-        db_01 = [tile([P, SLOTS], F32, "db_%d" % b) for b in range(2)]
-        nc.vector.tensor_copy(out=db_01[0][:], in_=sums_b[0])
-        drain(sums_b[1], db_01[1][:], 1.0)
+        db_0 = tile([P, SLOTS], F32, "db_0")
+        nc.vector.tensor_copy(out=db_0[:], in_=sums_b[0])
         x_23_pairs = placed(pair_words, BF16, "x_23_pairs", 2048)
         round_x(1, x_23_pairs)
-        for b in range(2):
-            scatter_vector(pb_win[b], i_list, db_01[b][:])
+        scatter_vector(pb_win[0], i_list, db_0[:])
 
-        x_23_woven = tile(half_woven, BF16, "x_23_woven")
+        x_23_woven = placed(half_woven, BF16, "x_23_woven", 8192 + 1024)
         turn_x(x_23_pairs, bank(7), "scalar", x_23_woven)
-        da_23 = placed([P, 2, 2, HALF], F32, "da_23", 2048)
+        da_23 = [placed([P, SLOTS], F32, "da_%d" % (2 + n), 1024 + 2048 * n) for n in range(2)]
         for n in range(2):
-            sums = multiply(v_23_mx, n, dz_mx, bank(n))
-            drain(sums.rearrange("p (h c) -> p h c", h=2), da_23[:, :, n, :], 1.0 / DECAY)
-        for h in range(2):
-            for n in range(2):
-                scatter_scalar(pa_win[2 + n], j_list, h, da_23[:, h, n, :])
+            drain(multiply(v_23_mx, n, dz_mx, bank(n)), da_23[n][:], 1.0 / DECAY)
         quantise(x_23_woven, x_23_mx, 0, E4M3)
-        for b in range(2):
-            partial = add_early(b, ("x_23_woven", None)[b])
-            db = tile([P, SLOTS], F32, "db_%d" % (2 + b), "m_%d" % b)
-            nc.vector.tensor_copy(out=db[:], in_=multiply(x_23_mx, b, g_mx, bank(2 + b)))
-            finish(b, partial, tile([P, TOKENS], F32, "new_m_%d" % b))
-            for h in range(2):
-                scatter_scalar(pb_win[2 + b], i_list, h, db[:, h * HALF:(h + 1) * HALF])
-        partial_2 = add_early(2)
-        partial_3 = add_early(3)
-        finish(2, partial_2, tile([P, TOKENS], F32, "new_m_2"), halves)
+        first, second = slice(0, HALF), slice(HALF, SLOTS)
+        scatter_scalar(pa_win[2], j_list, 0, da_23[0][:, first])
+        db_1 = placed([P, SLOTS], F32, "db_1", 8192)
+        drain(sums_b[1], db_1[:], 1.0)
+        db_2 = tile([P, SLOTS], F32, "db_2")
+        drain(multiply(x_23_mx, 0, g_mx, bank(2)), db_2[:], 1.0)
+        finish(0, add_early(0, placed([P, TOKENS], F32, "partial_0", 8192 + 2048)))
+        scatter_scalar(pa_win[2], j_list, 1, da_23[0][:, second])
+        scatter_scalar(pb_win[2], i_list, 0, db_2[:, first])
+        db_3 = tile([P, SLOTS], F32, "db_3")
+        drain(multiply(x_23_mx, 1, g_mx, bank(3)), db_3[:], 1.0)
+        scatter_scalar(pb_win[2], i_list, 1, db_2[:, second])
+        for h, cols in enumerate((first, second)):
+            scatter_scalar(pa_win[3], j_list, h, da_23[1][:, cols])
+            scatter_scalar(pb_win[3], i_list, h, db_3[:, cols])
+        scatter_vector(pb_win[1], i_list, db_1[:])
+        for b in (1, 2):
+            finish(b, add_early(b, tile([P, TOKENS], F32, "partial_%d" % b)))
+        partial_3 = add_early(3, tile([P, TOKENS], F32, "partial_3"))
         new_m = tile([P, TOKENS], F32, "new_m_3")
         new_w = tile([P, TOKENS], F32, "new_w_3")
         for cols in halves:
             momentum(3, partial_3, new_m, [cols])
             store(out_0, 3, new_m, [cols])
-        for cols in halves:
+        for cols in (slice(0, 512), slice(512, 768), slice(768, TOKENS)):
             table(3, new_m, new_w, [cols])
             store(out_1, 3, new_w, [cols])

@@ -5,6 +5,7 @@ from concourse.masks import make_identity
 
 F32 = mybir.dt.float32
 BF16 = mybir.dt.bfloat16
+I32 = mybir.dt.int32
 U32 = mybir.dt.uint32
 U16 = mybir.dt.uint16
 U8 = mybir.dt.uint8
@@ -54,9 +55,8 @@ def tile_attend_gtied_mom_kernel(tc, V, dz, xT, G, mT, wT, offs, joffs, out_0, o
             return lst
 
         x_rows, m_rows, w_rows = {}, {}, {}
-        v_0 = load_k_first(V, 0, P, "v_0")
+        v_01 = load_k_first(V, 0, HALF, "v_01")
         dz_a = load_k_first(dz, 0, HALF, "dz_a")
-        v_1 = load_k_first(V, P, HALF, "v_1")
         j_list = load_list(joffs, "j_list")
         dz_b = load_k_first(dz, HALF, SLOTS, "dz_b")
         for b in (0, 1):
@@ -76,10 +76,9 @@ def tile_attend_gtied_mom_kernel(tc, V, dz, xT, G, mT, wT, offs, joffs, out_0, o
 
         pa_win = [tile([P, TOKENS], F32, "pa_win_%d" % n) for n in range(3)]
         pb_win = [tile([P, TOKENS], F32, "pb_win_%d" % n) for n in range(3)]
-        for win in pa_win:
-            nc.vector.memset(win[:], 0.0)
-        for win in pb_win:
-            nc.gpsimd.memset(win[:], 0.0)
+        for win in pa_win + pb_win[:2]:
+            nc.vector.memset(win[:].bitcast(I32), 0)
+        nc.gpsimd.memset(pb_win[2][:], 0.0)
         pa_win.append(pa_win[0])
         pb_win.append(pb_win[0])
 
@@ -175,9 +174,8 @@ def tile_attend_gtied_mom_kernel(tc, V, dz, xT, G, mT, wT, offs, joffs, out_0, o
                     out=new_w[:, cols], in0=new_m[:, cols], scalar=-RATE, in1=w_rows[b][:, cols], op0=MULT, op1=ADD
                 )
 
-        def finish(b, both):
+        def finish(b, both, new_m):
             pieces = [slice(0, TOKENS)]
-            new_m = tile([P, TOKENS], F32, "new_m_%d" % b)
             new_w = tile([P, TOKENS], F32, "new_w_%d" % b)
             momentum(b, both, new_m, halves)
             store(out_0, b, new_m, pieces)
@@ -194,10 +192,13 @@ def tile_attend_gtied_mom_kernel(tc, V, dz, xT, G, mT, wT, offs, joffs, out_0, o
 
         half_woven = [P, HALF, PACK]
         pair_words = [P, 2, 2, P, 2]
-        quantise(weave(v_0, "scalar", tile([P, P, PACK], BF16, "v_0_woven")), v_01_mx, 0, E4M3)
-        quantise(weave(dz_a, "vector", tile(half_woven, BF16, "dz_a_woven")), dz_mx, 0, E5M2)
-        quantise(weave(v_1, "scalar", tile([P, P, PACK], BF16, "v_1_woven")), v_01_mx, P, E4M3)
-        dz_b_woven = weave(dz_b, "vector", tile(half_woven, BF16, "dz_b_woven"))
+        v_01_woven = weave(v_01, "scalar", tile(half_woven, BF16, "v_01_woven"))
+        dz_a_woven = weave(dz_a, "vector", tile(half_woven, BF16, "dz_a_woven"))
+        quantise(v_01_woven, v_01_mx, 0, E4M3)
+        quantise(dz_a_woven, dz_mx, 0, E5M2)
+        dz_b_woven = tile(half_woven, BF16, "dz_b_woven")
+        weave(dz_b[:, :, 0:P], "vector", dz_b_woven[:, 0:P, :])
+        weave(dz_b[:, :, P:], "scalar", dz_b_woven[:, P:, :])
         first_pair(0, (0, 1))
         x_01_pairs = placed(pair_words, BF16, "x_01_pairs", 3072)
         round_x(0, x_01_pairs)
@@ -219,34 +220,39 @@ def tile_attend_gtied_mom_kernel(tc, V, dz, xT, G, mT, wT, offs, joffs, out_0, o
         round_x(1, x_23_pairs)
         scatter_vector(pb_win[0], i_list, db_0[:])
 
+        first, second = slice(0, HALF), slice(HALF, SLOTS)
+        sums_a2 = multiply(v_23_mx, 0, dz_mx, bank(0))
+        da_2a = tile([P, HALF], F32, "da_2a")
+        drain(sums_a2[:, first], da_2a[:], 1.0 / DECAY)
+        scatter_scalar(pa_win[2], j_list, 0, da_2a[:])
         x_23_woven = placed(half_woven, BF16, "x_23_woven", 8192 + 1024)
         turn_x(x_23_pairs, bank(7), "scalar", x_23_woven)
-        da_23 = [placed([P, SLOTS], F32, "da_%d" % (2 + n), 1024 + 2048 * n) for n in range(2)]
-        for n in range(2):
-            drain(multiply(v_23_mx, n, dz_mx, bank(n)), da_23[n][:], 1.0 / DECAY)
+        da_2b = placed([P, HALF], F32, "da_2b", 2048)
+        drain(sums_a2[:, second], da_2b[:], 1.0 / DECAY)
+        da_3 = placed([P, SLOTS], F32, "da_3", 3072)
+        drain(multiply(v_23_mx, 1, dz_mx, bank(1)), da_3[:], 1.0 / DECAY)
+        partial_0 = add_early(0, tile([P, TOKENS], F32, "partial_0"))
         quantise(x_23_woven, x_23_mx, 0, E4M3)
-        first, second = slice(0, HALF), slice(HALF, SLOTS)
-        scatter_scalar(pa_win[2], j_list, 0, da_23[0][:, first])
         db_1 = placed([P, SLOTS], F32, "db_1", 8192)
         drain(sums_b[1], db_1[:], 1.0)
+        scatter_scalar(pa_win[2], j_list, 1, da_2b[:])
         db_2 = tile([P, SLOTS], F32, "db_2")
         drain(multiply(x_23_mx, 0, g_mx, bank(2)), db_2[:], 1.0)
-        finish(0, add_early(0, placed([P, TOKENS], F32, "partial_0", 8192 + 2048)))
-        scatter_scalar(pa_win[2], j_list, 1, da_23[0][:, second])
+        finish(0, partial_0, placed([P, TOKENS], F32, "new_m_0", 8192 + 2048))
         scatter_scalar(pb_win[2], i_list, 0, db_2[:, first])
         db_3 = tile([P, SLOTS], F32, "db_3")
         drain(multiply(x_23_mx, 1, g_mx, bank(3)), db_3[:], 1.0)
         scatter_scalar(pb_win[2], i_list, 1, db_2[:, second])
         for h, cols in enumerate((first, second)):
-            scatter_scalar(pa_win[3], j_list, h, da_23[1][:, cols])
+            scatter_scalar(pa_win[3], j_list, h, da_3[:, cols])
             scatter_scalar(pb_win[3], i_list, h, db_3[:, cols])
         scatter_vector(pb_win[1], i_list, db_1[:])
         for b in (1, 2):
-            finish(b, add_early(b, tile([P, TOKENS], F32, "partial_%d" % b)))
+            finish(b, add_early(b, tile([P, TOKENS], F32, "partial_%d" % b)), tile([P, TOKENS], F32, "new_m_%d" % b))
         partial_3 = add_early(3, tile([P, TOKENS], F32, "partial_3"))
         new_m = tile([P, TOKENS], F32, "new_m_3")
         new_w = tile([P, TOKENS], F32, "new_w_3")
-        for cols in halves:
+        for cols in (slice(0, 256), slice(256, 512), slice(512, TOKENS)):
             momentum(3, partial_3, new_m, [cols])
             store(out_0, 3, new_m, [cols])
         for cols in (slice(0, 512), slice(512, 768), slice(768, TOKENS)):

@@ -36,16 +36,18 @@ def tile_attend_gtied_mom_kernel(tc, V, dz, xT, G, mT, wT, offs, joffs, out_0, o
         reuse = ctx.enter_context(tc.tile_pool(name="reuse", bufs=1))
         psum = ctx.enter_context(tc.psum_pool(name="psum", bufs=1))
 
-        def tile(shape, dtype, name, over=None):
-            return keep.tile(shape, dtype, name=name, tag=over or name, align_bytes=64)
+        def tile(shape, dtype, name, at=None):
+            if at is None:
+                return keep.tile(shape, dtype, name=name, align_bytes=64)
+            return reuse.tile(shape, dtype, name=name, offset=at, align_bytes=64)
 
-        def load_k_first(src, c0, c1, name):
-            raw = tile([P, PACK, c1 - c0], F32, name)
+        def load_k_first(src, c0, c1, name, at=None):
+            raw = tile([P, PACK, c1 - c0], F32, name, at)
             nc.sync.dma_start(out=raw[:], in_=src.rearrange("(p j) n -> p j n", j=PACK)[:, :, c0:c1])
             return raw
 
-        def load_rows(src, b, name):
-            raw = tile([P, src.shape[1]], F32, name)
+        def load_rows(src, b, name, at=None):
+            raw = tile([P, src.shape[1]], F32, name, at)
             nc.sync.dma_start(out=raw[:], in_=src[b * P:(b + 1) * P, :])
             return raw
 
@@ -54,51 +56,27 @@ def tile_attend_gtied_mom_kernel(tc, V, dz, xT, G, mT, wT, offs, joffs, out_0, o
             nc.sync.dma_start(lst[:], src)
             return lst
 
-        x_rows, m_rows, w_rows = {}, {}, {}
-        v_01 = load_k_first(V, 0, HALF, "v_01")
-        dz_a = load_k_first(dz, 0, HALF, "dz_a")
-        j_list = load_list(joffs, "j_list")
-        dz_b = load_k_first(dz, HALF, SLOTS, "dz_b")
-        for b in (0, 1):
-            x_rows[b] = load_rows(xT, b, "x_%d" % b)
-        g_a = load_k_first(G, 0, HALF, "g_a")
-        g_b = load_k_first(G, HALF, SLOTS, "g_b")
-        i_list = load_list(offs, "i_list")
-        v_23 = load_k_first(V, HALF, SLOTS, "v_23")
-        for b in (2, 3):
-            x_rows[b] = load_rows(xT, b, "x_%d" % b)
-        for b in range(BLOCKS):
-            m_rows[b] = load_rows(mT, b, "m_%d" % b)
-            w_rows[b] = load_rows(wT, b, "w_%d" % b)
-
-        ident = keep.tile([P, P], F32, name="ident")
-        make_identity(nc, ident[:])
-
-        pa_win = [tile([P, TOKENS], F32, "pa_win_%d" % n) for n in range(3)]
-        pb_win = [tile([P, TOKENS], F32, "pb_win_%d" % n) for n in range(3)]
-        for win in pa_win + pb_win[:2]:
-            nc.vector.memset(win[:].bitcast(I32), 0)
-        nc.gpsimd.memset(pb_win[2][:], 0.0)
-        pa_win.append(pa_win[0])
-        pb_win.append(pb_win[0])
-
-        def placed(shape, dtype, name, offset):
-            return reuse.tile(shape, dtype, name=name, offset=offset, align_bytes=64)
-
-        def mx_operand(name, width=SLOTS, over=None):
-            return tile([P, width], U32, name + "_codes", over), tile([P, width], U8, name + "_scales")
-
-        dz_mx, g_mx = [mx_operand(n) for n in ("dz", "g")]
-        v_01_mx, v_23_mx, x_01_mx, x_23_mx = [mx_operand(n, HALF) for n in ("v_01", "v_23", "x_01", "x_23")]
-
-        def weave(raw, engine, woven):
-            dst = woven[:].rearrange("p (c i) t -> p c t i", i=4)
-            src = raw[:].rearrange("p t (c i) -> p c t i", i=4)
+        def copy(engine, dst, src):
             if engine == "vector":
                 nc.vector.tensor_copy(out=dst, in_=src)
             else:
                 nc.scalar.activation(out=dst, in_=src, func=COPY)
-            return woven
+
+        def window(name, engine, at=None):
+            win = tile([P, TOKENS], F32, name, at)
+            if engine == "vector":
+                nc.vector.memset(win[:].bitcast(I32), 0)
+            else:
+                nc.gpsimd.memset(win[:], 0.0)
+            return win
+
+        def mx_operand(name, width, at=None):
+            return tile([P, width], U32, name + "_codes", at), tile([P, width], U8, name + "_scales")
+
+        def weave(raw, engine, woven):
+            dst = woven.rearrange("p (c i) t -> p c t i", i=4)
+            src = raw.rearrange("p t (c i) -> p c t i", i=4)
+            copy(engine, dst, src)
 
         def quantise(woven, operand, c0, fmt):
             codes, scales = operand
@@ -106,29 +84,29 @@ def tile_attend_gtied_mom_kernel(tc, V, dz, xT, G, mT, wT, offs, joffs, out_0, o
             nc.vector.quantize_mx(
                 out=codes[:, cols].bitcast(fmt),
                 scales=scales[:, cols],
-                in_=woven[:].rearrange("p n t -> p (n t)"),
+                in_=woven.rearrange("p n t -> p (n t)"),
             )
 
-        def bank(n, width=SLOTS):
-            return psum.tile([P, SLOTS], F32, name="bank_%d" % n, tag="bank_%d" % n)[:, 0:width]
+        def bank(n):
+            return psum.tile([P, SLOTS], F32, name="bank_%d" % n, tag="bank_%d" % n)
 
-        def round_x(pair, pairs):
-            for n in range(2):
-                src = x_rows[2 * pair + n][:].rearrange("d (p u e) -> d u p e", u=2, e=2)
-                nc.vector.tensor_copy(out=pairs[:, n], in_=src)
+        def round_x(rows, engine, pairs):
+            copy(engine, pairs, rows[:].rearrange("d (p u e) -> d u p e", u=2, e=2))
 
-        def turn_x(pairs, turned, engine, woven):
+        def turn_x(pairs, turned):
             words = pairs[:].rearrange("d n u p e -> d (n u p e)").bitcast(F32)
-            for q in range(4):
+            for q in range(2 * pairs.shape[1]):
                 nc.tensor.transpose(turned[:, q * P:(q + 1) * P], words[:, q * P:(q + 1) * P], ident[:])
-            dst = woven[:].rearrange("p d t -> p (d t)").bitcast(F32).rearrange("p (n d u) -> p n d u", n=2, u=2)
-            src = turned.rearrange("p (n u d) -> p n d u", n=2, u=2)
+
+        def weave_x(turned, n, engine, woven):
+            dst = woven[:].rearrange("p d t -> p (d t)").bitcast(F32).rearrange("p (n d u) -> p n d u", n=n, u=2)
+            src = turned[:, 0:n * HALF].rearrange("p (n u d) -> p n d u", n=n, u=2)
             if engine == "vector":
                 nc.vector.tensor_copy(out=dst, in_=src)
             else:
                 nc.scalar.copy(out=dst, in_=src)
 
-        def multiply(stationary, n, moving, sums, c0=0, c1=SLOTS):
+        def multiply(stationary, n, moving, c0, c1, sums):
             cols = slice(n * P, (n + 1) * P)
             nc.tensor.matmul_mx(
                 out=sums,
@@ -139,122 +117,232 @@ def tile_attend_gtied_mom_kernel(tc, V, dz, xT, G, mT, wT, offs, joffs, out_0, o
                 start=True,
                 stop=True,
             )
-            return sums
 
-        def drain(sums, grad, scale):
-            nc.scalar.activation(out=grad, in_=sums, func=COPY, scale=scale)
+        def drain(engine, sums, grad, scale):
+            if engine == "vector":
+                nc.vector.tensor_scalar(out=grad, in0=sums, scalar1=scale, scalar2=None, op0=MULT)
+            else:
+                nc.scalar.activation(out=grad, in_=sums, func=COPY, scale=scale)
 
-        def scatter_scalar(win, lst, h, grad):
-            cols = slice(h * HALF // 16, (h + 1) * HALF // 16)
-            nc.scalar.activation(out=win[:].indirect(lst[:, cols]), in_=grad, func=COPY)
+        def scatter_scalar(win, lst, s0, s1, grad):
+            nc.scalar.activation(out=win[:].indirect(lst[:, s0 // 16:s1 // 16]), in_=grad, func=COPY)
 
-        def scatter_vector(win, lst, grad):
-            nc.vector.tensor_copy(win[:].indirect(lst[:]), grad)
+        def scatter_vector(win, lst, s0, s1, grad):
+            nc.vector.tensor_copy(win[:].indirect(lst[:, s0 // 16:s1 // 16]), grad)
 
         halves = [slice(0, 512), slice(512, TOKENS)]
+        whole = [slice(0, TOKENS)]
 
-        def add_early(b, both):
-            for cols in halves:
-                nc.vector.tensor_tensor(out=both[:, cols], in0=m_rows[b][:, cols], in1=pa_win[b][:, cols], op=ADD)
+        def add_first(engine, m, win, both, pieces):
+            eng = nc.vector if engine == "vector" else nc.gpsimd
+            for cols in pieces:
+                eng.tensor_tensor(out=both[:, cols], in0=m[:, cols], in1=win[:, cols], op=ADD)
             return both
+
+        def scale_add(dst, src, factor, other, pieces):
+            for cols in pieces:
+                nc.vector.scalar_tensor_tensor(
+                    out=dst[:, cols], in0=src[:, cols], scalar=factor, in1=other[:, cols], op0=MULT, op1=ADD
+                )
 
         def store(dst, b, src, pieces):
             for cols in pieces:
                 nc.sync.dma_start(out=dst[b * P:(b + 1) * P, cols], in_=src[:, cols])
 
-        def momentum(b, both, new_m, pieces):
-            for cols in pieces:
-                nc.vector.scalar_tensor_tensor(
-                    out=new_m[:, cols], in0=both[:, cols], scalar=DECAY, in1=pb_win[b][:, cols], op0=MULT, op1=ADD
-                )
+        m_rows, w_rows = {}, {}
 
-        def table(b, new_m, new_w, pieces):
-            for cols in pieces:
-                nc.vector.scalar_tensor_tensor(
-                    out=new_w[:, cols], in0=new_m[:, cols], scalar=-RATE, in1=w_rows[b][:, cols], op0=MULT, op1=ADD
-                )
+        def load_x(pair):
+            raw = tile([P, 2, K], F32, "x_%d" % pair)
+            rows = xT[pair * HALF:(pair + 1) * HALF, :]
+            nc.sync.dma_start(out=raw[:], in_=rows.rearrange("(n d) r -> d n r", n=2))
+            return raw
 
-        def finish(b, both, new_m):
-            pieces = [slice(0, TOKENS)]
-            new_w = tile([P, TOKENS], F32, "new_w_%d" % b)
-            momentum(b, both, new_m, halves)
-            store(out_0, b, new_m, pieces)
-            table(b, new_m, new_w, halves)
-            store(out_1, b, new_w, pieces)
+        v_01 = load_k_first(V, 0, HALF, "v_01")
+        dz_a = load_k_first(dz, 0, HALF, "dz_a")
+        j_list = load_list(joffs, "j_list")
+        dz_b = load_k_first(dz, HALF, SLOTS, "dz_b")
+        x_raw = [load_x(0)]
+        g_a = load_k_first(G, 0, HALF, "g_a")
+        g_b = load_k_first(G, HALF, SLOTS, "g_b", 16384 + 1984)
+        i_list = load_list(offs, "i_list")
+        x_raw.append(load_x(1))
+        v_23 = load_k_first(V, HALF, SLOTS, "v_23")
+        for rows, src, name, b in ((m_rows, mT, "m", 1), (m_rows, mT, "m", 0), (m_rows, mT, "m", 2), (w_rows, wT, "w", 0),
+                                   (w_rows, wT, "w", 2), (w_rows, wT, "w", 1), (m_rows, mT, "m", 3), (w_rows, wT, "w", 3)):
+            rows[b] = load_rows(src, b, "%s_%d" % (name, b))
+
+        ident = keep.tile([P, P], F32, name="ident")
+        make_identity(nc, ident[:])
+
+        pa_win = [window("pa_win_%d" % n, "vector") for n in range(3)]
+        pb_win = [window("pb_win_%d" % n, "vector" if n < 0 else "gpsimd") for n in range(3)]
+        pa_win.append(pa_win[0])
+        pb_win.append(pb_win[0])
+
+        dz_mx = mx_operand("dz", SLOTS)
+        v_01_mx, x_01_mx, x_23_mx = [mx_operand(n, HALF) for n in ("v_01", "x_01", "x_23")]
+        first, second = slice(0, HALF), slice(HALF, SLOTS)
 
         def first_pair(h, banks):
             grads = tile([P, 2, HALF], F32, "da_01_%d" % h)
             for b in range(2):
-                sums = multiply(v_01_mx, b, dz_mx, bank(banks[b], HALF), h * HALF, (h + 1) * HALF)
-                drain(sums, grads[:, b, :], 1.0 / DECAY)
+                sums = bank(banks[b])[:, first]
+                multiply(v_01_mx, b, dz_mx, h * HALF, (h + 1) * HALF, sums)
+                drain("scalar", sums, grads[:, b, :], (1.0, 1.0 / DECAY)[b])
             for b in range(2):
-                scatter_scalar(pa_win[b], j_list, h, grads[:, b, :])
+                scatter_scalar(pa_win[b], j_list, h * HALF, (h + 1) * HALF, grads[:, b, :])
 
-        half_woven = [P, HALF, PACK]
+        def product(stationary, n, moving, n_bank):
+            sums = bank(n_bank)
+            multiply(stationary, n, moving, 0, SLOTS, sums[:])
+            return sums
+
+        def woven_tile(name, at=None, width=HALF):
+            return tile([P, width, PACK], BF16, name, at)
+
+        def round_pair(raw, pairs):
+            nc.vector.tensor_copy(out=pairs[:], in_=raw[:].rearrange("d n (p u e) -> d n u p e", u=2, e=2))
+
         pair_words = [P, 2, 2, P, 2]
-        v_01_woven = weave(v_01, "scalar", tile(half_woven, BF16, "v_01_woven"))
-        dz_a_woven = weave(dz_a, "vector", tile(half_woven, BF16, "dz_a_woven"))
-        quantise(v_01_woven, v_01_mx, 0, E4M3)
-        quantise(dz_a_woven, dz_mx, 0, E5M2)
-        dz_b_woven = tile(half_woven, BF16, "dz_b_woven")
+        v_01_woven = woven_tile("v_01_woven")
+        weave(v_01[:], "scalar", v_01_woven[:])
+        dz_a_woven = woven_tile("dz_a_woven")
+        weave(dz_a[:, :, 0:192], "vector", dz_a_woven[:, 0:192, :])
+        weave(dz_a[:, :, 192:], "scalar", dz_a_woven[:, 192:, :])
+        quantise(v_01_woven[:], v_01_mx, 0, E4M3)
+        quantise(dz_a_woven[:], dz_mx, 0, E5M2)
+        dz_b_woven = woven_tile("dz_b_woven")
         weave(dz_b[:, :, 0:P], "vector", dz_b_woven[:, 0:P, :])
         weave(dz_b[:, :, P:], "scalar", dz_b_woven[:, P:, :])
         first_pair(0, (0, 1))
-        x_01_pairs = placed(pair_words, BF16, "x_01_pairs", 3072)
-        round_x(0, x_01_pairs)
-        quantise(dz_b_woven, dz_mx, HALF, E5M2)
+        x_01_pairs = tile(pair_words, BF16, "x_01_pairs", 4096)
+        round_pair(x_raw[0], x_01_pairs)
+        quantise(dz_b_woven[:], dz_mx, HALF, E5M2)
+        turned_01 = bank(4)
+        turn_x(x_01_pairs, turned_01)
         first_pair(1, (2, 3))
+        g_a_woven = woven_tile("g_a_woven")
+        weave(g_a[:], "vector", g_a_woven[:])
+        x_01_woven = woven_tile("x_01_woven")
+        weave_x(turned_01, 2, "vector", x_01_woven)
+        g_b_woven = woven_tile("g_b_woven", 3072)
+        weave(g_b[:], "vector", g_b_woven[:])
+        g_mx = mx_operand("g", SLOTS, 5120)
+        quantise(g_a_woven[:], g_mx, 0, E5M2)
+        x_23_pairs = tile(pair_words, BF16, "x_23_pairs", 16384)
+        round_pair(x_raw[1], x_23_pairs)
+        turned_23 = bank(5)
+        turn_x(x_23_pairs, turned_23)
+        quantise(x_01_woven[:], x_01_mx, 0, E4M3)
+        quantise(g_b_woven[:], g_mx, HALF, E5M2)
+        sums_b0 = product(x_01_mx, 0, g_mx, 4)
+        v_23_woven = woven_tile("v_23_woven", 16384 + 4032)
+        weave(v_23[:], "vector", v_23_woven[:])
+        x_23_woven = woven_tile("x_23_woven")
+        weave_x(turned_23, 2, "vector", x_23_woven)
+        v_23_mx = mx_operand("v_23", HALF, 16384)
+        quantise(v_23_woven[:], v_23_mx, 0, E4M3)
+        db_0 = tile([P, SLOTS], F32, "db_0", 16384 + 1984)
+        drain("vector", sums_b0[:], db_0[:], 1.0)
+        quantise(x_23_woven[:], x_23_mx, 0, E4M3)
+        scatter_vector(pb_win[0], i_list, 0, SLOTS, db_0[:])
+        sums_b1 = product(x_01_mx, 1, g_mx, 2)
+        sums_a2 = product(v_23_mx, 0, dz_mx, 0)
+        sums_b2 = product(x_23_mx, 0, g_mx, 1)
 
-        quantise(weave(g_a, "vector", tile(half_woven, BF16, "g_a_woven")), g_mx, 0, E5M2)
-        x_01_woven = tile(half_woven, BF16, "x_01_woven")
-        turn_x(x_01_pairs, bank(4), "vector", x_01_woven)
-        g_b_woven = weave(g_b, "vector", placed(half_woven, BF16, "g_b_woven", 2048))
-        quantise(x_01_woven, x_01_mx, 0, E4M3)
-        quantise(g_b_woven, g_mx, HALF, E5M2)
-        sums_b = [multiply(x_01_mx, b, g_mx, bank(5 + b)) for b in range(2)]
-        v_23_woven = weave(v_23, "vector", placed(half_woven, BF16, "v_23_woven", 4096))
-        quantise(v_23_woven, v_23_mx, 0, E4M3)
-        db_0 = tile([P, SLOTS], F32, "db_0")
-        nc.vector.tensor_copy(out=db_0[:], in_=sums_b[0])
-        x_23_pairs = placed(pair_words, BF16, "x_23_pairs", 2048)
-        round_x(1, x_23_pairs)
-        scatter_vector(pb_win[0], i_list, db_0[:])
-
-        first, second = slice(0, HALF), slice(HALF, SLOTS)
-        sums_a2 = multiply(v_23_mx, 0, dz_mx, bank(0))
-        da_2a = tile([P, HALF], F32, "da_2a")
-        drain(sums_a2[:, first], da_2a[:], 1.0 / DECAY)
-        scatter_scalar(pa_win[2], j_list, 0, da_2a[:])
-        x_23_woven = placed(half_woven, BF16, "x_23_woven", 8192 + 1024)
-        turn_x(x_23_pairs, bank(7), "scalar", x_23_woven)
-        da_2b = placed([P, HALF], F32, "da_2b", 2048)
-        drain(sums_a2[:, second], da_2b[:], 1.0 / DECAY)
-        da_3 = placed([P, SLOTS], F32, "da_3", 3072)
-        drain(multiply(v_23_mx, 1, dz_mx, bank(1)), da_3[:], 1.0 / DECAY)
-        partial_0 = add_early(0, tile([P, TOKENS], F32, "partial_0"))
-        quantise(x_23_woven, x_23_mx, 0, E4M3)
-        db_1 = placed([P, SLOTS], F32, "db_1", 8192)
-        drain(sums_b[1], db_1[:], 1.0)
-        scatter_scalar(pa_win[2], j_list, 1, da_2b[:])
+        da_2 = tile([P, SLOTS], F32, "da_2")
+        for cols in (first, second):
+            drain("scalar", sums_a2[:, cols], da_2[:, cols], 1.0 / DECAY)
+        scatter_scalar(pa_win[2], j_list, 0, HALF, da_2[:, first])
         db_2 = tile([P, SLOTS], F32, "db_2")
-        drain(multiply(x_23_mx, 0, g_mx, bank(2)), db_2[:], 1.0)
-        finish(0, partial_0, placed([P, TOKENS], F32, "new_m_0", 8192 + 2048))
-        scatter_scalar(pb_win[2], i_list, 0, db_2[:, first])
-        db_3 = tile([P, SLOTS], F32, "db_3")
-        drain(multiply(x_23_mx, 1, g_mx, bank(3)), db_3[:], 1.0)
-        scatter_scalar(pb_win[2], i_list, 1, db_2[:, second])
-        for h, cols in enumerate((first, second)):
-            scatter_scalar(pa_win[3], j_list, h, da_3[:, cols])
-            scatter_scalar(pb_win[3], i_list, h, db_3[:, cols])
-        scatter_vector(pb_win[1], i_list, db_1[:])
-        for b in (1, 2):
-            finish(b, add_early(b, tile([P, TOKENS], F32, "partial_%d" % b)), tile([P, TOKENS], F32, "new_m_%d" % b))
-        partial_3 = add_early(3, tile([P, TOKENS], F32, "partial_3"))
-        new_m = tile([P, TOKENS], F32, "new_m_3")
-        new_w = tile([P, TOKENS], F32, "new_w_3")
+        drain("scalar", sums_b2[:], db_2[:], 1.0)
+        scatter_scalar(pa_win[2], j_list, HALF, SLOTS, da_2[:, second])
+        scatter_scalar(pb_win[2], i_list, 0, HALF, db_2[:, first])
+        sums_y = bank(3)
+        multiply(x_23_mx, 1, g_mx, 0, HALF, sums_y[:, first])
+        multiply(v_23_mx, 1, dz_mx, 0, HALF, sums_y[:, second])
+
+        turned = [bank(0), bank(1)]
+        for win, opens in ((pa_win[0], True), (pb_win[0], False)):
+            for h in range(2):
+                for q in range(4):
+                    c = (4 * h + q) * P
+                    nc.tensor.matmul(turned[h][:, q * P:(q + 1) * P], lhsT=win[:, c:c + P], rhs=ident[:],
+                                     start=(opens and q == 0), stop=(not opens and q == 3), is_transpose=True)
+
+        share = 768
+        early = tile([P, TOKENS + share], F32, "early", 16384 + 3968)
+        partial_1, partial_2g = early[:, 0:TOKENS], early[:, TOKENS:]
+        nc.gpsimd.tensor_tensor(out=partial_1[:], in0=m_rows[1][:], in1=pa_win[1][:], op=ADD)
+        nc.gpsimd.tensor_tensor(out=partial_2g[:], in0=m_rows[2][:, 0:share], in1=pa_win[2][:, 0:share], op=ADD)
+
+        grads_y = tile([P, SLOTS], F32, "grads_y")
+        drain("vector", sums_y[:], grads_y[:], 1.0)
+        own = 224
+        db_1s = tile([P, SLOTS - own], F32, "db_1s", 16384 + 1024)
+        drain("vector", sums_b1[:, own:], db_1s[:], 1.0)
+        both_t = [tile([P, SLOTS], F32, "both_t_%d" % h, (None, 36864)[h]) for h in range(2)]
+        for h in range(2):
+            nc.vector.tensor_copy(out=both_t[h][:], in_=turned[h][:])
+        new_m = [tile([P, TOKENS], F32, "new_m_%d" % b, (None, None, 36864 + 1984, None)[b]) for b in range(BLOCKS)]
+        new_w = [tile([P, TOKENS], F32, "new_w_%d" % b) for b in range(BLOCKS)]
+
+        def turn_back(h):
+            both = bank(6 + h)
+            for q in range(4):
+                nc.tensor.transpose(both[:, q * P:(q + 1) * P], both_t[h][:, q * P:(q + 1) * P], ident[:])
+            return both
+
+        def momentum_0(h, both):
+            nc.vector.scalar_tensor_tensor(
+                out=new_m[0][:, halves[h]], in0=m_rows[0][:, halves[h]], scalar=DECAY, in1=both[:], op0=MULT, op1=ADD
+            )
+
+        momentum_0(0, turn_back(0))
+        store(out_0, 0, new_m[0], halves[:1])
+        sums_z = bank(1)
+        multiply(x_23_mx, 1, g_mx, HALF, SLOTS, sums_z[:, first])
+        multiply(v_23_mx, 1, dz_mx, HALF, SLOTS, sums_z[:, second])
+        grads_z = tile([P, SLOTS], F32, "grads_z")
+        drain("vector", sums_z[:], grads_z[:], 1.0)
+        momentum_0(1, turn_back(1))
+        store(out_0, 0, new_m[0], halves[1:])
+        db_1v = tile([P, own], F32, "db_1v", 36864 + 64 - 4 * own)
+        drain("vector", sums_b1[:, 0:own], db_1v[:], 1.0)
+
+        scatter_scalar(pb_win[1], i_list, own, SLOTS, db_1s[:])
+        scatter_scalar(pb_win[2], i_list, HALF, SLOTS, db_2[:, second])
+        scatter_scalar(pa_win[3], j_list, 0, HALF, grads_y[:, second])
+        scatter_scalar(pb_win[3], i_list, 0, HALF, grads_y[:, first])
+        scatter_scalar(pa_win[3], j_list, HALF, SLOTS, grads_z[:, second])
+        scatter_scalar(pb_win[3], i_list, HALF, SLOTS, grads_z[:, first])
+
+        def table(b, pieces, stores):
+            for cols in stores:
+                scale_add(new_w[b], new_m[b], -RATE, w_rows[b], [c for c in pieces if cols.start <= c.start < cols.stop])
+                store(out_1, b, new_w[b], [cols])
+
+        def momentum_2(part, cols):
+            nc.vector.scalar_tensor_tensor(
+                out=new_m[2][:, cols], in0=part, scalar=DECAY, in1=pb_win[2][:, cols], op0=MULT, op1=ADD
+            )
+
+        by_gpsimd, by_vector = slice(0, share), slice(share, TOKENS)
+        partial_2v = tile([P, TOKENS - share], F32, "partial_2v", 36864 + 64)
+        nc.vector.tensor_tensor(out=partial_2v[:], in0=m_rows[2][:, by_vector], in1=pa_win[2][:, by_vector], op=ADD)
+        table(0, whole, whole)
+        scatter_vector(pb_win[1], i_list, 0, own, db_1v[:])
+        momentum_2(partial_2g, by_gpsimd)
+        momentum_2(partial_2v[:], by_vector)
+        store(out_0, 2, new_m[2], whole)
+        scale_add(new_m[1], partial_1, DECAY, pb_win[1], whole)
+        store(out_0, 1, new_m[1], whole)
+        table(2, whole, whole)
+        table(1, whole, whole)
+        partial_3 = tile([P, TOKENS], F32, "partial_3", 36864 + 64)
+        scale_add(partial_3, m_rows[3], DECAY, pa_win[3], halves)
         for cols in (slice(0, 256), slice(256, 512), slice(512, TOKENS)):
-            momentum(3, partial_3, new_m, [cols])
-            store(out_0, 3, new_m, [cols])
-        for cols in (slice(0, 512), slice(512, 768), slice(768, TOKENS)):
-            table(3, new_m, new_w, [cols])
-            store(out_1, 3, new_w, [cols])
+            nc.vector.tensor_tensor(out=new_m[3][:, cols], in0=partial_3[:, cols], in1=pb_win[3][:, cols], op=ADD)
+            store(out_0, 3, new_m[3], [cols])
+        last = [slice(0, 512), slice(512, 768), slice(768, TOKENS)]
+        table(3, last, last)

@@ -173,9 +173,11 @@ def tile_attend_gtied_mom_kernel(tc, V, dz, xT, G, mT, wT, offs, joffs, out_0, o
 
         ident = keep.tile([P, P], F32, name="ident")
         make_identity(nc, ident[:])
+        ident_fwd = tile([P, P], F32, "ident_fwd", 61440)
+        nc.scalar.copy(out=ident_fwd[:], in_=ident[:])
 
         pa_win = [window("pa_win_%d" % n, "vector") for n in range(3)]
-        pb_win = [window("pb_win_%d" % n, "vector" if n < 0 else "gpsimd") for n in range(3)]
+        pb_win = [window("pb_win_%d" % n, "vector" if n < 1 else "gpsimd") for n in range(3)]
         pa_win.append(pa_win[0])
         pb_win.append(pb_win[0])
 
@@ -236,28 +238,31 @@ def tile_attend_gtied_mom_kernel(tc, V, dz, xT, G, mT, wT, offs, joffs, out_0, o
         quantise(x_01_woven[:], x_01_mx, 0, E4M3)
         quantise(g_b_woven[:], g_mx, HALF, E5M2)
         sums_b0 = product(x_01_mx, 0, g_mx, 4)
+        sums_b1 = product(x_01_mx, 1, g_mx, 2)
         v_23_woven = woven_tile("v_23_woven", 16384 + 4032)
         weave(v_23[:], "vector", v_23_woven[:])
-        x_23_woven = woven_tile("x_23_woven")
+        x_23_woven = woven_tile("x_23_woven", 53248)
         weave_x(turned_23, 2, "vector", x_23_woven)
-        v_23_mx = mx_operand("v_23", HALF, 16384)
+        v_23_mx = mx_operand("v_23", HALF, 16384 + 64)
         quantise(v_23_woven[:], v_23_mx, 0, E4M3)
-        db_0 = tile([P, SLOTS], F32, "db_0", 16384 + 1984)
+        db_0 = tile([P, SLOTS], F32, "db_0", 16384 - 1984)
         drain("vector", sums_b0[:], db_0[:], 1.0)
         quantise(x_23_woven[:], x_23_mx, 0, E4M3)
+        own = 256
+        db_1v = tile([P, own], F32, "db_1v", 16384 + 1088)
+        drain("vector", sums_b1[:, 0:own], db_1v[:], 1.0)
         scatter_vector(pb_win[0], i_list, 0, SLOTS, db_0[:])
-        sums_b1 = product(x_01_mx, 1, g_mx, 2)
+        scatter_vector(pb_win[1], i_list, 0, own, db_1v[:])
         sums_a2 = product(v_23_mx, 0, dz_mx, 0)
         sums_b2 = product(x_23_mx, 0, g_mx, 1)
 
-        da_2 = tile([P, SLOTS], F32, "da_2")
-        for cols in (first, second):
-            drain("scalar", sums_a2[:, cols], da_2[:, cols], 1.0 / DECAY)
-        scatter_scalar(pa_win[2], j_list, 0, HALF, da_2[:, first])
+        da_2 = tile([P, SLOTS], F32, "da_2", 53248)
+        drain("scalar", sums_a2[:], da_2[:], 1.0 / DECAY)
         db_2 = tile([P, SLOTS], F32, "db_2")
         drain("scalar", sums_b2[:], db_2[:], 1.0)
-        scatter_scalar(pa_win[2], j_list, HALF, SLOTS, da_2[:, second])
-        scatter_scalar(pb_win[2], i_list, 0, HALF, db_2[:, first])
+        for cols in (first, second):
+            scatter_scalar(pa_win[2], j_list, cols.start, cols.stop, da_2[:, cols])
+            scatter_scalar(pb_win[2], i_list, cols.start, cols.stop, db_2[:, cols])
         sums_y = bank(3)
         multiply(x_23_mx, 1, g_mx, 0, HALF, sums_y[:, first])
         multiply(v_23_mx, 1, dz_mx, 0, HALF, sums_y[:, second])
@@ -267,20 +272,15 @@ def tile_attend_gtied_mom_kernel(tc, V, dz, xT, G, mT, wT, offs, joffs, out_0, o
             for h in range(2):
                 for q in range(4):
                     c = (4 * h + q) * P
-                    nc.tensor.matmul(turned[h][:, q * P:(q + 1) * P], lhsT=win[:, c:c + P], rhs=ident[:],
+                    nc.tensor.matmul(turned[h][:, q * P:(q + 1) * P], lhsT=win[:, c:c + P], rhs=ident_fwd[:],
                                      start=(opens and q == 0), stop=(not opens and q == 3), is_transpose=True)
 
-        share = 768
-        early = tile([P, TOKENS + share], F32, "early", 16384 + 3968)
+        share = 640
+        early = tile([P, TOKENS + share], F32, "early", 16384 + 1152)
         partial_1, partial_2g = early[:, 0:TOKENS], early[:, TOKENS:]
         nc.gpsimd.tensor_tensor(out=partial_1[:], in0=m_rows[1][:], in1=pa_win[1][:], op=ADD)
         nc.gpsimd.tensor_tensor(out=partial_2g[:], in0=m_rows[2][:, 0:share], in1=pa_win[2][:, 0:share], op=ADD)
 
-        grads_y = tile([P, SLOTS], F32, "grads_y")
-        drain("vector", sums_y[:], grads_y[:], 1.0)
-        own = 224
-        db_1s = tile([P, SLOTS - own], F32, "db_1s", 16384 + 1024)
-        drain("vector", sums_b1[:, own:], db_1s[:], 1.0)
         both_t = [tile([P, SLOTS], F32, "both_t_%d" % h, (None, 36864)[h]) for h in range(2)]
         for h in range(2):
             nc.vector.tensor_copy(out=both_t[h][:], in_=turned[h][:])
@@ -298,6 +298,10 @@ def tile_attend_gtied_mom_kernel(tc, V, dz, xT, G, mT, wT, offs, joffs, out_0, o
                 out=new_m[0][:, halves[h]], in0=m_rows[0][:, halves[h]], scalar=DECAY, in1=both[:], op0=MULT, op1=ADD
             )
 
+        db_1s = tile([P, SLOTS - own], F32, "db_1s", 61440 + 64)
+        drain("vector", sums_b1[:, own:], db_1s[:], 1.0)
+        grads_y = tile([P, SLOTS], F32, "grads_y", 61440 - 1984)
+        drain("vector", sums_y[:], grads_y[:], 1.0)
         momentum_0(0, turn_back(0))
         store(out_0, 0, new_m[0], halves[:1])
         sums_z = bank(1)
@@ -307,11 +311,8 @@ def tile_attend_gtied_mom_kernel(tc, V, dz, xT, G, mT, wT, offs, joffs, out_0, o
         drain("vector", sums_z[:], grads_z[:], 1.0)
         momentum_0(1, turn_back(1))
         store(out_0, 0, new_m[0], halves[1:])
-        db_1v = tile([P, own], F32, "db_1v", 36864 + 64 - 4 * own)
-        drain("vector", sums_b1[:, 0:own], db_1v[:], 1.0)
 
         scatter_scalar(pb_win[1], i_list, own, SLOTS, db_1s[:])
-        scatter_scalar(pb_win[2], i_list, HALF, SLOTS, db_2[:, second])
         scatter_scalar(pa_win[3], j_list, 0, HALF, grads_y[:, second])
         scatter_scalar(pb_win[3], i_list, 0, HALF, grads_y[:, first])
         scatter_scalar(pa_win[3], j_list, HALF, SLOTS, grads_z[:, second])
@@ -331,7 +332,6 @@ def tile_attend_gtied_mom_kernel(tc, V, dz, xT, G, mT, wT, offs, joffs, out_0, o
         partial_2v = tile([P, TOKENS - share], F32, "partial_2v", 36864 + 64)
         nc.vector.tensor_tensor(out=partial_2v[:], in0=m_rows[2][:, by_vector], in1=pa_win[2][:, by_vector], op=ADD)
         table(0, whole, whole)
-        scatter_vector(pb_win[1], i_list, 0, own, db_1v[:])
         momentum_2(partial_2g, by_gpsimd)
         momentum_2(partial_2v[:], by_vector)
         store(out_0, 2, new_m[2], whole)

@@ -267,6 +267,9 @@ def tile_attend_gtied_mom_kernel(tc, V, dz, xT, G, mT, wT, offs, joffs, out_0, o
         multiply(x_23_mx, 1, g_mx, 0, HALF, sums_y[:, first])
         multiply(v_23_mx, 1, dz_mx, 0, HALF, sums_y[:, second])
 
+        sums_z = bank(5)
+        multiply(x_23_mx, 1, g_mx, HALF, SLOTS, sums_z[:, first])
+        multiply(v_23_mx, 1, dz_mx, HALF, SLOTS, sums_z[:, second])
         turned = [bank(0), bank(1)]
         for win, opens in ((pa_win[0], True), (pb_win[0], False)):
             for h in range(2):
@@ -300,17 +303,13 @@ def tile_attend_gtied_mom_kernel(tc, V, dz, xT, G, mT, wT, offs, joffs, out_0, o
 
         db_1s = tile([P, SLOTS - own], F32, "db_1s", 61440 + 64)
         drain("vector", sums_b1[:, own:], db_1s[:], 1.0)
-        grads_y = tile([P, SLOTS], F32, "grads_y", 61440 - 1984)
-        drain("vector", sums_y[:], grads_y[:], 1.0)
-        momentum_0(0, turn_back(0))
-        store(out_0, 0, new_m[0], halves[:1])
-        sums_z = bank(1)
-        multiply(x_23_mx, 1, g_mx, HALF, SLOTS, sums_z[:, first])
-        multiply(v_23_mx, 1, dz_mx, HALF, SLOTS, sums_z[:, second])
-        grads_z = tile([P, SLOTS], F32, "grads_z")
-        drain("vector", sums_z[:], grads_z[:], 1.0)
-        momentum_0(1, turn_back(1))
-        store(out_0, 0, new_m[0], halves[1:])
+        grads_3 = tile([P, 2, SLOTS], F32, "grads_3", 61440 + 64 - 4096)
+        grads_y, grads_z = grads_3[:, 0, :], grads_3[:, 1, :]
+        drain("vector", sums_y[:], grads_y, 1.0)
+        drain("vector", sums_z[:], grads_z, 1.0)
+        for h in range(2):
+            momentum_0(h, turn_back(h))
+            store(out_0, 0, new_m[0], halves[h:h + 1])
 
         scatter_scalar(pb_win[1], i_list, own, SLOTS, db_1s[:])
         scatter_scalar(pa_win[3], j_list, 0, HALF, grads_y[:, second])

@@ -124,8 +124,8 @@ def tile_attend_gtied_mom_kernel(tc, V, dz, xT, G, mT, wT, offs, joffs, out_0, o
             else:
                 nc.scalar.activation(out=grad, in_=sums, func=COPY, scale=scale)
 
-        def scatter_scalar(win, lst, s0, s1, grad):
-            nc.scalar.activation(out=win[:].indirect(lst[:, s0 // 16:s1 // 16]), in_=grad, func=COPY)
+        def scatter_scalar(win, lst, s0, s1, grad, scale=1.0):
+            nc.scalar.activation(out=win[:].indirect(lst[:, s0 // 16:s1 // 16]), in_=grad, func=COPY, scale=scale)
 
         def scatter_vector(win, lst, s0, s1, grad):
             nc.vector.tensor_copy(win[:].indirect(lst[:, s0 // 16:s1 // 16]), grad)
@@ -241,28 +241,34 @@ def tile_attend_gtied_mom_kernel(tc, V, dz, xT, G, mT, wT, offs, joffs, out_0, o
         sums_b1 = product(x_01_mx, 1, g_mx, 2)
         v_23_woven = woven_tile("v_23_woven", 16384 + 4032)
         weave(v_23[:], "vector", v_23_woven[:])
-        x_23_woven = woven_tile("x_23_woven", 53248)
+        x_23_woven = woven_tile("x_23_woven")
         weave_x(turned_23, 2, "vector", x_23_woven)
         v_23_mx = mx_operand("v_23", HALF, 16384 + 64)
         quantise(v_23_woven[:], v_23_mx, 0, E4M3)
         db_0 = tile([P, SLOTS], F32, "db_0", 16384 - 1984)
         drain("vector", sums_b0[:], db_0[:], 1.0)
         quantise(x_23_woven[:], x_23_mx, 0, E4M3)
-        own = 256
+        own = 224
         db_1v = tile([P, own], F32, "db_1v", 16384 + 1088)
         drain("vector", sums_b1[:, 0:own], db_1v[:], 1.0)
         scatter_vector(pb_win[0], i_list, 0, SLOTS, db_0[:])
         scatter_vector(pb_win[1], i_list, 0, own, db_1v[:])
-        sums_a2 = product(v_23_mx, 0, dz_mx, 0)
-        sums_b2 = product(x_23_mx, 0, g_mx, 1)
 
-        da_2 = tile([P, SLOTS], F32, "da_2", 53248)
-        drain("scalar", sums_a2[:], da_2[:], 1.0 / DECAY)
-        db_2 = tile([P, SLOTS], F32, "db_2")
-        drain("scalar", sums_b2[:], db_2[:], 1.0)
-        for cols in (first, second):
-            scatter_scalar(pa_win[2], j_list, cols.start, cols.stop, da_2[:, cols])
-            scatter_scalar(pb_win[2], i_list, cols.start, cols.stop, db_2[:, cols])
+        grads_2 = tile([P, 4, HALF], F32, "grads_2")
+        sums = bank(0)
+        multiply(v_23_mx, 0, dz_mx, 0, HALF, sums[:, first])
+        drain("scalar", sums[:, first], grads_2[:, 0, :], 1.0)
+        scatter_scalar(pa_win[2], j_list, 0, HALF, grads_2[:, 0, :], 1.0 / DECAY)
+        sums = bank(1)
+        multiply(v_23_mx, 0, dz_mx, HALF, SLOTS, sums[:, first])
+        multiply(x_23_mx, 0, g_mx, 0, HALF, sums[:, second])
+        drain("scalar", sums[:], grads_2[:, 1:3, :].rearrange("p n s -> p (n s)"), 1.0)
+        sums = bank(6)
+        multiply(x_23_mx, 0, g_mx, HALF, SLOTS, sums[:, first])
+        drain("scalar", sums[:, first], grads_2[:, 3, :], 1.0)
+        scatter_scalar(pb_win[2], i_list, 0, HALF, grads_2[:, 2, :])
+        scatter_scalar(pa_win[2], j_list, HALF, SLOTS, grads_2[:, 1, :], 1.0 / DECAY)
+        scatter_scalar(pb_win[2], i_list, HALF, SLOTS, grads_2[:, 3, :])
         sums_y = bank(3)
         multiply(x_23_mx, 1, g_mx, 0, HALF, sums_y[:, first])
         multiply(v_23_mx, 1, dz_mx, 0, HALF, sums_y[:, second])
@@ -270,7 +276,7 @@ def tile_attend_gtied_mom_kernel(tc, V, dz, xT, G, mT, wT, offs, joffs, out_0, o
         sums_z = bank(5)
         multiply(x_23_mx, 1, g_mx, HALF, SLOTS, sums_z[:, first])
         multiply(v_23_mx, 1, dz_mx, HALF, SLOTS, sums_z[:, second])
-        turned = [bank(0), bank(1)]
+        turned = [bank(0), bank(4)]
         for win, opens in ((pa_win[0], True), (pb_win[0], False)):
             for h in range(2):
                 for q in range(4):
@@ -278,7 +284,7 @@ def tile_attend_gtied_mom_kernel(tc, V, dz, xT, G, mT, wT, offs, joffs, out_0, o
                     nc.tensor.matmul(turned[h][:, q * P:(q + 1) * P], lhsT=win[:, c:c + P], rhs=ident_fwd[:],
                                      start=(opens and q == 0), stop=(not opens and q == 3), is_transpose=True)
 
-        share = 640
+        share = 576
         early = tile([P, TOKENS + share], F32, "early", 16384 + 1152)
         partial_1, partial_2g = early[:, 0:TOKENS], early[:, TOKENS:]
         nc.gpsimd.tensor_tensor(out=partial_1[:], in0=m_rows[1][:], in1=pa_win[1][:], op=ADD)
@@ -328,7 +334,7 @@ def tile_attend_gtied_mom_kernel(tc, V, dz, xT, G, mT, wT, offs, joffs, out_0, o
             )
 
         by_gpsimd, by_vector = slice(0, share), slice(share, TOKENS)
-        partial_2v = tile([P, TOKENS - share], F32, "partial_2v", 36864 + 64)
+        partial_2v = tile([P, TOKENS - share], F32, "partial_2v", 36864 + 64 - 4 * (TOKENS - share))
         nc.vector.tensor_tensor(out=partial_2v[:], in0=m_rows[2][:, by_vector], in1=pa_win[2][:, by_vector], op=ADD)
         table(0, whole, whole)
         momentum_2(partial_2g, by_gpsimd)

@@ -248,7 +248,7 @@ def tile_attend_gtied_mom_kernel(tc, V, dz, xT, G, mT, wT, offs, joffs, out_0, o
         db_0 = tile([P, SLOTS], F32, "db_0", 16384 - 1984)
         drain("vector", sums_b0[:], db_0[:], 1.0)
         quantise(x_23_woven[:], x_23_mx, 0, E4M3)
-        own = 224
+        own = 288
         db_1v = tile([P, own], F32, "db_1v", 16384 + 1088)
         drain("vector", sums_b1[:, 0:own], db_1v[:], 1.0)
         scatter_vector(pb_win[0], i_list, 0, SLOTS, db_0[:])
@@ -284,7 +284,7 @@ def tile_attend_gtied_mom_kernel(tc, V, dz, xT, G, mT, wT, offs, joffs, out_0, o
                     nc.tensor.matmul(turned[h][:, q * P:(q + 1) * P], lhsT=win[:, c:c + P], rhs=ident_fwd[:],
                                      start=(opens and q == 0), stop=(not opens and q == 3), is_transpose=True)
 
-        share = 576
+        share = 640
         early = tile([P, TOKENS + share], F32, "early", 16384 + 1152)
         partial_1, partial_2g = early[:, 0:TOKENS], early[:, TOKENS:]
         nc.gpsimd.tensor_tensor(out=partial_1[:], in0=m_rows[1][:], in1=pa_win[1][:], op=ADD)

@@ -284,8 +284,8 @@ def tile_attend_gtied_mom_kernel(tc, V, dz, xT, G, mT, wT, offs, joffs, out_0, o
                     nc.tensor.matmul(turned[h][:, q * P:(q + 1) * P], lhsT=win[:, c:c + P], rhs=ident_fwd[:],
                                      start=(opens and q == 0), stop=(not opens and q == 3), is_transpose=True)
 
-        share = 640
-        early = tile([P, TOKENS + share], F32, "early", 16384 + 1152)
+        share = 448
+        early = tile([P, TOKENS + share], F32, "early", 16384 - 1920 - 4 * (TOKENS + share))
         partial_1, partial_2g = early[:, 0:TOKENS], early[:, TOKENS:]
         nc.gpsimd.tensor_tensor(out=partial_1[:], in0=m_rows[1][:], in1=pa_win[1][:], op=ADD)
         nc.gpsimd.tensor_tensor(out=partial_2g[:], in0=m_rows[2][:, 0:share], in1=pa_win[2][:, 0:share], op=ADD)

@@ -124,8 +124,8 @@ def tile_attend_gtied_mom_kernel(tc, V, dz, xT, G, mT, wT, offs, joffs, out_0, o
             else:
                 nc.scalar.activation(out=grad, in_=sums, func=COPY, scale=scale)
 
-        def scatter_scalar(win, lst, s0, s1, grad, scale=1.0):
-            nc.scalar.activation(out=win[:].indirect(lst[:, s0 // 16:s1 // 16]), in_=grad, func=COPY, scale=scale)
+        def scatter_scalar(win, lst, s0, s1, grad):
+            nc.scalar.activation(out=win[:].indirect(lst[:, s0 // 16:s1 // 16]), in_=grad, func=COPY)
 
         def scatter_vector(win, lst, s0, s1, grad):
             nc.vector.tensor_copy(win[:].indirect(lst[:, s0 // 16:s1 // 16]), grad)
@@ -177,7 +177,7 @@ def tile_attend_gtied_mom_kernel(tc, V, dz, xT, G, mT, wT, offs, joffs, out_0, o
         nc.scalar.copy(out=ident_fwd[:], in_=ident[:])
 
         pa_win = [window("pa_win_%d" % n, "vector") for n in range(3)]
-        pb_win = [window("pb_win_%d" % n, "vector" if n < 1 else "gpsimd") for n in range(3)]
+        pb_win = [window("pb_win_%d" % n, "vector" if n < 2 else "gpsimd") for n in range(3)]
         pa_win.append(pa_win[0])
         pb_win.append(pb_win[0])
 
@@ -241,7 +241,7 @@ def tile_attend_gtied_mom_kernel(tc, V, dz, xT, G, mT, wT, offs, joffs, out_0, o
         sums_b1 = product(x_01_mx, 1, g_mx, 2)
         v_23_woven = woven_tile("v_23_woven", 16384 + 4032)
         weave(v_23[:], "vector", v_23_woven[:])
-        x_23_woven = woven_tile("x_23_woven")
+        x_23_woven = woven_tile("x_23_woven", 53248)
         weave_x(turned_23, 2, "vector", x_23_woven)
         v_23_mx = mx_operand("v_23", HALF, 16384 + 64)
         quantise(v_23_woven[:], v_23_mx, 0, E4M3)
@@ -253,22 +253,16 @@ def tile_attend_gtied_mom_kernel(tc, V, dz, xT, G, mT, wT, offs, joffs, out_0, o
         drain("vector", sums_b1[:, 0:own], db_1v[:], 1.0)
         scatter_vector(pb_win[0], i_list, 0, SLOTS, db_0[:])
         scatter_vector(pb_win[1], i_list, 0, own, db_1v[:])
+        sums_a2 = product(v_23_mx, 0, dz_mx, 0)
+        sums_b2 = product(x_23_mx, 0, g_mx, 1)
 
-        grads_2 = tile([P, 4, HALF], F32, "grads_2")
-        sums = bank(0)
-        multiply(v_23_mx, 0, dz_mx, 0, HALF, sums[:, first])
-        drain("scalar", sums[:, first], grads_2[:, 0, :], 1.0)
-        scatter_scalar(pa_win[2], j_list, 0, HALF, grads_2[:, 0, :], 1.0 / DECAY)
-        sums = bank(1)
-        multiply(v_23_mx, 0, dz_mx, HALF, SLOTS, sums[:, first])
-        multiply(x_23_mx, 0, g_mx, 0, HALF, sums[:, second])
-        drain("scalar", sums[:], grads_2[:, 1:3, :].rearrange("p n s -> p (n s)"), 1.0)
-        sums = bank(6)
-        multiply(x_23_mx, 0, g_mx, HALF, SLOTS, sums[:, first])
-        drain("scalar", sums[:, first], grads_2[:, 3, :], 1.0)
-        scatter_scalar(pb_win[2], i_list, 0, HALF, grads_2[:, 2, :])
-        scatter_scalar(pa_win[2], j_list, HALF, SLOTS, grads_2[:, 1, :], 1.0 / DECAY)
-        scatter_scalar(pb_win[2], i_list, HALF, SLOTS, grads_2[:, 3, :])
+        da_2 = tile([P, SLOTS], F32, "da_2", 53248)
+        drain("scalar", sums_a2[:], da_2[:], 1.0 / DECAY)
+        db_2 = tile([P, SLOTS], F32, "db_2")
+        drain("scalar", sums_b2[:], db_2[:], 1.0)
+        for cols in (first, second):
+            scatter_scalar(pa_win[2], j_list, cols.start, cols.stop, da_2[:, cols])
+            scatter_scalar(pb_win[2], i_list, cols.start, cols.stop, db_2[:, cols])
         sums_y = bank(3)
         multiply(x_23_mx, 1, g_mx, 0, HALF, sums_y[:, first])
         multiply(v_23_mx, 1, dz_mx, 0, HALF, sums_y[:, second])
@@ -276,7 +270,7 @@ def tile_attend_gtied_mom_kernel(tc, V, dz, xT, G, mT, wT, offs, joffs, out_0, o
         sums_z = bank(5)
         multiply(x_23_mx, 1, g_mx, HALF, SLOTS, sums_z[:, first])
         multiply(v_23_mx, 1, dz_mx, HALF, SLOTS, sums_z[:, second])
-        turned = [bank(0), bank(4)]
+        turned = [bank(0), bank(1)]
         for win, opens in ((pa_win[0], True), (pb_win[0], False)):
             for h in range(2):
                 for q in range(4):

@@ -25,6 +25,7 @@ HALF = 256
 BLOCKS = D // P
 DECAY = 0.9
 RATE = 0.1
+SHARE = 640
 
 FLOPS = 2 * 2 * K * D * SLOTS
 
@@ -41,14 +42,20 @@ def tile_attend_gtied_mom_kernel(tc, V, dz, xT, G, mT, wT, offs, joffs, out_0, o
                 return keep.tile(shape, dtype, name=name, align_bytes=64)
             return reuse.tile(shape, dtype, name=name, offset=at, align_bytes=64)
 
-        def load_k_first(src, c0, c1, name, at=None):
-            raw = tile([P, PACK, c1 - c0], F32, name, at)
+        def load_k_first(src, c0, c1, name):
+            raw = tile([P, PACK, c1 - c0], F32, name)
             nc.sync.dma_start(out=raw[:], in_=src.rearrange("(p j) n -> p j n", j=PACK)[:, :, c0:c1])
             return raw
 
-        def load_rows(src, b, name, at=None):
-            raw = tile([P, src.shape[1]], F32, name, at)
+        def load_rows(src, b, name):
+            raw = tile([P, TOKENS], F32, name)
             nc.sync.dma_start(out=raw[:], in_=src[b * P:(b + 1) * P, :])
+            return raw
+
+        def load_x(pair):
+            raw = tile([P, 2, K], F32, "x_%d" % pair)
+            rows = xT[pair * HALF:(pair + 1) * HALF, :]
+            nc.sync.dma_start(out=raw[:], in_=rows.rearrange("(n d) r -> d n r", n=2))
             return raw
 
         def load_list(src, name):
@@ -56,14 +63,8 @@ def tile_attend_gtied_mom_kernel(tc, V, dz, xT, G, mT, wT, offs, joffs, out_0, o
             nc.sync.dma_start(lst[:], src)
             return lst
 
-        def copy(engine, dst, src):
-            if engine == "vector":
-                nc.vector.tensor_copy(out=dst, in_=src)
-            else:
-                nc.scalar.activation(out=dst, in_=src, func=COPY)
-
-        def window(name, engine, at=None):
-            win = tile([P, TOKENS], F32, name, at)
+        def window(name, engine):
+            win = tile([P, TOKENS], F32, name)
             if engine == "vector":
                 nc.vector.memset(win[:].bitcast(I32), 0)
             else:
@@ -73,10 +74,15 @@ def tile_attend_gtied_mom_kernel(tc, V, dz, xT, G, mT, wT, offs, joffs, out_0, o
         def mx_operand(name, width, at=None):
             return tile([P, width], U32, name + "_codes", at), tile([P, width], U8, name + "_scales")
 
-        def weave(raw, engine, woven):
-            dst = woven.rearrange("p (c i) t -> p c t i", i=4)
-            src = raw.rearrange("p t (c i) -> p c t i", i=4)
-            copy(engine, dst, src)
+        def weave(raw, engine, name, at=None):
+            woven = tile([P, raw.shape[2], PACK], BF16, name, at)
+            dst = woven[:].rearrange("p (c i) t -> p c t i", i=4)
+            src = raw[:].rearrange("p t (c i) -> p c t i", i=4)
+            if engine == "vector":
+                nc.vector.tensor_copy(out=dst, in_=src)
+            else:
+                nc.scalar.activation(out=dst, in_=src, func=COPY)
+            return woven
 
         def quantise(woven, operand, c0, fmt):
             codes, scales = operand
@@ -84,27 +90,27 @@ def tile_attend_gtied_mom_kernel(tc, V, dz, xT, G, mT, wT, offs, joffs, out_0, o
             nc.vector.quantize_mx(
                 out=codes[:, cols].bitcast(fmt),
                 scales=scales[:, cols],
-                in_=woven.rearrange("p n t -> p (n t)"),
+                in_=woven[:].rearrange("p n t -> p (n t)"),
             )
 
         def bank(n):
             return psum.tile([P, SLOTS], F32, name="bank_%d" % n, tag="bank_%d" % n)
 
-        def round_x(rows, engine, pairs):
-            copy(engine, pairs, rows[:].rearrange("d (p u e) -> d u p e", u=2, e=2))
+        def round_x(raw, name, at=None):
+            pairs = tile([P, 2, 2, P, 2], BF16, name, at)
+            nc.vector.tensor_copy(out=pairs[:], in_=raw[:].rearrange("d n (p u e) -> d n u p e", u=2, e=2))
+            return pairs
 
         def turn_x(pairs, turned):
             words = pairs[:].rearrange("d n u p e -> d (n u p e)").bitcast(F32)
-            for q in range(2 * pairs.shape[1]):
+            for q in range(4):
                 nc.tensor.transpose(turned[:, q * P:(q + 1) * P], words[:, q * P:(q + 1) * P], ident[:])
 
-        def weave_x(turned, n, engine, woven):
-            dst = woven[:].rearrange("p d t -> p (d t)").bitcast(F32).rearrange("p (n d u) -> p n d u", n=n, u=2)
-            src = turned[:, 0:n * HALF].rearrange("p (n u d) -> p n d u", n=n, u=2)
-            if engine == "vector":
-                nc.vector.tensor_copy(out=dst, in_=src)
-            else:
-                nc.scalar.copy(out=dst, in_=src)
+        def weave_x(turned, name):
+            woven = tile([P, HALF, PACK], BF16, name)
+            dst = woven[:].rearrange("p d t -> p (d t)").bitcast(F32).rearrange("p (n d u) -> p n d u", n=2, u=2)
+            nc.vector.tensor_copy(out=dst, in_=turned[:].rearrange("p (n u d) -> p n d u", n=2, u=2))
+            return woven
 
         def multiply(stationary, n, moving, c0, c1, sums):
             cols = slice(n * P, (n + 1) * P)
@@ -118,230 +124,183 @@ def tile_attend_gtied_mom_kernel(tc, V, dz, xT, G, mT, wT, offs, joffs, out_0, o
                 stop=True,
             )
 
-        def drain(engine, sums, grad, scale):
+        def drain(engine, sums, width, scale, name, at=None):
+            grad = tile([P, width], F32, name, at)
             if engine == "vector":
-                nc.vector.tensor_scalar(out=grad, in0=sums, scalar1=scale, scalar2=None, op0=MULT)
+                nc.vector.tensor_scalar(out=grad[:], in0=sums[:, 0:width], scalar1=scale, scalar2=None, op0=MULT)
             else:
-                nc.scalar.activation(out=grad, in_=sums, func=COPY, scale=scale)
+                nc.scalar.activation(out=grad[:], in_=sums[:, 0:width], func=COPY, scale=scale)
+            return grad
 
         def scatter_scalar(win, lst, s0, s1, grad):
             nc.scalar.activation(out=win[:].indirect(lst[:, s0 // 16:s1 // 16]), in_=grad, func=COPY)
 
-        def scatter_vector(win, lst, s0, s1, grad):
-            nc.vector.tensor_copy(win[:].indirect(lst[:, s0 // 16:s1 // 16]), grad)
+        def scale_add(dst, src, factor, other):
+            nc.vector.scalar_tensor_tensor(out=dst, in0=src, scalar=factor, in1=other, op0=MULT, op1=ADD)
 
-        halves = [slice(0, 512), slice(512, TOKENS)]
-        whole = [slice(0, TOKENS)]
-
-        def add_first(engine, m, win, both, pieces):
-            eng = nc.vector if engine == "vector" else nc.gpsimd
-            for cols in pieces:
-                eng.tensor_tensor(out=both[:, cols], in0=m[:, cols], in1=win[:, cols], op=ADD)
-            return both
-
-        def scale_add(dst, src, factor, other, pieces):
-            for cols in pieces:
-                nc.vector.scalar_tensor_tensor(
-                    out=dst[:, cols], in0=src[:, cols], scalar=factor, in1=other[:, cols], op0=MULT, op1=ADD
-                )
-
-        def store(dst, b, src, pieces):
-            for cols in pieces:
-                nc.sync.dma_start(out=dst[b * P:(b + 1) * P, cols], in_=src[:, cols])
-
-        m_rows, w_rows = {}, {}
-
-        def load_x(pair):
-            raw = tile([P, 2, K], F32, "x_%d" % pair)
-            rows = xT[pair * HALF:(pair + 1) * HALF, :]
-            nc.sync.dma_start(out=raw[:], in_=rows.rearrange("(n d) r -> d n r", n=2))
-            return raw
+        def store(dst, b, src, cols):
+            nc.sync.dma_start(out=dst[b * P:(b + 1) * P, cols], in_=src[:, cols])
 
         v_01 = load_k_first(V, 0, HALF, "v_01")
-        dz_a = load_k_first(dz, 0, HALF, "dz_a")
+        dz_parts = [(0, P), (P, HALF), (HALF, SLOTS)]
+        dz_raw = [load_k_first(dz, 0, P, "dz_0")]
         j_list = load_list(joffs, "j_list")
-        dz_b = load_k_first(dz, HALF, SLOTS, "dz_b")
-        x_raw = [load_x(0)]
-        g_a = load_k_first(G, 0, HALF, "g_a")
-        g_b = load_k_first(G, HALF, SLOTS, "g_b", 16384 + 1984)
+        dz_raw.extend(load_k_first(dz, c0, c1, "dz_%d" % c0) for c0, c1 in dz_parts[1:])
+        v_23 = load_k_first(V, HALF, D, "v_23")
+        x_raw = [load_x(0), load_x(1)]
+        g_raw = load_k_first(G, 0, SLOTS, "g")
         i_list = load_list(offs, "i_list")
-        x_raw.append(load_x(1))
-        v_23 = load_k_first(V, HALF, SLOTS, "v_23")
-        for rows, src, name, b in ((m_rows, mT, "m", 1), (m_rows, mT, "m", 0), (m_rows, mT, "m", 2), (w_rows, wT, "w", 0),
-                                   (w_rows, wT, "w", 2), (w_rows, wT, "w", 1), (m_rows, mT, "m", 3), (w_rows, wT, "w", 3)):
+        m_rows, w_rows = {}, {}
+        for rows, src, name, b in ((m_rows, mT, "m", 0), (m_rows, mT, "m", 2), (m_rows, mT, "m", 1), (w_rows, wT, "w", 0),
+                                   (m_rows, mT, "m", 3), (w_rows, wT, "w", 1), (w_rows, wT, "w", 2), (w_rows, wT, "w", 3)):
             rows[b] = load_rows(src, b, "%s_%d" % (name, b))
 
         ident = keep.tile([P, P], F32, name="ident")
         make_identity(nc, ident[:])
-        ident_fwd = tile([P, P], F32, "ident_fwd", 61440)
+        ident_fwd = tile([P, P], F32, "ident_fwd", 28672)
         nc.scalar.copy(out=ident_fwd[:], in_=ident[:])
 
-        pa_win = [window("pa_win_%d" % n, "vector") for n in range(3)]
-        pb_win = [window("pb_win_%d" % n, "vector" if n < 2 else "gpsimd") for n in range(3)]
-        pa_win.append(pa_win[0])
+        pa_win = [window("pa_win_%d" % n, "vector") for n in range(4)]
+        pb_win = [window("pb_win_%d" % n, "vector") for n in range(3)]
         pb_win.append(pb_win[0])
 
         dz_mx = mx_operand("dz", SLOTS)
-        v_01_mx, x_01_mx, x_23_mx = [mx_operand(n, HALF) for n in ("v_01", "x_01", "x_23")]
+        v_01_mx, v_23_mx, x_01_mx, x_23_mx = [mx_operand(n, HALF) for n in ("v_01", "v_23", "x_01", "x_23")]
+        g_mx = mx_operand("g", SLOTS, 8192)
         first, second = slice(0, HALF), slice(HALF, SLOTS)
+        halves = [slice(0, 512), slice(512, TOKENS)]
 
-        def first_pair(h, banks):
-            grads = tile([P, 2, HALF], F32, "da_01_%d" % h)
+        def pair_products(part, n_bank):
+            c0, c1 = dz_parts[part]
+            sums = bank(n_bank)
             for b in range(2):
-                sums = bank(banks[b])[:, first]
-                multiply(v_01_mx, b, dz_mx, h * HALF, (h + 1) * HALF, sums)
-                drain("scalar", sums, grads[:, b, :], (1.0, 1.0 / DECAY)[b])
+                multiply(v_01_mx, b, dz_mx, c0, c1, sums[:, b * (c1 - c0):(b + 1) * (c1 - c0)])
+            return sums
+
+        def pair_scatters(part, sums):
+            c0, c1 = dz_parts[part]
+            width = c1 - c0
+            grads = drain("vector", sums, 2 * width, 1.0 / DECAY, "da_01_%d" % part)
             for b in range(2):
-                scatter_scalar(pa_win[b], j_list, h * HALF, (h + 1) * HALF, grads[:, b, :])
+                scatter_scalar(pa_win[b], j_list, c0, c1, grads[:, b * width:(b + 1) * width])
 
         def product(stationary, n, moving, n_bank):
             sums = bank(n_bank)
             multiply(stationary, n, moving, 0, SLOTS, sums[:])
             return sums
 
-        def woven_tile(name, at=None, width=HALF):
-            return tile([P, width, PACK], BF16, name, at)
-
-        def round_pair(raw, pairs):
-            nc.vector.tensor_copy(out=pairs[:], in_=raw[:].rearrange("d n (p u e) -> d n u p e", u=2, e=2))
-
-        pair_words = [P, 2, 2, P, 2]
-        v_01_woven = woven_tile("v_01_woven")
-        weave(v_01[:], "scalar", v_01_woven[:])
-        dz_a_woven = woven_tile("dz_a_woven")
-        weave(dz_a[:, :, 0:192], "vector", dz_a_woven[:, 0:192, :])
-        weave(dz_a[:, :, 192:], "scalar", dz_a_woven[:, 192:, :])
-        quantise(v_01_woven[:], v_01_mx, 0, E4M3)
-        quantise(dz_a_woven[:], dz_mx, 0, E5M2)
-        dz_b_woven = woven_tile("dz_b_woven")
-        weave(dz_b[:, :, 0:P], "vector", dz_b_woven[:, 0:P, :])
-        weave(dz_b[:, :, P:], "scalar", dz_b_woven[:, P:, :])
-        first_pair(0, (0, 1))
-        x_01_pairs = tile(pair_words, BF16, "x_01_pairs", 4096)
-        round_pair(x_raw[0], x_01_pairs)
-        quantise(dz_b_woven[:], dz_mx, HALF, E5M2)
-        turned_01 = bank(4)
-        turn_x(x_01_pairs, turned_01)
-        first_pair(1, (2, 3))
-        g_a_woven = woven_tile("g_a_woven")
-        weave(g_a[:], "vector", g_a_woven[:])
-        x_01_woven = woven_tile("x_01_woven")
-        weave_x(turned_01, 2, "vector", x_01_woven)
-        g_b_woven = woven_tile("g_b_woven", 3072)
-        weave(g_b[:], "vector", g_b_woven[:])
-        g_mx = mx_operand("g", SLOTS, 5120)
-        quantise(g_a_woven[:], g_mx, 0, E5M2)
-        x_23_pairs = tile(pair_words, BF16, "x_23_pairs", 16384)
-        round_pair(x_raw[1], x_23_pairs)
-        turned_23 = bank(5)
-        turn_x(x_23_pairs, turned_23)
-        quantise(x_01_woven[:], x_01_mx, 0, E4M3)
-        quantise(g_b_woven[:], g_mx, HALF, E5M2)
-        sums_b0 = product(x_01_mx, 0, g_mx, 4)
-        sums_b1 = product(x_01_mx, 1, g_mx, 2)
-        v_23_woven = woven_tile("v_23_woven", 16384 + 4032)
-        weave(v_23[:], "vector", v_23_woven[:])
-        x_23_woven = woven_tile("x_23_woven", 53248)
-        weave_x(turned_23, 2, "vector", x_23_woven)
-        v_23_mx = mx_operand("v_23", HALF, 16384 + 64)
-        quantise(v_23_woven[:], v_23_mx, 0, E4M3)
-        db_0 = tile([P, SLOTS], F32, "db_0", 16384 - 1984)
-        drain("vector", sums_b0[:], db_0[:], 1.0)
-        quantise(x_23_woven[:], x_23_mx, 0, E4M3)
-        own = 288
-        db_1v = tile([P, own], F32, "db_1v", 16384 + 1088)
-        drain("vector", sums_b1[:, 0:own], db_1v[:], 1.0)
-        scatter_vector(pb_win[0], i_list, 0, SLOTS, db_0[:])
-        scatter_vector(pb_win[1], i_list, 0, own, db_1v[:])
+        v_01_woven = weave(v_01, "scalar", "v_01_woven")
+        dz_woven = weave(dz_raw[0], "vector", "dz_0_woven")
+        quantise(v_01_woven, v_01_mx, 0, E4M3)
+        quantise(dz_woven, dz_mx, 0, E5M2)
+        sums = pair_products(0, 0)
+        dz_woven = weave(dz_raw[1], "vector", "dz_1_woven")
+        pair_scatters(0, sums)
+        quantise(dz_woven, dz_mx, P, E5M2)
+        sums = pair_products(1, 1)
+        dz_woven = weave(dz_raw[2], "vector", "dz_2_woven")
+        pair_scatters(1, sums)
+        quantise(dz_woven, dz_mx, HALF, E5M2)
+        sums = pair_products(2, 2)
+        v_23_woven = weave(v_23, "vector", "v_23_woven")
+        pair_scatters(2, sums)
+        quantise(v_23_woven, v_23_mx, 0, E4M3)
         sums_a2 = product(v_23_mx, 0, dz_mx, 0)
-        sums_b2 = product(x_23_mx, 0, g_mx, 1)
-
-        da_2 = tile([P, SLOTS], F32, "da_2", 53248)
-        drain("scalar", sums_a2[:], da_2[:], 1.0 / DECAY)
-        db_2 = tile([P, SLOTS], F32, "db_2")
-        drain("scalar", sums_b2[:], db_2[:], 1.0)
+        sums_a3 = product(v_23_mx, 1, dz_mx, 1)
+        x_01_pairs = round_x(x_raw[0], "x_01_pairs", 0)
+        turned_01 = bank(3)
+        turn_x(x_01_pairs, turned_01)
+        da_2 = drain("vector", sums_a2, SLOTS, 1.0 / DECAY, "da_2")
+        x_23_pairs = round_x(x_raw[1], "x_23_pairs")
+        turned_23 = bank(4)
+        turn_x(x_23_pairs, turned_23)
+        da_3 = drain("vector", sums_a3, SLOTS, 1.0 / DECAY, "da_3")
         for cols in (first, second):
             scatter_scalar(pa_win[2], j_list, cols.start, cols.stop, da_2[:, cols])
-            scatter_scalar(pb_win[2], i_list, cols.start, cols.stop, db_2[:, cols])
-        sums_y = bank(3)
-        multiply(x_23_mx, 1, g_mx, 0, HALF, sums_y[:, first])
-        multiply(v_23_mx, 1, dz_mx, 0, HALF, sums_y[:, second])
+            scatter_scalar(pa_win[3], j_list, cols.start, cols.stop, da_3[:, cols])
+        x_01_woven = weave_x(turned_01, "x_01_woven")
+        g_woven = weave(g_raw, "vector", "g_woven", 1984)
+        quantise(x_01_woven, x_01_mx, 0, E4M3)
+        quantise(g_woven, g_mx, 0, E5M2)
+        sums_b0 = product(x_01_mx, 0, g_mx, 1)
+        x_23_woven = weave_x(turned_23, "x_23_woven")
+        quantise(x_23_woven, x_23_mx, 0, E4M3)
+        db_0 = drain("vector", sums_b0, SLOTS, 1.0 / DECAY, "db_0", 16384)
 
-        sums_z = bank(5)
-        multiply(x_23_mx, 1, g_mx, HALF, SLOTS, sums_z[:, first])
-        multiply(v_23_mx, 1, dz_mx, HALF, SLOTS, sums_z[:, second])
-        turned = [bank(0), bank(1)]
-        for win, opens in ((pa_win[0], True), (pb_win[0], False)):
+        def pieces(n_bank, parts):
+            sums = bank(n_bank)
+            at = 0
+            for b, c0, c1 in parts:
+                multiply((x_01_mx, x_23_mx)[b // 2], b % 2, g_mx, c0, c1, sums[:, at:at + c1 - c0])
+                at = at + c1 - c0
+            return sums
+
+        sums_x = pieces(2, [(1, 0, HALF), (2, 0, HALF)])
+        sums_y = pieces(4, [(1, HALF, SLOTS), (3, 0, P)])
+        sums_z = pieces(5, [(2, HALF, SLOTS)])
+        sums_w = pieces(6, [(3, P, HALF), (3, HALF, SLOTS)])
+        db_x = drain("vector", sums_x, SLOTS, 1.0, "db_x")
+        nc.vector.tensor_copy(pb_win[0][:].indirect(i_list[:]), db_0[:])
+        scatter_scalar(pb_win[1], i_list, 0, HALF, db_x[:, first])
+        scatter_scalar(pb_win[2], i_list, 0, HALF, db_x[:, second])
+
+        turned = [bank(3), bank(0)]
+        for n, addend in enumerate((pa_win[0], m_rows[0], pb_win[0])):
             for h in range(2):
                 for q in range(4):
                     c = (4 * h + q) * P
-                    nc.tensor.matmul(turned[h][:, q * P:(q + 1) * P], lhsT=win[:, c:c + P], rhs=ident_fwd[:],
-                                     start=(opens and q == 0), stop=(not opens and q == 3), is_transpose=True)
+                    nc.tensor.matmul(turned[h][:, q * P:(q + 1) * P], lhsT=addend[:, c:c + P], rhs=ident_fwd[:],
+                                     start=(n == 0 and q == 0), stop=(n == 2 and q == 3), is_transpose=True)
 
-        share = 448
-        early = tile([P, TOKENS + share], F32, "early", 16384 - 1920 - 4 * (TOKENS + share))
-        partial_1, partial_2g = early[:, 0:TOKENS], early[:, TOKENS:]
+        by_gpsimd, by_vector = slice(0, SHARE), slice(SHARE, TOKENS)
+        partial_2v = tile([P, TOKENS - SHARE], F32, "partial_2v", 8192 + 1984)
+        nc.vector.tensor_tensor(out=partial_2v[:], in0=m_rows[2][:, by_vector], in1=pa_win[2][:, by_vector], op=ADD)
+        partial_1 = tile([P, TOKENS], F32, "partial_1", 16384 + 1984)
         nc.gpsimd.tensor_tensor(out=partial_1[:], in0=m_rows[1][:], in1=pa_win[1][:], op=ADD)
-        nc.gpsimd.tensor_tensor(out=partial_2g[:], in0=m_rows[2][:, 0:share], in1=pa_win[2][:, 0:share], op=ADD)
+        partial_2g = tile([P, SHARE], F32, "partial_2g", 16384 + 64 - 4 * SHARE)
+        nc.gpsimd.tensor_tensor(out=partial_2g[:], in0=m_rows[2][:, by_gpsimd], in1=pa_win[2][:, by_gpsimd], op=ADD)
 
-        both_t = [tile([P, SLOTS], F32, "both_t_%d" % h, (None, 36864)[h]) for h in range(2)]
-        for h in range(2):
-            nc.vector.tensor_copy(out=both_t[h][:], in_=turned[h][:])
-        new_m = [tile([P, TOKENS], F32, "new_m_%d" % b, (None, None, 36864 + 1984, None)[b]) for b in range(BLOCKS)]
+        db_y = drain("vector", sums_y, HALF + P, 1.0, "db_y")
+        new_m_t = [drain("vector", turned[h], SLOTS, DECAY, "new_m_t_%d" % h, (None, 40960)[h]) for h in range(2)]
+        db_z = drain("vector", sums_z, HALF, 1.0, "db_z", 28672 + 448)
+        db_w = drain("vector", sums_w, HALF + P, 1.0, "db_w", 28672 + 64 - 4 * (HALF + P))
+        scatter_scalar(pb_win[1], i_list, HALF, SLOTS, db_y[:, first])
+        scatter_scalar(pb_win[3], i_list, 0, P, db_y[:, HALF:])
+        scatter_scalar(pb_win[2], i_list, HALF, SLOTS, db_z[:])
+        scatter_scalar(pb_win[3], i_list, P, SLOTS, db_w[:])
+
+        places = (None, 40960 + 1984, 16384 + 1984 + 4032, None)
+        new_m = [tile([P, TOKENS], F32, "new_m_%d" % b, places[b]) for b in range(BLOCKS)]
         new_w = [tile([P, TOKENS], F32, "new_w_%d" % b) for b in range(BLOCKS)]
 
-        def turn_back(h):
-            both = bank(6 + h)
-            for q in range(4):
-                nc.tensor.transpose(both[:, q * P:(q + 1) * P], both_t[h][:, q * P:(q + 1) * P], ident[:])
-            return both
-
-        def momentum_0(h, both):
-            nc.vector.scalar_tensor_tensor(
-                out=new_m[0][:, halves[h]], in0=m_rows[0][:, halves[h]], scalar=DECAY, in1=both[:], op0=MULT, op1=ADD
-            )
-
-        db_1s = tile([P, SLOTS - own], F32, "db_1s", 61440 + 64)
-        drain("vector", sums_b1[:, own:], db_1s[:], 1.0)
-        grads_3 = tile([P, 2, SLOTS], F32, "grads_3", 61440 + 64 - 4096)
-        grads_y, grads_z = grads_3[:, 0, :], grads_3[:, 1, :]
-        drain("vector", sums_y[:], grads_y, 1.0)
-        drain("vector", sums_z[:], grads_z, 1.0)
         for h in range(2):
-            momentum_0(h, turn_back(h))
-            store(out_0, 0, new_m[0], halves[h:h + 1])
+            back = bank(1 + h)
+            for q in range(4):
+                nc.tensor.transpose(back[:, q * P:(q + 1) * P], new_m_t[h][:, q * P:(q + 1) * P], ident[:])
+            nc.vector.tensor_copy(out=new_m[0][:, halves[h]], in_=back[:])
+            store(out_0, 0, new_m[0], halves[h])
+            scale_add(new_w[0][:, halves[h]], back[:], -RATE, w_rows[0][:, halves[h]])
+            store(out_1, 0, new_w[0], halves[h])
 
-        scatter_scalar(pb_win[1], i_list, own, SLOTS, db_1s[:])
-        scatter_scalar(pa_win[3], j_list, 0, HALF, grads_y[:, second])
-        scatter_scalar(pb_win[3], i_list, 0, HALF, grads_y[:, first])
-        scatter_scalar(pa_win[3], j_list, HALF, SLOTS, grads_z[:, second])
-        scatter_scalar(pb_win[3], i_list, HALF, SLOTS, grads_z[:, first])
+        partial_3 = tile([P, TOKENS], F32, "partial_3", 40960 + 64 - 4096)
+        nc.vector.tensor_tensor(out=partial_3[:], in0=m_rows[3][:], in1=pa_win[3][:], op=ADD)
+        for cols in halves:
+            scale_add(new_m[1][:, cols], partial_1[:, cols], DECAY, pb_win[1][:, cols])
+            store(out_0, 1, new_m[1], cols)
+        for cols in halves:
+            scale_add(new_w[1][:, cols], new_m[1][:, cols], -RATE, w_rows[1][:, cols])
+            store(out_1, 1, new_w[1], cols)
 
-        def table(b, pieces, stores):
-            for cols in stores:
-                scale_add(new_w[b], new_m[b], -RATE, w_rows[b], [c for c in pieces if cols.start <= c.start < cols.stop])
-                store(out_1, b, new_w[b], [cols])
+        for cols, part in ((by_gpsimd, partial_2g), (by_vector, partial_2v)):
+            scale_add(new_m[2][:, cols], part[:], DECAY, pb_win[2][:, cols])
+            store(out_0, 2, new_m[2], cols)
+        for cols in (by_gpsimd, by_vector):
+            scale_add(new_w[2][:, cols], new_m[2][:, cols], -RATE, w_rows[2][:, cols])
+            store(out_1, 2, new_w[2], cols)
 
-        def momentum_2(part, cols):
-            nc.vector.scalar_tensor_tensor(
-                out=new_m[2][:, cols], in0=part, scalar=DECAY, in1=pb_win[2][:, cols], op0=MULT, op1=ADD
-            )
-
-        by_gpsimd, by_vector = slice(0, share), slice(share, TOKENS)
-        partial_2v = tile([P, TOKENS - share], F32, "partial_2v", 36864 + 64 - 4 * (TOKENS - share))
-        nc.vector.tensor_tensor(out=partial_2v[:], in0=m_rows[2][:, by_vector], in1=pa_win[2][:, by_vector], op=ADD)
-        table(0, whole, whole)
-        momentum_2(partial_2g, by_gpsimd)
-        momentum_2(partial_2v[:], by_vector)
-        store(out_0, 2, new_m[2], whole)
-        scale_add(new_m[1], partial_1, DECAY, pb_win[1], whole)
-        store(out_0, 1, new_m[1], whole)
-        table(2, whole, whole)
-        table(1, whole, whole)
-        partial_3 = tile([P, TOKENS], F32, "partial_3", 36864 + 64)
-        scale_add(partial_3, m_rows[3], DECAY, pa_win[3], halves)
         for cols in (slice(0, 256), slice(256, 512), slice(512, TOKENS)):
-            nc.vector.tensor_tensor(out=new_m[3][:, cols], in0=partial_3[:, cols], in1=pb_win[3][:, cols], op=ADD)
-            store(out_0, 3, new_m[3], [cols])
-        last = [slice(0, 512), slice(512, 768), slice(768, TOKENS)]
-        table(3, last, last)
+            scale_add(new_m[3][:, cols], partial_3[:, cols], DECAY, pb_win[3][:, cols])
+            store(out_0, 3, new_m[3], cols)
+        for cols in (slice(0, 512), slice(512, 768), slice(768, TOKENS)):
+            scale_add(new_w[3][:, cols], new_m[3][:, cols], -RATE, w_rows[3][:, cols])
+            store(out_1, 3, new_w[3], cols)

@@ -25,7 +25,7 @@ HALF = 256
 BLOCKS = D // P
 DECAY = 0.9
 RATE = 0.1
-SHARE = 640
+SHARE = 384
 
 FLOPS = 2 * 2 * K * D * SLOTS
 
@@ -77,7 +77,7 @@ def tile_attend_gtied_mom_kernel(tc, V, dz, xT, G, mT, wT, offs, joffs, out_0, o
         def weave(raw, engine, name, at=None):
             woven = tile([P, raw.shape[2], PACK], BF16, name, at)
             dst = woven[:].rearrange("p (c i) t -> p c t i", i=4)
-            src = raw[:].rearrange("p t (c i) -> p c t i", i=4)
+            src = raw.rearrange("p t (c i) -> p c t i", i=4)
             if engine == "vector":
                 nc.vector.tensor_copy(out=dst, in_=src)
             else:
@@ -143,16 +143,16 @@ def tile_attend_gtied_mom_kernel(tc, V, dz, xT, G, mT, wT, offs, joffs, out_0, o
 
         v_01 = load_k_first(V, 0, HALF, "v_01")
         dz_parts = [(0, P), (P, HALF), (HALF, SLOTS)]
-        dz_raw = [load_k_first(dz, 0, P, "dz_0")]
+        dz_first = load_k_first(dz, 0, P, "dz_first")
         j_list = load_list(joffs, "j_list")
-        dz_raw.extend(load_k_first(dz, c0, c1, "dz_%d" % c0) for c0, c1 in dz_parts[1:])
+        dz_rest = load_k_first(dz, P, SLOTS, "dz_rest")
         v_23 = load_k_first(V, HALF, D, "v_23")
         x_raw = [load_x(0), load_x(1)]
         g_raw = load_k_first(G, 0, SLOTS, "g")
         i_list = load_list(offs, "i_list")
         m_rows, w_rows = {}, {}
-        for rows, src, name, b in ((m_rows, mT, "m", 0), (m_rows, mT, "m", 2), (m_rows, mT, "m", 1), (w_rows, wT, "w", 0),
-                                   (m_rows, mT, "m", 3), (w_rows, wT, "w", 1), (w_rows, wT, "w", 2), (w_rows, wT, "w", 3)):
+        for rows, src, name, b in ((m_rows, mT, "m", 0), (m_rows, mT, "m", 2), (m_rows, mT, "m", 1), (m_rows, mT, "m", 3),
+                                   (w_rows, wT, "w", 0), (w_rows, wT, "w", 1), (w_rows, wT, "w", 2), (w_rows, wT, "w", 3)):
             rows[b] = load_rows(src, b, "%s_%d" % (name, b))
 
         ident = keep.tile([P, P], F32, name="ident")
@@ -177,10 +177,10 @@ def tile_attend_gtied_mom_kernel(tc, V, dz, xT, G, mT, wT, offs, joffs, out_0, o
                 multiply(v_01_mx, b, dz_mx, c0, c1, sums[:, b * (c1 - c0):(b + 1) * (c1 - c0)])
             return sums
 
-        def pair_scatters(part, sums):
+        def pair_scatters(part, sums, engine):
             c0, c1 = dz_parts[part]
             width = c1 - c0
-            grads = drain("vector", sums, 2 * width, 1.0 / DECAY, "da_01_%d" % part)
+            grads = drain(engine, sums, 2 * width, 1.0 / DECAY, "da_01_%d" % part)
             for b in range(2):
                 scatter_scalar(pa_win[b], j_list, c0, c1, grads[:, b * width:(b + 1) * width])
 
@@ -189,22 +189,21 @@ def tile_attend_gtied_mom_kernel(tc, V, dz, xT, G, mT, wT, offs, joffs, out_0, o
             multiply(stationary, n, moving, 0, SLOTS, sums[:])
             return sums
 
-        v_01_woven = weave(v_01, "scalar", "v_01_woven")
-        dz_woven = weave(dz_raw[0], "vector", "dz_0_woven")
+        v_01_woven = weave(v_01[:], "scalar", "v_01_woven")
+        dz_woven = [weave(dz_first[:], "vector", "dz_0_woven")]
         quantise(v_01_woven, v_01_mx, 0, E4M3)
-        quantise(dz_woven, dz_mx, 0, E5M2)
-        sums = pair_products(0, 0)
-        dz_woven = weave(dz_raw[1], "vector", "dz_1_woven")
-        pair_scatters(0, sums)
-        quantise(dz_woven, dz_mx, P, E5M2)
-        sums = pair_products(1, 1)
-        dz_woven = weave(dz_raw[2], "vector", "dz_2_woven")
-        pair_scatters(1, sums)
-        quantise(dz_woven, dz_mx, HALF, E5M2)
-        sums = pair_products(2, 2)
-        v_23_woven = weave(v_23, "vector", "v_23_woven")
-        pair_scatters(2, sums)
+        quantise(dz_woven[0], dz_mx, 0, E5M2)
+        pair_scatters(0, pair_products(0, 0), "scalar")
+        dz_woven.append(weave(dz_rest[:, :, 0:P], "vector", "dz_1_woven", 49152))
+        dz_woven.append(weave(dz_rest[:, :, P:], "vector", "dz_2_woven"))
+        quantise(dz_woven[1], dz_mx, P, E5M2)
+        sums_1 = pair_products(1, 1)
+        quantise(dz_woven[2], dz_mx, HALF, E5M2)
+        sums_2 = pair_products(2, 2)
+        v_23_woven = weave(v_23[:], "vector", "v_23_woven", 49152 + 960)
+        pair_scatters(1, sums_1, "vector")
         quantise(v_23_woven, v_23_mx, 0, E4M3)
+        pair_scatters(2, sums_2, "vector")
         sums_a2 = product(v_23_mx, 0, dz_mx, 0)
         sums_a3 = product(v_23_mx, 1, dz_mx, 1)
         x_01_pairs = round_x(x_raw[0], "x_01_pairs", 0)
@@ -219,7 +218,7 @@ def tile_attend_gtied_mom_kernel(tc, V, dz, xT, G, mT, wT, offs, joffs, out_0, o
             scatter_scalar(pa_win[2], j_list, cols.start, cols.stop, da_2[:, cols])
             scatter_scalar(pa_win[3], j_list, cols.start, cols.stop, da_3[:, cols])
         x_01_woven = weave_x(turned_01, "x_01_woven")
-        g_woven = weave(g_raw, "vector", "g_woven", 1984)
+        g_woven = weave(g_raw[:], "vector", "g_woven", 1984)
         quantise(x_01_woven, x_01_mx, 0, E4M3)
         quantise(g_woven, g_mx, 0, E5M2)
         sums_b0 = product(x_01_mx, 0, g_mx, 1)
@@ -235,14 +234,13 @@ def tile_attend_gtied_mom_kernel(tc, V, dz, xT, G, mT, wT, offs, joffs, out_0, o
                 at = at + c1 - c0
             return sums
 
-        sums_x = pieces(2, [(1, 0, HALF), (2, 0, HALF)])
-        sums_y = pieces(4, [(1, HALF, SLOTS), (3, 0, P)])
-        sums_z = pieces(5, [(2, HALF, SLOTS)])
+        sums_x = pieces(2, [(1, 0, HALF)])
+        sums_y = pieces(4, [(2, 0, P), (1, HALF, SLOTS)])
+        sums_z = pieces(5, [(3, 0, P), (2, P, HALF), (2, HALF, SLOTS)])
         sums_w = pieces(6, [(3, P, HALF), (3, HALF, SLOTS)])
-        db_x = drain("vector", sums_x, SLOTS, 1.0, "db_x")
+        db_x = drain("vector", sums_x, HALF, 1.0, "db_x")
         nc.vector.tensor_copy(pb_win[0][:].indirect(i_list[:]), db_0[:])
-        scatter_scalar(pb_win[1], i_list, 0, HALF, db_x[:, first])
-        scatter_scalar(pb_win[2], i_list, 0, HALF, db_x[:, second])
+        scatter_scalar(pb_win[1], i_list, 0, HALF, db_x[:])
 
         turned = [bank(3), bank(0)]
         for n, addend in enumerate((pa_win[0], m_rows[0], pb_win[0])):
@@ -257,16 +255,20 @@ def tile_attend_gtied_mom_kernel(tc, V, dz, xT, G, mT, wT, offs, joffs, out_0, o
         nc.vector.tensor_tensor(out=partial_2v[:], in0=m_rows[2][:, by_vector], in1=pa_win[2][:, by_vector], op=ADD)
         partial_1 = tile([P, TOKENS], F32, "partial_1", 16384 + 1984)
         nc.gpsimd.tensor_tensor(out=partial_1[:], in0=m_rows[1][:], in1=pa_win[1][:], op=ADD)
-        partial_2g = tile([P, SHARE], F32, "partial_2g", 16384 + 64 - 4 * SHARE)
-        nc.gpsimd.tensor_tensor(out=partial_2g[:], in0=m_rows[2][:, by_gpsimd], in1=pa_win[2][:, by_gpsimd], op=ADD)
+        partial_g = tile([P, 2, SHARE], F32, "partial_g", 16384 + 64 - 8 * SHARE)
+        for b in (2, 3):
+            nc.gpsimd.tensor_tensor(
+                out=partial_g[:, b - 2, :], in0=m_rows[b][:, by_gpsimd], in1=pa_win[b][:, by_gpsimd], op=ADD
+            )
 
-        db_y = drain("vector", sums_y, HALF + P, 1.0, "db_y")
+        db_y = drain("vector", sums_y, P + HALF, 1.0, "db_y")
+        scatter_scalar(pb_win[2], i_list, 0, P, db_y[:, 0:P])
+        scatter_scalar(pb_win[1], i_list, HALF, SLOTS, db_y[:, P:])
         new_m_t = [drain("vector", turned[h], SLOTS, DECAY, "new_m_t_%d" % h, (None, 40960)[h]) for h in range(2)]
-        db_z = drain("vector", sums_z, HALF, 1.0, "db_z", 28672 + 448)
-        db_w = drain("vector", sums_w, HALF + P, 1.0, "db_w", 28672 + 64 - 4 * (HALF + P))
-        scatter_scalar(pb_win[1], i_list, HALF, SLOTS, db_y[:, first])
-        scatter_scalar(pb_win[3], i_list, 0, P, db_y[:, HALF:])
-        scatter_scalar(pb_win[2], i_list, HALF, SLOTS, db_z[:])
+        db_z = drain("vector", sums_z, SLOTS, 1.0, "db_z", 28672 + 448)
+        db_w = drain("vector", sums_w, P + HALF, 1.0, "db_w", 28672 + 64 - 4 * (P + HALF))
+        scatter_scalar(pb_win[3], i_list, 0, P, db_z[:, 0:P])
+        scatter_scalar(pb_win[2], i_list, P, SLOTS, db_z[:, P:])
         scatter_scalar(pb_win[3], i_list, P, SLOTS, db_w[:])
 
         places = (None, 40960 + 1984, 16384 + 1984 + 4032, None)
@@ -282,25 +284,26 @@ def tile_attend_gtied_mom_kernel(tc, V, dz, xT, G, mT, wT, offs, joffs, out_0, o
             scale_add(new_w[0][:, halves[h]], back[:], -RATE, w_rows[0][:, halves[h]])
             store(out_1, 0, new_w[0], halves[h])
 
-        partial_3 = tile([P, TOKENS], F32, "partial_3", 40960 + 64 - 4096)
-        nc.vector.tensor_tensor(out=partial_3[:], in0=m_rows[3][:], in1=pa_win[3][:], op=ADD)
+        whole = slice(0, TOKENS)
         for cols in halves:
             scale_add(new_m[1][:, cols], partial_1[:, cols], DECAY, pb_win[1][:, cols])
             store(out_0, 1, new_m[1], cols)
         for cols in halves:
             scale_add(new_w[1][:, cols], new_m[1][:, cols], -RATE, w_rows[1][:, cols])
-            store(out_1, 1, new_w[1], cols)
+        store(out_1, 1, new_w[1], whole)
 
-        for cols, part in ((by_gpsimd, partial_2g), (by_vector, partial_2v)):
-            scale_add(new_m[2][:, cols], part[:], DECAY, pb_win[2][:, cols])
-            store(out_0, 2, new_m[2], cols)
+        for cols, part in ((by_gpsimd, partial_g[:, 0, :]), (by_vector, partial_2v[:])):
+            scale_add(new_m[2][:, cols], part, DECAY, pb_win[2][:, cols])
+        store(out_0, 2, new_m[2], whole)
         for cols in (by_gpsimd, by_vector):
             scale_add(new_w[2][:, cols], new_m[2][:, cols], -RATE, w_rows[2][:, cols])
-            store(out_1, 2, new_w[2], cols)
+        store(out_1, 2, new_w[2], whole)
 
-        for cols in (slice(0, 256), slice(256, 512), slice(512, TOKENS)):
-            scale_add(new_m[3][:, cols], partial_3[:, cols], DECAY, pb_win[3][:, cols])
+        partial_3v = tile([P, TOKENS - SHARE], F32, "partial_3v", 40960 + 64 - 4 * (TOKENS - SHARE))
+        nc.vector.tensor_tensor(out=partial_3v[:], in0=m_rows[3][:, by_vector], in1=pa_win[3][:, by_vector], op=ADD)
+        for cols, part in ((by_gpsimd, partial_g[:, 1, :]), (by_vector, partial_3v[:])):
+            scale_add(new_m[3][:, cols], part, DECAY, pb_win[3][:, cols])
             store(out_0, 3, new_m[3], cols)
-        for cols in (slice(0, 512), slice(512, 768), slice(768, TOKENS)):
+        for cols in (by_gpsimd, slice(SHARE, 768), slice(768, TOKENS)):
             scale_add(new_w[3][:, cols], new_m[3][:, cols], -RATE, w_rows[3][:, cols])
             store(out_1, 3, new_w[3], cols)

@@ -14,6 +14,7 @@ E5M2 = mybir.dt.float8_e5m2_x4
 COPY = mybir.ActivationFunctionType.Copy
 MULT = mybir.AluOpType.mult
 ADD = mybir.AluOpType.add
+SUBTRACT = mybir.AluOpType.subtract
 
 P = 128
 PACK = 4
@@ -264,7 +265,7 @@ def tile_attend_gtied_mom_kernel(tc, V, dz, xT, G, mT, wT, offs, joffs, out_0, o
         db_y = drain("vector", sums_y, P + HALF, 1.0, "db_y")
         scatter_scalar(pb_win[2], i_list, 0, P, db_y[:, 0:P])
         scatter_scalar(pb_win[1], i_list, HALF, SLOTS, db_y[:, P:])
-        new_m_t = [drain("vector", turned[h], SLOTS, DECAY, "new_m_t_%d" % h, (None, 40960)[h]) for h in range(2)]
+        new_m_t = [drain("vector", turned[h], SLOTS, DECAY * RATE, "new_m_t_%d" % h, (None, 40960)[h]) for h in range(2)]
         db_z = drain("vector", sums_z, SLOTS, 1.0, "db_z", 28672 + 448)
         db_w = drain("vector", sums_w, P + HALF, 1.0, "db_w", 28672 + 64 - 4 * (P + HALF))
         scatter_scalar(pb_win[3], i_list, 0, P, db_z[:, 0:P])
@@ -279,9 +280,13 @@ def tile_attend_gtied_mom_kernel(tc, V, dz, xT, G, mT, wT, offs, joffs, out_0, o
             back = bank(1 + h)
             for q in range(4):
                 nc.tensor.transpose(back[:, q * P:(q + 1) * P], new_m_t[h][:, q * P:(q + 1) * P], ident[:])
-            nc.vector.tensor_copy(out=new_m[0][:, halves[h]], in_=back[:])
+            nc.vector.tensor_scalar(
+                out=new_m[0][:, halves[h]], in0=back[:], scalar1=1.0 / RATE, scalar2=None, op0=MULT
+            )
             store(out_0, 0, new_m[0], halves[h])
-            scale_add(new_w[0][:, halves[h]], back[:], -RATE, w_rows[0][:, halves[h]])
+            nc.vector.tensor_tensor(
+                out=new_w[0][:, halves[h]], in0=w_rows[0][:, halves[h]], in1=back[:], op=SUBTRACT
+            )
             store(out_1, 0, new_w[0], halves[h])
 
         whole = slice(0, TOKENS)

@@ -43,8 +43,8 @@ def tile_attend_gtied_mom_kernel(tc, V, dz, xT, G, mT, wT, offs, joffs, out_0, o
                 return keep.tile(shape, dtype, name=name, align_bytes=64)
             return reuse.tile(shape, dtype, name=name, offset=at, align_bytes=64)
 
-        def load_k_first(src, c0, c1, name):
-            raw = tile([P, PACK, c1 - c0], F32, name)
+        def load_k_first(src, c0, c1, name, at=None):
+            raw = tile([P, PACK, c1 - c0], F32, name, at)
             nc.sync.dma_start(out=raw[:], in_=src.rearrange("(p j) n -> p j n", j=PACK)[:, :, c0:c1])
             return raw
 
@@ -53,8 +53,8 @@ def tile_attend_gtied_mom_kernel(tc, V, dz, xT, G, mT, wT, offs, joffs, out_0, o
             nc.sync.dma_start(out=raw[:], in_=src[b * P:(b + 1) * P, :])
             return raw
 
-        def load_x(pair):
-            raw = tile([P, 2, K], F32, "x_%d" % pair)
+        def load_x(pair, at=None):
+            raw = tile([P, 2, K], F32, "x_%d" % pair, at)
             rows = xT[pair * HALF:(pair + 1) * HALF, :]
             nc.sync.dma_start(out=raw[:], in_=rows.rearrange("(n d) r -> d n r", n=2))
             return raw
@@ -64,12 +64,9 @@ def tile_attend_gtied_mom_kernel(tc, V, dz, xT, G, mT, wT, offs, joffs, out_0, o
             nc.sync.dma_start(lst[:], src)
             return lst
 
-        def window(name, engine):
-            win = tile([P, TOKENS], F32, name)
-            if engine == "vector":
-                nc.vector.memset(win[:].bitcast(I32), 0)
-            else:
-                nc.gpsimd.memset(win[:], 0.0)
+        def window(name, at=None):
+            win = tile([P, TOKENS], F32, name, at)
+            nc.vector.memset(win[:].bitcast(I32), 0)
             return win
 
         def mx_operand(name, width, at=None):
@@ -142,13 +139,13 @@ def tile_attend_gtied_mom_kernel(tc, V, dz, xT, G, mT, wT, offs, joffs, out_0, o
         def store(dst, b, src, cols):
             nc.sync.dma_start(out=dst[b * P:(b + 1) * P, cols], in_=src[:, cols])
 
-        v_01 = load_k_first(V, 0, HALF, "v_01")
+        v_01 = load_k_first(V, 0, HALF, "v_01", 90112)
         dz_parts = [(0, P), (P, HALF), (HALF, SLOTS)]
-        dz_first = load_k_first(dz, 0, P, "dz_first")
+        dz_raw = [load_k_first(dz, 0, P, "dz_0")]
         j_list = load_list(joffs, "j_list")
-        dz_rest = load_k_first(dz, P, SLOTS, "dz_rest")
+        dz_raw.extend(load_k_first(dz, c0, c1, "dz_%d" % c0) for c0, c1 in dz_parts[1:])
         v_23 = load_k_first(V, HALF, D, "v_23")
-        x_raw = [load_x(0), load_x(1)]
+        x_raw = [load_x(0, 65536), load_x(1)]
         g_raw = load_k_first(G, 0, SLOTS, "g")
         i_list = load_list(offs, "i_list")
         m_rows, w_rows = {}, {}
@@ -161,12 +158,12 @@ def tile_attend_gtied_mom_kernel(tc, V, dz, xT, G, mT, wT, offs, joffs, out_0, o
         ident_fwd = tile([P, P], F32, "ident_fwd", 28672)
         nc.scalar.copy(out=ident_fwd[:], in_=ident[:])
 
-        pa_win = [window("pa_win_%d" % n, "vector") for n in range(4)]
-        pb_win = [window("pb_win_%d" % n, "vector") for n in range(3)]
-        pb_win.append(pb_win[0])
+        pa_win = [window("pa_win_%d" % n) for n in range(4)]
+        pb_win = [window("pb_win_0")]
 
-        dz_mx = mx_operand("dz", SLOTS)
-        v_01_mx, v_23_mx, x_01_mx, x_23_mx = [mx_operand(n, HALF) for n in ("v_01", "v_23", "x_01", "x_23")]
+        dz_mx = mx_operand("dz", SLOTS, 90112 + 4032)
+        v_01_mx, x_01_mx, x_23_mx = [mx_operand(n, HALF) for n in ("v_01", "x_01", "x_23")]
+        v_23_mx = mx_operand("v_23", HALF, 0)
         g_mx = mx_operand("g", SLOTS, 8192)
         first, second = slice(0, HALF), slice(HALF, SLOTS)
         halves = [slice(0, 512), slice(512, TOKENS)]
@@ -190,38 +187,41 @@ def tile_attend_gtied_mom_kernel(tc, V, dz, xT, G, mT, wT, offs, joffs, out_0, o
             multiply(stationary, n, moving, 0, SLOTS, sums[:])
             return sums
 
-        v_01_woven = weave(v_01[:], "scalar", "v_01_woven")
-        dz_woven = [weave(dz_first[:], "vector", "dz_0_woven")]
+        v_01_woven = weave(v_01[:], "scalar", "v_01_woven", 49152)
+        dz_woven = [weave(dz_raw[0][:], "vector", "dz_0_woven", 81920)]
         quantise(v_01_woven, v_01_mx, 0, E4M3)
         quantise(dz_woven[0], dz_mx, 0, E5M2)
         pair_scatters(0, pair_products(0, 0), "scalar")
-        dz_woven.append(weave(dz_rest[:, :, 0:P], "vector", "dz_1_woven", 49152))
-        dz_woven.append(weave(dz_rest[:, :, P:], "vector", "dz_2_woven"))
+        dz_woven.append(weave(dz_raw[1][:], "vector", "dz_1_woven", 49152 + 1984))
+        pb_win.append(window("pb_win_1", 81920 + 64 - 4096))
         quantise(dz_woven[1], dz_mx, P, E5M2)
         sums_1 = pair_products(1, 1)
+        dz_woven.append(weave(dz_raw[2][:], "vector", "dz_2_woven", 81920 + 960))
+        pair_scatters(1, sums_1, "vector")
         quantise(dz_woven[2], dz_mx, HALF, E5M2)
         sums_2 = pair_products(2, 2)
-        v_23_woven = weave(v_23[:], "vector", "v_23_woven", 49152 + 960)
-        pair_scatters(1, sums_1, "vector")
+        v_23_woven = weave(v_23[:], "vector", "v_23_woven", 49152 + 1984 + 960)
+        pb_win.append(window("pb_win_2", 81920 + 960 + 1984))
+        pb_win.append(pb_win[0])
         quantise(v_23_woven, v_23_mx, 0, E4M3)
         pair_scatters(2, sums_2, "vector")
         sums_a2 = product(v_23_mx, 0, dz_mx, 0)
         sums_a3 = product(v_23_mx, 1, dz_mx, 1)
-        x_01_pairs = round_x(x_raw[0], "x_01_pairs", 0)
+        x_01_pairs = round_x(x_raw[0], "x_01_pairs", 49152 + 1984 + 960 + 1984)
         turned_01 = bank(3)
         turn_x(x_01_pairs, turned_01)
-        da_2 = drain("vector", sums_a2, SLOTS, 1.0 / DECAY, "da_2")
-        x_23_pairs = round_x(x_raw[1], "x_23_pairs")
+        x_23_pairs = round_x(x_raw[1], "x_23_pairs", 65536 + 4032)
         turned_23 = bank(4)
         turn_x(x_23_pairs, turned_23)
+        da_2 = drain("vector", sums_a2, SLOTS, 1.0 / DECAY, "da_2")
         da_3 = drain("vector", sums_a3, SLOTS, 1.0 / DECAY, "da_3")
         for cols in (first, second):
             scatter_scalar(pa_win[2], j_list, cols.start, cols.stop, da_2[:, cols])
             scatter_scalar(pa_win[3], j_list, cols.start, cols.stop, da_3[:, cols])
+        g_woven = weave(g_raw[:], "vector", "g_woven", 960)
         x_01_woven = weave_x(turned_01, "x_01_woven")
-        g_woven = weave(g_raw[:], "vector", "g_woven", 1984)
-        quantise(x_01_woven, x_01_mx, 0, E4M3)
         quantise(g_woven, g_mx, 0, E5M2)
+        quantise(x_01_woven, x_01_mx, 0, E4M3)
         sums_b0 = product(x_01_mx, 0, g_mx, 1)
         x_23_woven = weave_x(turned_23, "x_23_woven")
         quantise(x_23_woven, x_23_mx, 0, E4M3)
@@ -297,6 +297,8 @@ def tile_attend_gtied_mom_kernel(tc, V, dz, xT, G, mT, wT, offs, joffs, out_0, o
             scale_add(new_w[1][:, cols], new_m[1][:, cols], -RATE, w_rows[1][:, cols])
         store(out_1, 1, new_w[1], whole)
 
+        partial_3v = tile([P, TOKENS - SHARE], F32, "partial_3v", 40960 + 64 - 4 * (TOKENS - SHARE))
+        nc.vector.tensor_tensor(out=partial_3v[:], in0=m_rows[3][:, by_vector], in1=pa_win[3][:, by_vector], op=ADD)
         for cols, part in ((by_gpsimd, partial_g[:, 0, :]), (by_vector, partial_2v[:])):
             scale_add(new_m[2][:, cols], part, DECAY, pb_win[2][:, cols])
         store(out_0, 2, new_m[2], whole)
@@ -304,8 +306,6 @@ def tile_attend_gtied_mom_kernel(tc, V, dz, xT, G, mT, wT, offs, joffs, out_0, o
             scale_add(new_w[2][:, cols], new_m[2][:, cols], -RATE, w_rows[2][:, cols])
         store(out_1, 2, new_w[2], whole)
 
-        partial_3v = tile([P, TOKENS - SHARE], F32, "partial_3v", 40960 + 64 - 4 * (TOKENS - SHARE))
-        nc.vector.tensor_tensor(out=partial_3v[:], in0=m_rows[3][:, by_vector], in1=pa_win[3][:, by_vector], op=ADD)
         for cols, part in ((by_gpsimd, partial_g[:, 1, :]), (by_vector, partial_3v[:])):
             scale_add(new_m[3][:, cols], part, DECAY, pb_win[3][:, cols])
             store(out_0, 3, new_m[3], cols)

@@ -48,13 +48,13 @@ def tile_attend_gtied_mom_kernel(tc, V, dz, xT, G, mT, wT, offs, joffs, out_0, o
             nc.sync.dma_start(out=raw[:], in_=src.rearrange("(p j) n -> p j n", j=PACK)[:, :, c0:c1])
             return raw
 
-        def load_rows(src, b, name):
-            raw = tile([P, TOKENS], F32, name)
+        def load_rows(src, b, name, at=None):
+            raw = tile([P, TOKENS], F32, name, at)
             nc.sync.dma_start(out=raw[:], in_=src[b * P:(b + 1) * P, :])
             return raw
 
-        def load_x(pair, at=None):
-            raw = tile([P, 2, K], F32, "x_%d" % pair, at)
+        def load_x(pair):
+            raw = tile([P, 2, K], F32, "x_%d" % pair)
             rows = xT[pair * HALF:(pair + 1) * HALF, :]
             nc.sync.dma_start(out=raw[:], in_=rows.rearrange("(n d) r -> d n r", n=2))
             return raw
@@ -104,8 +104,8 @@ def tile_attend_gtied_mom_kernel(tc, V, dz, xT, G, mT, wT, offs, joffs, out_0, o
             for q in range(4):
                 nc.tensor.transpose(turned[:, q * P:(q + 1) * P], words[:, q * P:(q + 1) * P], ident[:])
 
-        def weave_x(turned, name):
-            woven = tile([P, HALF, PACK], BF16, name)
+        def weave_x(turned, name, at=None):
+            woven = tile([P, HALF, PACK], BF16, name, at)
             dst = woven[:].rearrange("p d t -> p (d t)").bitcast(F32).rearrange("p (n d u) -> p n d u", n=2, u=2)
             nc.vector.tensor_copy(out=dst, in_=turned[:].rearrange("p (n u d) -> p n d u", n=2, u=2))
             return woven
@@ -130,8 +130,8 @@ def tile_attend_gtied_mom_kernel(tc, V, dz, xT, G, mT, wT, offs, joffs, out_0, o
                 nc.scalar.activation(out=grad[:], in_=sums[:, 0:width], func=COPY, scale=scale)
             return grad
 
-        def scatter_scalar(win, lst, s0, s1, grad):
-            nc.scalar.activation(out=win[:].indirect(lst[:, s0 // 16:s1 // 16]), in_=grad, func=COPY)
+        def scatter_scalar(win, lst, s0, s1, grad, scale=1.0):
+            nc.scalar.activation(out=win[:].indirect(lst[:, s0 // 16:s1 // 16]), in_=grad, func=COPY, scale=scale)
 
         def scale_add(dst, src, factor, other):
             nc.vector.scalar_tensor_tensor(out=dst, in0=src, scalar=factor, in1=other, op0=MULT, op1=ADD)
@@ -145,25 +145,25 @@ def tile_attend_gtied_mom_kernel(tc, V, dz, xT, G, mT, wT, offs, joffs, out_0, o
         j_list = load_list(joffs, "j_list")
         dz_raw.extend(load_k_first(dz, c0, c1, "dz_%d" % c0) for c0, c1 in dz_parts[1:])
         v_23 = load_k_first(V, HALF, D, "v_23")
-        x_raw = [load_x(0, 65536), load_x(1)]
-        g_raw = load_k_first(G, 0, SLOTS, "g")
+        x_raw = [load_x(0), load_x(1)]
+        g_raw = load_k_first(G, 0, SLOTS, "g", 28672 + 64 - 8192)
         i_list = load_list(offs, "i_list")
         m_rows, w_rows = {}, {}
-        for rows, src, name, b in ((m_rows, mT, "m", 0), (m_rows, mT, "m", 2), (m_rows, mT, "m", 1), (m_rows, mT, "m", 3),
-                                   (w_rows, wT, "w", 0), (w_rows, wT, "w", 1), (w_rows, wT, "w", 2), (w_rows, wT, "w", 3)):
-            rows[b] = load_rows(src, b, "%s_%d" % (name, b))
+        for rows, src, name, b in ((m_rows, mT, "m", 1), (m_rows, mT, "m", 0), (w_rows, wT, "w", 1), (m_rows, mT, "m", 2),
+                                   (m_rows, mT, "m", 3), (w_rows, wT, "w", 0), (w_rows, wT, "w", 2), (w_rows, wT, "w", 3)):
+            rows[b] = load_rows(src, b, "%s_%d" % (name, b), 32768 if (name, b) == ("w", 1) else None)
 
         ident = keep.tile([P, P], F32, name="ident")
         make_identity(nc, ident[:])
-        ident_fwd = tile([P, P], F32, "ident_fwd", 28672)
-        nc.scalar.copy(out=ident_fwd[:], in_=ident[:])
 
-        pa_win = [window("pa_win_%d" % n) for n in range(4)]
-        pb_win = [window("pb_win_0")]
+        pa_win = [window("pa_win_%d" % n) for n in range(3)]
+        pb_win = [window("pb_win_%d" % n) for n in range(2)]
+        pa_win.append(pa_win[0])
+        pb_win.extend([pb_win[1], pb_win[0]])
 
         dz_mx = mx_operand("dz", SLOTS, 90112 + 4032)
         v_01_mx, x_01_mx, x_23_mx = [mx_operand(n, HALF) for n in ("v_01", "x_01", "x_23")]
-        v_23_mx = mx_operand("v_23", HALF, 0)
+        v_23_mx = mx_operand("v_23", HALF)
         g_mx = mx_operand("g", SLOTS, 8192)
         first, second = slice(0, HALF), slice(HALF, SLOTS)
         halves = [slice(0, 512), slice(512, TOKENS)]
@@ -182,102 +182,108 @@ def tile_attend_gtied_mom_kernel(tc, V, dz, xT, G, mT, wT, offs, joffs, out_0, o
             for b in range(2):
                 scatter_scalar(pa_win[b], j_list, c0, c1, grads[:, b * width:(b + 1) * width])
 
-        def product(stationary, n, moving, n_bank):
+        def pieces(n_bank, parts):
             sums = bank(n_bank)
-            multiply(stationary, n, moving, 0, SLOTS, sums[:])
+            at = 0
+            for stationary, n, moving, c0, c1 in parts:
+                multiply(stationary, n, moving, c0, c1, sums[:, at:at + c1 - c0])
+                at = at + c1 - c0
             return sums
+
+        def add_turned(addend, unit, opens, closes):
+            for h in range(2):
+                for q in range(4):
+                    c = (4 * h + q) * P
+                    nc.tensor.matmul(turned[h][:, q * P:(q + 1) * P], lhsT=addend[:, c:c + P], rhs=unit[:],
+                                     start=(opens and q == 0), stop=(closes and q == 3), is_transpose=True)
 
         v_01_woven = weave(v_01[:], "scalar", "v_01_woven", 49152)
         dz_woven = [weave(dz_raw[0][:], "vector", "dz_0_woven", 81920)]
         quantise(v_01_woven, v_01_mx, 0, E4M3)
         quantise(dz_woven[0], dz_mx, 0, E5M2)
+        dz_woven.append(weave(dz_raw[1][:], "scalar", "dz_1_woven", 90112 + 64 - 1024))
         pair_scatters(0, pair_products(0, 0), "scalar")
-        dz_woven.append(weave(dz_raw[1][:], "vector", "dz_1_woven", 49152 + 1984))
-        pb_win.append(window("pb_win_1", 81920 + 64 - 4096))
+        dz_woven.append(weave(dz_raw[2][:], "vector", "dz_2_woven", 49152 + 64 - 2048))
         quantise(dz_woven[1], dz_mx, P, E5M2)
         sums_1 = pair_products(1, 1)
-        dz_woven.append(weave(dz_raw[2][:], "vector", "dz_2_woven", 81920 + 960))
-        pair_scatters(1, sums_1, "vector")
         quantise(dz_woven[2], dz_mx, HALF, E5M2)
         sums_2 = pair_products(2, 2)
-        v_23_woven = weave(v_23[:], "vector", "v_23_woven", 49152 + 1984 + 960)
-        pb_win.append(window("pb_win_2", 81920 + 960 + 1984))
-        pb_win.append(pb_win[0])
+        v_23_woven = weave(v_23[:], "vector", "v_23_woven", 87168)
+        pair_scatters(1, sums_1, "vector")
         quantise(v_23_woven, v_23_mx, 0, E4M3)
         pair_scatters(2, sums_2, "vector")
-        sums_a2 = product(v_23_mx, 0, dz_mx, 0)
-        sums_a3 = product(v_23_mx, 1, dz_mx, 1)
-        x_01_pairs = round_x(x_raw[0], "x_01_pairs", 49152 + 1984 + 960 + 1984)
+        sums_a = pieces(1, [(v_23_mx, 0, dz_mx, 0, HALF), (v_23_mx, 1, dz_mx, 0, HALF)])
+        x_01_pairs = round_x(x_raw[0], "x_01_pairs", 85184)
         turned_01 = bank(3)
         turn_x(x_01_pairs, turned_01)
-        x_23_pairs = round_x(x_raw[1], "x_23_pairs", 65536 + 4032)
+        x_23_pairs = round_x(x_raw[1], "x_23_pairs", 87168 + 1984)
         turned_23 = bank(4)
         turn_x(x_23_pairs, turned_23)
-        da_2 = drain("vector", sums_a2, SLOTS, 1.0 / DECAY, "da_2")
-        da_3 = drain("vector", sums_a3, SLOTS, 1.0 / DECAY, "da_3")
-        for cols in (first, second):
-            scatter_scalar(pa_win[2], j_list, cols.start, cols.stop, da_2[:, cols])
-            scatter_scalar(pa_win[3], j_list, cols.start, cols.stop, da_3[:, cols])
-        g_woven = weave(g_raw[:], "vector", "g_woven", 960)
+        da_first = drain("vector", sums_a, SLOTS, 1.0 / DECAY, "da_first")
         x_01_woven = weave_x(turned_01, "x_01_woven")
-        quantise(g_woven, g_mx, 0, E5M2)
+        turned = [bank(3), bank(1)]
+        add_turned(pa_win[0], ident, True, False)
+        scatter_scalar(pa_win[2], j_list, 0, HALF, da_first[:, first])
+        scatter_scalar(pa_win[3], j_list, 0, HALF, da_first[:, second])
+        g_woven = weave(g_raw[:], "vector", "g_woven", 81152)
         quantise(x_01_woven, x_01_mx, 0, E4M3)
-        sums_b0 = product(x_01_mx, 0, g_mx, 1)
-        x_23_woven = weave_x(turned_23, "x_23_woven")
-        quantise(x_23_woven, x_23_mx, 0, E4M3)
-        db_0 = drain("vector", sums_b0, SLOTS, 1.0 / DECAY, "db_0", 16384)
-
-        def pieces(n_bank, parts):
-            sums = bank(n_bank)
-            at = 0
-            for b, c0, c1 in parts:
-                multiply((x_01_mx, x_23_mx)[b // 2], b % 2, g_mx, c0, c1, sums[:, at:at + c1 - c0])
-                at = at + c1 - c0
-            return sums
-
-        sums_x = pieces(2, [(1, 0, HALF)])
-        sums_y = pieces(4, [(2, 0, P), (1, HALF, SLOTS)])
-        sums_z = pieces(5, [(3, 0, P), (2, P, HALF), (2, HALF, SLOTS)])
-        sums_w = pieces(6, [(3, P, HALF), (3, HALF, SLOTS)])
-        db_x = drain("vector", sums_x, HALF, 1.0, "db_x")
-        nc.vector.tensor_copy(pb_win[0][:].indirect(i_list[:]), db_0[:])
-        scatter_scalar(pb_win[1], i_list, 0, HALF, db_x[:])
-
-        turned = [bank(3), bank(0)]
-        for n, addend in enumerate((pa_win[0], m_rows[0], pb_win[0])):
-            for h in range(2):
-                for q in range(4):
-                    c = (4 * h + q) * P
-                    nc.tensor.matmul(turned[h][:, q * P:(q + 1) * P], lhsT=addend[:, c:c + P], rhs=ident_fwd[:],
-                                     start=(n == 0 and q == 0), stop=(n == 2 and q == 3), is_transpose=True)
-
-        by_gpsimd, by_vector = slice(0, SHARE), slice(SHARE, TOKENS)
-        partial_2v = tile([P, TOKENS - SHARE], F32, "partial_2v", 8192 + 1984)
-        nc.vector.tensor_tensor(out=partial_2v[:], in0=m_rows[2][:, by_vector], in1=pa_win[2][:, by_vector], op=ADD)
-        partial_1 = tile([P, TOKENS], F32, "partial_1", 16384 + 1984)
+        quantise(g_woven, g_mx, 0, E5M2)
+        sums_x = pieces(0, [(x_01_mx, 0, g_mx, 0, HALF), (v_23_mx, 0, dz_mx, HALF, SLOTS)])
+        sums_u = pieces(2, [(x_01_mx, 0, g_mx, HALF, SLOTS), (v_23_mx, 1, dz_mx, HALF, SLOTS)])
+        sums_b1 = pieces(5, [(x_01_mx, 1, g_mx, 0, SLOTS)])
+        partial_1 = tile([P, TOKENS], F32, "partial_1", 81152 + 64 - 4096)
         nc.gpsimd.tensor_tensor(out=partial_1[:], in0=m_rows[1][:], in1=pa_win[1][:], op=ADD)
-        partial_g = tile([P, 2, SHARE], F32, "partial_g", 16384 + 64 - 8 * SHARE)
-        for b in (2, 3):
-            nc.gpsimd.tensor_tensor(
-                out=partial_g[:, b - 2, :], in0=m_rows[b][:, by_gpsimd], in1=pa_win[b][:, by_gpsimd], op=ADD
-            )
+        x_23_woven = weave_x(turned_23, "x_23_woven", 28672)
+        grads_x = drain("vector", sums_x, SLOTS, 1.0 / DECAY, "grads_x")
+        grads_u = drain("vector", sums_u, SLOTS, 1.0 / DECAY, "grads_u")
+        db_1 = drain("vector", sums_b1, SLOTS, 1.0, "db_1", 16384)
+        quantise(x_23_woven, x_23_mx, 0, E4M3)
+        nc.vector.tensor_copy(pb_win[1][:].indirect(i_list[:]), db_1[:])
+        sums_y = pieces(4, [(x_23_mx, 0, g_mx, 0, HALF), (x_23_mx, 1, g_mx, 0, P)])
+        sums_z = pieces(6, [(x_23_mx, 0, g_mx, HALF, SLOTS)])
+        sums_w = pieces(7, [(x_23_mx, 1, g_mx, P, HALF), (x_23_mx, 1, g_mx, HALF, SLOTS)])
+        ident_late = tile([P, P], F32, "ident_late", 28672)
+        nc.vector.tensor_copy(out=ident_late[:], in_=ident[:])
+        add_turned(m_rows[0], ident_late, False, False)
+        for cols, grads, win in ((first, grads_x, pa_win[2]), (second, grads_u, pa_win[3])):
+            scatter_scalar(pb_win[0], i_list, cols.start, cols.stop, grads[:, first])
+            scatter_scalar(win, j_list, HALF, SLOTS, grads[:, second])
+        add_turned(pb_win[0], ident_late, False, True)
 
-        db_y = drain("vector", sums_y, P + HALF, 1.0, "db_y")
-        scatter_scalar(pb_win[2], i_list, 0, P, db_y[:, 0:P])
-        scatter_scalar(pb_win[1], i_list, HALF, SLOTS, db_y[:, P:])
-        new_m_t = [drain("vector", turned[h], SLOTS, DECAY * RATE, "new_m_t_%d" % h, (None, 40960)[h]) for h in range(2)]
-        db_z = drain("vector", sums_z, SLOTS, 1.0, "db_z", 28672 + 448)
-        db_w = drain("vector", sums_w, P + HALF, 1.0, "db_w", 28672 + 64 - 4 * (P + HALF))
-        scatter_scalar(pb_win[3], i_list, 0, P, db_z[:, 0:P])
-        scatter_scalar(pb_win[2], i_list, P, SLOTS, db_z[:, P:])
-        scatter_scalar(pb_win[3], i_list, P, SLOTS, db_w[:])
-
-        places = (None, 40960 + 1984, 16384 + 1984 + 4032, None)
+        places = (None, None, 40960 + 1984, None)
         new_m = [tile([P, TOKENS], F32, "new_m_%d" % b, places[b]) for b in range(BLOCKS)]
         new_w = [tile([P, TOKENS], F32, "new_w_%d" % b) for b in range(BLOCKS)]
+        whole = slice(0, TOKENS)
+        by_gpsimd, by_vector = slice(0, SHARE), slice(SHARE, TOKENS)
+
+        def finish(b, partial):
+            for cols in halves:
+                scale_add(new_m[b][:, cols], partial[:, cols], DECAY, pb_win[b][:, cols])
+            store(out_0, b, new_m[b], whole)
+            for cols in halves:
+                scale_add(new_w[b][:, cols], new_m[b][:, cols], -RATE, w_rows[b][:, cols])
+            store(out_1, b, new_w[b], whole)
+
+        db_y = drain("vector", sums_y, HALF + P, 1.0, "db_y", 8192 + 1984)
+        finish(1, partial_1)
+
+        partial_2 = tile([P, TOKENS], F32, "partial_2", 32768 + 4032)
+        nc.gpsimd.tensor_tensor(out=partial_2[:], in0=m_rows[2][:], in1=pa_win[2][:], op=ADD)
+        partial_3g = tile([P, SHARE], F32, "partial_3g", 32768 + 64 - 4 * SHARE)
+        nc.gpsimd.tensor_tensor(out=partial_3g[:], in0=m_rows[3][:, by_gpsimd], in1=pa_win[3][:, by_gpsimd], op=ADD)
+
+        new_m_t = [
+            drain("vector", turned[h], SLOTS, DECAY * RATE, "new_m_t_%d" % h, (None, 40960)[h]) for h in range(2)
+        ]
+        db_z = drain("vector", sums_z, HALF, 1.0, "db_z", 28672 + 448)
+        db_w = drain("vector", sums_w, P + HALF, 1.0, "db_w", 28672 + 64 - 4 * (P + HALF))
+        scatter_scalar(pb_win[2], i_list, 0, HALF, db_y[:, first])
+        scatter_scalar(pb_win[3], i_list, 0, P, db_y[:, HALF:])
+        scatter_scalar(pb_win[2], i_list, HALF, SLOTS, db_z[:])
+        scatter_scalar(pb_win[3], i_list, P, SLOTS, db_w[:])
 
         for h in range(2):
-            back = bank(1 + h)
+            back = bank(2 * h)
             for q in range(4):
                 nc.tensor.transpose(back[:, q * P:(q + 1) * P], new_m_t[h][:, q * P:(q + 1) * P], ident[:])
             nc.vector.tensor_scalar(
@@ -289,25 +295,12 @@ def tile_attend_gtied_mom_kernel(tc, V, dz, xT, G, mT, wT, offs, joffs, out_0, o
             )
             store(out_1, 0, new_w[0], halves[h])
 
-        whole = slice(0, TOKENS)
-        for cols in halves:
-            scale_add(new_m[1][:, cols], partial_1[:, cols], DECAY, pb_win[1][:, cols])
-            store(out_0, 1, new_m[1], cols)
-        for cols in halves:
-            scale_add(new_w[1][:, cols], new_m[1][:, cols], -RATE, w_rows[1][:, cols])
-        store(out_1, 1, new_w[1], whole)
+        finish(2, partial_2)
 
-        partial_3v = tile([P, TOKENS - SHARE], F32, "partial_3v", 40960 + 64 - 4 * (TOKENS - SHARE))
+        partial_3v = tile([P, TOKENS - SHARE], F32, "partial_3v", 32768 + 4032 + 64)
         nc.vector.tensor_tensor(out=partial_3v[:], in0=m_rows[3][:, by_vector], in1=pa_win[3][:, by_vector], op=ADD)
-        for cols, part in ((by_gpsimd, partial_g[:, 0, :]), (by_vector, partial_2v[:])):
-            scale_add(new_m[2][:, cols], part, DECAY, pb_win[2][:, cols])
-        store(out_0, 2, new_m[2], whole)
-        for cols in (by_gpsimd, by_vector):
-            scale_add(new_w[2][:, cols], new_m[2][:, cols], -RATE, w_rows[2][:, cols])
-        store(out_1, 2, new_w[2], whole)
-
-        for cols, part in ((by_gpsimd, partial_g[:, 1, :]), (by_vector, partial_3v[:])):
-            scale_add(new_m[3][:, cols], part, DECAY, pb_win[3][:, cols])
+        for cols, part in ((by_gpsimd, partial_3g), (by_vector, partial_3v)):
+            scale_add(new_m[3][:, cols], part[:], DECAY, pb_win[3][:, cols])
             store(out_0, 3, new_m[3], cols)
         for cols in (by_gpsimd, slice(SHARE, 768), slice(768, TOKENS)):
             scale_add(new_w[3][:, cols], new_m[3][:, cols], -RATE, w_rows[3][:, cols])

@@ -53,8 +53,8 @@ def tile_attend_gtied_mom_kernel(tc, V, dz, xT, G, mT, wT, offs, joffs, out_0, o
             nc.sync.dma_start(out=raw[:], in_=src[b * P:(b + 1) * P, :])
             return raw
 
-        def load_x(pair):
-            raw = tile([P, 2, K], F32, "x_%d" % pair)
+        def load_x(pair, at=None):
+            raw = tile([P, 2, K], F32, "x_%d" % pair, at)
             rows = xT[pair * HALF:(pair + 1) * HALF, :]
             nc.sync.dma_start(out=raw[:], in_=rows.rearrange("(n d) r -> d n r", n=2))
             return raw
@@ -66,20 +66,26 @@ def tile_attend_gtied_mom_kernel(tc, V, dz, xT, G, mT, wT, offs, joffs, out_0, o
 
         def window(name, at=None):
             win = tile([P, TOKENS], F32, name, at)
-            nc.vector.memset(win[:].bitcast(I32), 0)
+            if at is None:
+                nc.vector.memset(win[:].bitcast(I32), 0)
+            else:
+                nc.gpsimd.memset(win[:], 0.0)
             return win
 
         def mx_operand(name, width, at=None):
             return tile([P, width], U32, name + "_codes", at), tile([P, width], U8, name + "_scales")
 
-        def weave(raw, engine, name, at=None):
-            woven = tile([P, raw.shape[2], PACK], BF16, name, at)
-            dst = woven[:].rearrange("p (c i) t -> p c t i", i=4)
+        def weave_into(woven, raw, engine):
+            dst = woven.rearrange("p (c i) t -> p c t i", i=4)
             src = raw.rearrange("p t (c i) -> p c t i", i=4)
             if engine == "vector":
                 nc.vector.tensor_copy(out=dst, in_=src)
             else:
                 nc.scalar.activation(out=dst, in_=src, func=COPY)
+
+        def weave(raw, engine, name, at=None):
+            woven = tile([P, raw.shape[2], PACK], BF16, name, at)
+            weave_into(woven[:], raw, engine)
             return woven
 
         def quantise(woven, operand, c0, fmt):
@@ -145,21 +151,19 @@ def tile_attend_gtied_mom_kernel(tc, V, dz, xT, G, mT, wT, offs, joffs, out_0, o
         j_list = load_list(joffs, "j_list")
         dz_raw.extend(load_k_first(dz, c0, c1, "dz_%d" % c0) for c0, c1 in dz_parts[1:])
         v_23 = load_k_first(V, HALF, D, "v_23")
-        x_raw = [load_x(0), load_x(1)]
+        x_raw = [load_x(0, 57344), load_x(1)]
         g_raw = load_k_first(G, 0, SLOTS, "g", 28672 + 64 - 8192)
         i_list = load_list(offs, "i_list")
         m_rows, w_rows = {}, {}
         for rows, src, name, b in ((m_rows, mT, "m", 1), (m_rows, mT, "m", 0), (w_rows, wT, "w", 1), (m_rows, mT, "m", 2),
                                    (m_rows, mT, "m", 3), (w_rows, wT, "w", 0), (w_rows, wT, "w", 2), (w_rows, wT, "w", 3)):
-            rows[b] = load_rows(src, b, "%s_%d" % (name, b), 32768 if (name, b) == ("w", 1) else None)
+            rows[b] = load_rows(src, b, "%s_%d" % (name, b), {("w", 1): 32768, ("m", 2): 65536 + 2048}.get((name, b)))
 
         ident = keep.tile([P, P], F32, name="ident")
         make_identity(nc, ident[:])
 
         pa_win = [window("pa_win_%d" % n) for n in range(3)]
-        pb_win = [window("pb_win_%d" % n) for n in range(2)]
         pa_win.append(pa_win[0])
-        pb_win.extend([pb_win[1], pb_win[0]])
 
         dz_mx = mx_operand("dz", SLOTS, 90112 + 4032)
         v_01_mx, x_01_mx, x_23_mx = [mx_operand(n, HALF) for n in ("v_01", "x_01", "x_23")]
@@ -197,7 +201,9 @@ def tile_attend_gtied_mom_kernel(tc, V, dz, xT, G, mT, wT, offs, joffs, out_0, o
                     nc.tensor.matmul(turned[h][:, q * P:(q + 1) * P], lhsT=addend[:, c:c + P], rhs=unit[:],
                                      start=(opens and q == 0), stop=(closes and q == 3), is_transpose=True)
 
-        v_01_woven = weave(v_01[:], "scalar", "v_01_woven", 49152)
+        v_01_woven = tile([P, HALF, PACK], BF16, "v_01_woven", 49152)
+        weave_into(v_01_woven[:, 0:P, :], v_01[:, :, 0:P], "vector")
+        weave_into(v_01_woven[:, P:, :], v_01[:, :, P:], "scalar")
         dz_woven = [weave(dz_raw[0][:], "vector", "dz_0_woven", 81920)]
         quantise(v_01_woven, v_01_mx, 0, E4M3)
         quantise(dz_woven[0], dz_mx, 0, E5M2)
@@ -209,14 +215,17 @@ def tile_attend_gtied_mom_kernel(tc, V, dz, xT, G, mT, wT, offs, joffs, out_0, o
         quantise(dz_woven[2], dz_mx, HALF, E5M2)
         sums_2 = pair_products(2, 2)
         v_23_woven = weave(v_23[:], "vector", "v_23_woven", 87168)
+        pb_win = [window("pb_win_0", 49152)]
         pair_scatters(1, sums_1, "vector")
-        quantise(v_23_woven, v_23_mx, 0, E4M3)
         pair_scatters(2, sums_2, "vector")
+        quantise(v_23_woven, v_23_mx, 0, E4M3)
         sums_a = pieces(1, [(v_23_mx, 0, dz_mx, 0, HALF), (v_23_mx, 1, dz_mx, 0, HALF)])
         x_01_pairs = round_x(x_raw[0], "x_01_pairs", 85184)
         turned_01 = bank(3)
         turn_x(x_01_pairs, turned_01)
         x_23_pairs = round_x(x_raw[1], "x_23_pairs", 87168 + 1984)
+        pb_win.append(window("pb_win_1", 57344 + 4032))
+        pb_win.extend([pb_win[1], pb_win[0]])
         turned_23 = bank(4)
         turn_x(x_23_pairs, turned_23)
         da_first = drain("vector", sums_a, SLOTS, 1.0 / DECAY, "da_first")
@@ -225,13 +234,17 @@ def tile_attend_gtied_mom_kernel(tc, V, dz, xT, G, mT, wT, offs, joffs, out_0, o
         add_turned(pa_win[0], ident, True, False)
         scatter_scalar(pa_win[2], j_list, 0, HALF, da_first[:, first])
         scatter_scalar(pa_win[3], j_list, 0, HALF, da_first[:, second])
-        g_woven = weave(g_raw[:], "vector", "g_woven", 81152)
+        g_woven = [
+            weave(g_raw[:, :, cols], "vector", "g_woven_%d" % cols.start, at)
+            for cols, at in ((first, 83200), (second, 83200 + 64 - 2048 - 64))
+        ]
         quantise(x_01_woven, x_01_mx, 0, E4M3)
-        quantise(g_woven, g_mx, 0, E5M2)
-        sums_x = pieces(0, [(x_01_mx, 0, g_mx, 0, HALF), (v_23_mx, 0, dz_mx, HALF, SLOTS)])
-        sums_u = pieces(2, [(x_01_mx, 0, g_mx, HALF, SLOTS), (v_23_mx, 1, dz_mx, HALF, SLOTS)])
+        quantise(g_woven[0], g_mx, 0, E5M2)
+        quantise(g_woven[1], g_mx, HALF, E5M2)
+        sums_x = pieces(0, [(v_23_mx, 0, dz_mx, HALF, SLOTS), (x_01_mx, 0, g_mx, 0, HALF)])
+        sums_u = pieces(2, [(v_23_mx, 1, dz_mx, HALF, SLOTS), (x_01_mx, 0, g_mx, HALF, SLOTS)])
         sums_b1 = pieces(5, [(x_01_mx, 1, g_mx, 0, SLOTS)])
-        partial_1 = tile([P, TOKENS], F32, "partial_1", 81152 + 64 - 4096)
+        partial_1 = tile([P, TOKENS], F32, "partial_1", 83200 + 1984)
         nc.gpsimd.tensor_tensor(out=partial_1[:], in0=m_rows[1][:], in1=pa_win[1][:], op=ADD)
         x_23_woven = weave_x(turned_23, "x_23_woven", 28672)
         grads_x = drain("vector", sums_x, SLOTS, 1.0 / DECAY, "grads_x")
@@ -246,8 +259,8 @@ def tile_attend_gtied_mom_kernel(tc, V, dz, xT, G, mT, wT, offs, joffs, out_0, o
         nc.vector.tensor_copy(out=ident_late[:], in_=ident[:])
         add_turned(m_rows[0], ident_late, False, False)
         for cols, grads, win in ((first, grads_x, pa_win[2]), (second, grads_u, pa_win[3])):
-            scatter_scalar(pb_win[0], i_list, cols.start, cols.stop, grads[:, first])
-            scatter_scalar(win, j_list, HALF, SLOTS, grads[:, second])
+            scatter_scalar(pb_win[0], i_list, cols.start, cols.stop, grads[:, second])
+            scatter_scalar(win, j_list, HALF, SLOTS, grads[:, first])
         add_turned(pb_win[0], ident_late, False, True)
 
         places = (None, None, 40960 + 1984, None)
@@ -269,7 +282,7 @@ def tile_attend_gtied_mom_kernel(tc, V, dz, xT, G, mT, wT, offs, joffs, out_0, o
 
         partial_2 = tile([P, TOKENS], F32, "partial_2", 32768 + 4032)
         nc.gpsimd.tensor_tensor(out=partial_2[:], in0=m_rows[2][:], in1=pa_win[2][:], op=ADD)
-        partial_3g = tile([P, SHARE], F32, "partial_3g", 32768 + 64 - 4 * SHARE)
+        partial_3g = tile([P, SHARE], F32, "partial_3g", 65536 + 2048 + 4032)
         nc.gpsimd.tensor_tensor(out=partial_3g[:], in0=m_rows[3][:, by_gpsimd], in1=pa_win[3][:, by_gpsimd], op=ADD)
 
         new_m_t = [

@@ -26,7 +26,8 @@ HALF = 256
 BLOCKS = D // P
 DECAY = 0.9
 RATE = 0.1
-SHARE = 384
+SHARE = 192
+EARLY = 640
 
 FLOPS = 2 * 2 * K * D * SLOTS
 
@@ -53,8 +54,8 @@ def tile_attend_gtied_mom_kernel(tc, V, dz, xT, G, mT, wT, offs, joffs, out_0, o
             nc.sync.dma_start(out=raw[:], in_=src[b * P:(b + 1) * P, :])
             return raw
 
-        def load_x(pair, at=None):
-            raw = tile([P, 2, K], F32, "x_%d" % pair, at)
+        def load_x(pair):
+            raw = tile([P, 2, K], F32, "x_%d" % pair)
             rows = xT[pair * HALF:(pair + 1) * HALF, :]
             nc.sync.dma_start(out=raw[:], in_=rows.rearrange("(n d) r -> d n r", n=2))
             return raw
@@ -64,12 +65,9 @@ def tile_attend_gtied_mom_kernel(tc, V, dz, xT, G, mT, wT, offs, joffs, out_0, o
             nc.sync.dma_start(lst[:], src)
             return lst
 
-        def window(name, at=None):
-            win = tile([P, TOKENS], F32, name, at)
-            if at is None:
-                nc.vector.memset(win[:].bitcast(I32), 0)
-            else:
-                nc.gpsimd.memset(win[:], 0.0)
+        def window(name):
+            win = tile([P, TOKENS], F32, name)
+            nc.vector.memset(win[:].bitcast(I32), 0)
             return win
 
         def mx_operand(name, width, at=None):
@@ -151,7 +149,7 @@ def tile_attend_gtied_mom_kernel(tc, V, dz, xT, G, mT, wT, offs, joffs, out_0, o
         j_list = load_list(joffs, "j_list")
         dz_raw.extend(load_k_first(dz, c0, c1, "dz_%d" % c0) for c0, c1 in dz_parts[1:])
         v_23 = load_k_first(V, HALF, D, "v_23")
-        x_raw = [load_x(0, 57344), load_x(1)]
+        x_raw = [load_x(0), load_x(1)]
         g_raw = load_k_first(G, 0, SLOTS, "g", 28672 + 64 - 8192)
         i_list = load_list(offs, "i_list")
         m_rows, w_rows = {}, {}
@@ -163,7 +161,9 @@ def tile_attend_gtied_mom_kernel(tc, V, dz, xT, G, mT, wT, offs, joffs, out_0, o
         make_identity(nc, ident[:])
 
         pa_win = [window("pa_win_%d" % n) for n in range(3)]
+        pb_win = [window("pb_win_%d" % n) for n in range(2)]
         pa_win.append(pa_win[0])
+        pb_win.extend([pb_win[1], pb_win[0]])
 
         dz_mx = mx_operand("dz", SLOTS, 90112 + 4032)
         v_01_mx, x_01_mx, x_23_mx = [mx_operand(n, HALF) for n in ("v_01", "x_01", "x_23")]
@@ -201,9 +201,7 @@ def tile_attend_gtied_mom_kernel(tc, V, dz, xT, G, mT, wT, offs, joffs, out_0, o
                     nc.tensor.matmul(turned[h][:, q * P:(q + 1) * P], lhsT=addend[:, c:c + P], rhs=unit[:],
                                      start=(opens and q == 0), stop=(closes and q == 3), is_transpose=True)
 
-        v_01_woven = tile([P, HALF, PACK], BF16, "v_01_woven", 49152)
-        weave_into(v_01_woven[:, 0:P, :], v_01[:, :, 0:P], "vector")
-        weave_into(v_01_woven[:, P:, :], v_01[:, :, P:], "scalar")
+        v_01_woven = weave(v_01[:], "scalar", "v_01_woven", 49152)
         dz_woven = [weave(dz_raw[0][:], "vector", "dz_0_woven", 81920)]
         quantise(v_01_woven, v_01_mx, 0, E4M3)
         quantise(dz_woven[0], dz_mx, 0, E5M2)
@@ -215,17 +213,14 @@ def tile_attend_gtied_mom_kernel(tc, V, dz, xT, G, mT, wT, offs, joffs, out_0, o
         quantise(dz_woven[2], dz_mx, HALF, E5M2)
         sums_2 = pair_products(2, 2)
         v_23_woven = weave(v_23[:], "vector", "v_23_woven", 87168)
-        pb_win = [window("pb_win_0", 49152)]
         pair_scatters(1, sums_1, "vector")
-        pair_scatters(2, sums_2, "vector")
         quantise(v_23_woven, v_23_mx, 0, E4M3)
+        pair_scatters(2, sums_2, "vector")
         sums_a = pieces(1, [(v_23_mx, 0, dz_mx, 0, HALF), (v_23_mx, 1, dz_mx, 0, HALF)])
         x_01_pairs = round_x(x_raw[0], "x_01_pairs", 85184)
         turned_01 = bank(3)
         turn_x(x_01_pairs, turned_01)
         x_23_pairs = round_x(x_raw[1], "x_23_pairs", 87168 + 1984)
-        pb_win.append(window("pb_win_1", 57344 + 4032))
-        pb_win.extend([pb_win[1], pb_win[0]])
         turned_23 = bank(4)
         turn_x(x_23_pairs, turned_23)
         da_first = drain("vector", sums_a, SLOTS, 1.0 / DECAY, "da_first")
@@ -244,14 +239,17 @@ def tile_attend_gtied_mom_kernel(tc, V, dz, xT, G, mT, wT, offs, joffs, out_0, o
         sums_x = pieces(0, [(v_23_mx, 0, dz_mx, HALF, SLOTS), (x_01_mx, 0, g_mx, 0, HALF)])
         sums_u = pieces(2, [(v_23_mx, 1, dz_mx, HALF, SLOTS), (x_01_mx, 0, g_mx, HALF, SLOTS)])
         sums_b1 = pieces(5, [(x_01_mx, 1, g_mx, 0, SLOTS)])
-        partial_1 = tile([P, TOKENS], F32, "partial_1", 83200 + 1984)
-        nc.gpsimd.tensor_tensor(out=partial_1[:], in0=m_rows[1][:], in1=pa_win[1][:], op=ADD)
+        early, late = slice(0, EARLY), slice(EARLY, TOKENS)
+        partial_1g = tile([P, EARLY], F32, "partial_1g", 83200 + 1984)
+        nc.gpsimd.tensor_tensor(out=partial_1g[:], in0=m_rows[1][:, early], in1=pa_win[1][:, early], op=ADD)
         x_23_woven = weave_x(turned_23, "x_23_woven", 28672)
         grads_x = drain("vector", sums_x, SLOTS, 1.0 / DECAY, "grads_x")
         grads_u = drain("vector", sums_u, SLOTS, 1.0 / DECAY, "grads_u")
         db_1 = drain("vector", sums_b1, SLOTS, 1.0, "db_1", 16384)
         quantise(x_23_woven, x_23_mx, 0, E4M3)
         nc.vector.tensor_copy(pb_win[1][:].indirect(i_list[:]), db_1[:])
+        partial_1v = tile([P, TOKENS - EARLY], F32, "partial_1v", 28672 + 1984)
+        nc.vector.tensor_tensor(out=partial_1v[:], in0=m_rows[1][:, late], in1=pa_win[1][:, late], op=ADD)
         sums_y = pieces(4, [(x_23_mx, 0, g_mx, 0, HALF), (x_23_mx, 1, g_mx, 0, P)])
         sums_z = pieces(6, [(x_23_mx, 0, g_mx, HALF, SLOTS)])
         sums_w = pieces(7, [(x_23_mx, 1, g_mx, P, HALF), (x_23_mx, 1, g_mx, HALF, SLOTS)])
@@ -269,16 +267,16 @@ def tile_attend_gtied_mom_kernel(tc, V, dz, xT, G, mT, wT, offs, joffs, out_0, o
         whole = slice(0, TOKENS)
         by_gpsimd, by_vector = slice(0, SHARE), slice(SHARE, TOKENS)
 
-        def finish(b, partial):
-            for cols in halves:
-                scale_add(new_m[b][:, cols], partial[:, cols], DECAY, pb_win[b][:, cols])
+        def finish(b, parts):
+            for cols, partial in parts:
+                scale_add(new_m[b][:, cols], partial, DECAY, pb_win[b][:, cols])
             store(out_0, b, new_m[b], whole)
-            for cols in halves:
+            for cols, partial in parts:
                 scale_add(new_w[b][:, cols], new_m[b][:, cols], -RATE, w_rows[b][:, cols])
             store(out_1, b, new_w[b], whole)
 
         db_y = drain("vector", sums_y, HALF + P, 1.0, "db_y", 8192 + 1984)
-        finish(1, partial_1)
+        finish(1, [(early, partial_1g[:]), (late, partial_1v[:])])
 
         partial_2 = tile([P, TOKENS], F32, "partial_2", 32768 + 4032)
         nc.gpsimd.tensor_tensor(out=partial_2[:], in0=m_rows[2][:], in1=pa_win[2][:], op=ADD)
@@ -308,13 +306,15 @@ def tile_attend_gtied_mom_kernel(tc, V, dz, xT, G, mT, wT, offs, joffs, out_0, o
             )
             store(out_1, 0, new_w[0], halves[h])
 
-        finish(2, partial_2)
+        finish(2, [(cols, partial_2[:, cols]) for cols in halves])
 
         partial_3v = tile([P, TOKENS - SHARE], F32, "partial_3v", 32768 + 4032 + 64)
         nc.vector.tensor_tensor(out=partial_3v[:], in0=m_rows[3][:, by_vector], in1=pa_win[3][:, by_vector], op=ADD)
-        for cols, part in ((by_gpsimd, partial_3g), (by_vector, partial_3v)):
-            scale_add(new_m[3][:, cols], part[:], DECAY, pb_win[3][:, cols])
+        middle = 512 - SHARE
+        for cols, part in ((by_gpsimd, partial_3g[:]), (slice(SHARE, 512), partial_3v[:, 0:middle]),
+                           (halves[1], partial_3v[:, middle:])):
+            scale_add(new_m[3][:, cols], part, DECAY, pb_win[3][:, cols])
             store(out_0, 3, new_m[3], cols)
-        for cols in (by_gpsimd, slice(SHARE, 768), slice(768, TOKENS)):
+        for cols in (halves[0], slice(512, 768), slice(768, TOKENS)):
             scale_add(new_w[3][:, cols], new_m[3][:, cols], -RATE, w_rows[3][:, cols])
             store(out_1, 3, new_w[3], cols)

@@ -26,8 +26,7 @@ HALF = 256
 BLOCKS = D // P
 DECAY = 0.9
 RATE = 0.1
-SHARE = 192
-EARLY = 640
+SHARE = 640
 
 FLOPS = 2 * 2 * K * D * SLOTS
 
@@ -239,17 +238,14 @@ def tile_attend_gtied_mom_kernel(tc, V, dz, xT, G, mT, wT, offs, joffs, out_0, o
         sums_x = pieces(0, [(v_23_mx, 0, dz_mx, HALF, SLOTS), (x_01_mx, 0, g_mx, 0, HALF)])
         sums_u = pieces(2, [(v_23_mx, 1, dz_mx, HALF, SLOTS), (x_01_mx, 0, g_mx, HALF, SLOTS)])
         sums_b1 = pieces(5, [(x_01_mx, 1, g_mx, 0, SLOTS)])
-        early, late = slice(0, EARLY), slice(EARLY, TOKENS)
-        partial_1g = tile([P, EARLY], F32, "partial_1g", 83200 + 1984)
-        nc.gpsimd.tensor_tensor(out=partial_1g[:], in0=m_rows[1][:, early], in1=pa_win[1][:, early], op=ADD)
+        partial_1 = tile([P, TOKENS], F32, "partial_1", 83200 + 1984)
+        nc.gpsimd.tensor_tensor(out=partial_1[:], in0=m_rows[1][:], in1=pa_win[1][:], op=ADD)
         x_23_woven = weave_x(turned_23, "x_23_woven", 28672)
         grads_x = drain("vector", sums_x, SLOTS, 1.0 / DECAY, "grads_x")
         grads_u = drain("vector", sums_u, SLOTS, 1.0 / DECAY, "grads_u")
         db_1 = drain("vector", sums_b1, SLOTS, 1.0, "db_1", 16384)
         quantise(x_23_woven, x_23_mx, 0, E4M3)
         nc.vector.tensor_copy(pb_win[1][:].indirect(i_list[:]), db_1[:])
-        partial_1v = tile([P, TOKENS - EARLY], F32, "partial_1v", 28672 + 1984)
-        nc.vector.tensor_tensor(out=partial_1v[:], in0=m_rows[1][:, late], in1=pa_win[1][:, late], op=ADD)
         sums_y = pieces(4, [(x_23_mx, 0, g_mx, 0, HALF), (x_23_mx, 1, g_mx, 0, P)])
         sums_z = pieces(6, [(x_23_mx, 0, g_mx, HALF, SLOTS)])
         sums_w = pieces(7, [(x_23_mx, 1, g_mx, P, HALF), (x_23_mx, 1, g_mx, HALF, SLOTS)])
@@ -276,12 +272,14 @@ def tile_attend_gtied_mom_kernel(tc, V, dz, xT, G, mT, wT, offs, joffs, out_0, o
             store(out_1, b, new_w[b], whole)
 
         db_y = drain("vector", sums_y, HALF + P, 1.0, "db_y", 8192 + 1984)
-        finish(1, [(early, partial_1g[:]), (late, partial_1v[:])])
+        finish(1, [(cols, partial_1[:, cols]) for cols in halves])
 
-        partial_2 = tile([P, TOKENS], F32, "partial_2", 32768 + 4032)
-        nc.gpsimd.tensor_tensor(out=partial_2[:], in0=m_rows[2][:], in1=pa_win[2][:], op=ADD)
-        partial_3g = tile([P, SHARE], F32, "partial_3g", 65536 + 2048 + 4032)
-        nc.gpsimd.tensor_tensor(out=partial_3g[:], in0=m_rows[3][:, by_gpsimd], in1=pa_win[3][:, by_gpsimd], op=ADD)
+        partial_2v = tile([P, TOKENS - SHARE], F32, "partial_2v", 83200 + 1984 + 4032)
+        nc.vector.tensor_tensor(out=partial_2v[:], in0=m_rows[2][:, by_vector], in1=pa_win[2][:, by_vector], op=ADD)
+        partial_2g = tile([P, SHARE], F32, "partial_2g", 32768 + 4032)
+        nc.gpsimd.tensor_tensor(out=partial_2g[:], in0=m_rows[2][:, by_gpsimd], in1=pa_win[2][:, by_gpsimd], op=ADD)
+        partial_3 = tile([P, TOKENS], F32, "partial_3", 65536 + 2048 + 4032)
+        nc.gpsimd.tensor_tensor(out=partial_3[:], in0=m_rows[3][:], in1=pa_win[3][:], op=ADD)
 
         new_m_t = [
             drain("vector", turned[h], SLOTS, DECAY * RATE, "new_m_t_%d" % h, (None, 40960)[h]) for h in range(2)
@@ -306,14 +304,10 @@ def tile_attend_gtied_mom_kernel(tc, V, dz, xT, G, mT, wT, offs, joffs, out_0, o
             )
             store(out_1, 0, new_w[0], halves[h])
 
-        finish(2, [(cols, partial_2[:, cols]) for cols in halves])
+        finish(2, [(by_vector, partial_2v[:]), (by_gpsimd, partial_2g[:])])
 
-        partial_3v = tile([P, TOKENS - SHARE], F32, "partial_3v", 32768 + 4032 + 64)
-        nc.vector.tensor_tensor(out=partial_3v[:], in0=m_rows[3][:, by_vector], in1=pa_win[3][:, by_vector], op=ADD)
-        middle = 512 - SHARE
-        for cols, part in ((by_gpsimd, partial_3g[:]), (slice(SHARE, 512), partial_3v[:, 0:middle]),
-                           (halves[1], partial_3v[:, middle:])):
-            scale_add(new_m[3][:, cols], part, DECAY, pb_win[3][:, cols])
+        for cols in (slice(0, 256), slice(256, 512), halves[1]):
+            scale_add(new_m[3][:, cols], partial_3[:, cols], DECAY, pb_win[3][:, cols])
             store(out_0, 3, new_m[3], cols)
         for cols in (halves[0], slice(512, 768), slice(768, TOKENS)):
             scale_add(new_w[3][:, cols], new_m[3][:, cols], -RATE, w_rows[3][:, cols])

@@ -64,8 +64,8 @@ def tile_attend_gtied_mom_kernel(tc, V, dz, xT, G, mT, wT, offs, joffs, out_0, o
             nc.sync.dma_start(lst[:], src)
             return lst
 
-        def window(name):
-            win = tile([P, TOKENS], F32, name)
+        def window(name, at=None):
+            win = tile([P, TOKENS], F32, name, at)
             nc.vector.memset(win[:].bitcast(I32), 0)
             return win
 
@@ -160,9 +160,8 @@ def tile_attend_gtied_mom_kernel(tc, V, dz, xT, G, mT, wT, offs, joffs, out_0, o
         make_identity(nc, ident[:])
 
         pa_win = [window("pa_win_%d" % n) for n in range(3)]
-        pb_win = [window("pb_win_%d" % n) for n in range(2)]
+        pb_win = [window("pb_win_0")]
         pa_win.append(pa_win[0])
-        pb_win.extend([pb_win[1], pb_win[0]])
 
         dz_mx = mx_operand("dz", SLOTS, 90112 + 4032)
         v_01_mx, x_01_mx, x_23_mx = [mx_operand(n, HALF) for n in ("v_01", "x_01", "x_23")]
@@ -178,10 +177,10 @@ def tile_attend_gtied_mom_kernel(tc, V, dz, xT, G, mT, wT, offs, joffs, out_0, o
                 multiply(v_01_mx, b, dz_mx, c0, c1, sums[:, b * (c1 - c0):(b + 1) * (c1 - c0)])
             return sums
 
-        def pair_scatters(part, sums, engine):
+        def pair_scatters(part, sums):
             c0, c1 = dz_parts[part]
             width = c1 - c0
-            grads = drain(engine, sums, 2 * width, 1.0 / DECAY, "da_01_%d" % part)
+            grads = drain("vector", sums, 2 * width, 1.0 / DECAY, "da_01_%d" % part)
             for b in range(2):
                 scatter_scalar(pa_win[b], j_list, c0, c1, grads[:, b * width:(b + 1) * width])
 
@@ -200,37 +199,44 @@ def tile_attend_gtied_mom_kernel(tc, V, dz, xT, G, mT, wT, offs, joffs, out_0, o
                     nc.tensor.matmul(turned[h][:, q * P:(q + 1) * P], lhsT=addend[:, c:c + P], rhs=unit[:],
                                      start=(opens and q == 0), stop=(closes and q == 3), is_transpose=True)
 
-        v_01_woven = weave(v_01[:], "scalar", "v_01_woven", 49152)
+        v_01_woven = tile([P, HALF, PACK], BF16, "v_01_woven", 49152)
+        weave_into(v_01_woven[:, 0:64, :], v_01[:, :, 0:64], "vector")
+        weave_into(v_01_woven[:, 64:, :], v_01[:, :, 64:], "scalar")
         dz_woven = [weave(dz_raw[0][:], "vector", "dz_0_woven", 81920)]
         quantise(v_01_woven, v_01_mx, 0, E4M3)
         quantise(dz_woven[0], dz_mx, 0, E5M2)
         dz_woven.append(weave(dz_raw[1][:], "scalar", "dz_1_woven", 90112 + 64 - 1024))
-        pair_scatters(0, pair_products(0, 0), "scalar")
-        dz_woven.append(weave(dz_raw[2][:], "vector", "dz_2_woven", 49152 + 64 - 2048))
+        opening = [pieces((0, 7)[b], [(v_01_mx, b, dz_mx, 0, P)]) for b in range(2)]
+        opening = [drain("scalar", opening[b], P, 1.0 / DECAY, "da_0_%d" % b) for b in range(2)]
+        for b in range(2):
+            scatter_scalar(pa_win[b], j_list, 0, P, opening[b][:])
+        pb_win.append(window("pb_win_1", 49152 + 1984))
+        pb_win.extend([pb_win[1], pb_win[0]])
         quantise(dz_woven[1], dz_mx, P, E5M2)
         sums_1 = pair_products(1, 1)
+        dz_woven.append(weave(dz_raw[2][:], "vector", "dz_2_woven", 49152 + 64 - 2048))
+        pair_scatters(1, sums_1)
         quantise(dz_woven[2], dz_mx, HALF, E5M2)
         sums_2 = pair_products(2, 2)
         v_23_woven = weave(v_23[:], "vector", "v_23_woven", 87168)
-        pair_scatters(1, sums_1, "vector")
-        quantise(v_23_woven, v_23_mx, 0, E4M3)
-        pair_scatters(2, sums_2, "vector")
-        sums_a = pieces(1, [(v_23_mx, 0, dz_mx, 0, HALF), (v_23_mx, 1, dz_mx, 0, HALF)])
-        x_01_pairs = round_x(x_raw[0], "x_01_pairs", 85184)
+        x_01_pairs = round_x(x_raw[0], "x_01_pairs", 49152 + 64 - 2048 + 64 - 2048)
         turned_01 = bank(3)
         turn_x(x_01_pairs, turned_01)
+        pair_scatters(2, sums_2)
+        quantise(v_23_woven, v_23_mx, 0, E4M3)
+        sums_a = pieces(1, [(v_23_mx, 0, dz_mx, 0, HALF), (v_23_mx, 1, dz_mx, 0, HALF)])
         x_23_pairs = round_x(x_raw[1], "x_23_pairs", 87168 + 1984)
         turned_23 = bank(4)
         turn_x(x_23_pairs, turned_23)
-        da_first = drain("vector", sums_a, SLOTS, 1.0 / DECAY, "da_first")
         x_01_woven = weave_x(turned_01, "x_01_woven")
+        da_first = drain("vector", sums_a, SLOTS, 1.0 / DECAY, "da_first")
         turned = [bank(3), bank(1)]
         add_turned(pa_win[0], ident, True, False)
         scatter_scalar(pa_win[2], j_list, 0, HALF, da_first[:, first])
         scatter_scalar(pa_win[3], j_list, 0, HALF, da_first[:, second])
         g_woven = [
             weave(g_raw[:, :, cols], "vector", "g_woven_%d" % cols.start, at)
-            for cols, at in ((first, 83200), (second, 83200 + 64 - 2048 - 64))
+            for cols, at in ((first, 45184 + 64 - 2048), (second, 81152))
         ]
         quantise(x_01_woven, x_01_mx, 0, E4M3)
         quantise(g_woven[0], g_mx, 0, E5M2)
@@ -238,7 +244,7 @@ def tile_attend_gtied_mom_kernel(tc, V, dz, xT, G, mT, wT, offs, joffs, out_0, o
         sums_x = pieces(0, [(v_23_mx, 0, dz_mx, HALF, SLOTS), (x_01_mx, 0, g_mx, 0, HALF)])
         sums_u = pieces(2, [(v_23_mx, 1, dz_mx, HALF, SLOTS), (x_01_mx, 0, g_mx, HALF, SLOTS)])
         sums_b1 = pieces(5, [(x_01_mx, 1, g_mx, 0, SLOTS)])
-        partial_1 = tile([P, TOKENS], F32, "partial_1", 83200 + 1984)
+        partial_1 = tile([P, TOKENS], F32, "partial_1", 45184 + 64 - 2048 + 64 - 4096)
         nc.gpsimd.tensor_tensor(out=partial_1[:], in0=m_rows[1][:], in1=pa_win[1][:], op=ADD)
         x_23_woven = weave_x(turned_23, "x_23_woven", 28672)
         grads_x = drain("vector", sums_x, SLOTS, 1.0 / DECAY, "grads_x")
@@ -257,7 +263,7 @@ def tile_attend_gtied_mom_kernel(tc, V, dz, xT, G, mT, wT, offs, joffs, out_0, o
             scatter_scalar(win, j_list, HALF, SLOTS, grads[:, first])
         add_turned(pb_win[0], ident_late, False, True)
 
-        places = (None, None, 40960 + 1984, None)
+        places = (None, None, 57344 + 1984, None)
         new_m = [tile([P, TOKENS], F32, "new_m_%d" % b, places[b]) for b in range(BLOCKS)]
         new_w = [tile([P, TOKENS], F32, "new_w_%d" % b) for b in range(BLOCKS)]
         whole = slice(0, TOKENS)
@@ -274,15 +280,15 @@ def tile_attend_gtied_mom_kernel(tc, V, dz, xT, G, mT, wT, offs, joffs, out_0, o
         db_y = drain("vector", sums_y, HALF + P, 1.0, "db_y", 8192 + 1984)
         finish(1, [(cols, partial_1[:, cols]) for cols in halves])
 
-        partial_2v = tile([P, TOKENS - SHARE], F32, "partial_2v", 83200 + 1984 + 4032)
+        partial_2v = tile([P, TOKENS - SHARE], F32, "partial_2v", 39168 + 64 - 4 * (TOKENS - SHARE))
         nc.vector.tensor_tensor(out=partial_2v[:], in0=m_rows[2][:, by_vector], in1=pa_win[2][:, by_vector], op=ADD)
-        partial_2g = tile([P, SHARE], F32, "partial_2g", 32768 + 4032)
+        partial_2g = tile([P, SHARE], F32, "partial_2g", 32768 + 64 - 4 * SHARE)
         nc.gpsimd.tensor_tensor(out=partial_2g[:], in0=m_rows[2][:, by_gpsimd], in1=pa_win[2][:, by_gpsimd], op=ADD)
         partial_3 = tile([P, TOKENS], F32, "partial_3", 65536 + 2048 + 4032)
         nc.gpsimd.tensor_tensor(out=partial_3[:], in0=m_rows[3][:], in1=pa_win[3][:], op=ADD)
 
         new_m_t = [
-            drain("vector", turned[h], SLOTS, DECAY * RATE, "new_m_t_%d" % h, (None, 40960)[h]) for h in range(2)
+            drain("vector", turned[h], SLOTS, DECAY * RATE, "new_m_t_%d" % h, (None, 57344)[h]) for h in range(2)
         ]
         db_z = drain("vector", sums_z, HALF, 1.0, "db_z", 28672 + 448)
         db_w = drain("vector", sums_w, P + HALF, 1.0, "db_w", 28672 + 64 - 4 * (P + HALF))
@@ -306,9 +312,9 @@ def tile_attend_gtied_mom_kernel(tc, V, dz, xT, G, mT, wT, offs, joffs, out_0, o
 
         finish(2, [(by_vector, partial_2v[:]), (by_gpsimd, partial_2g[:])])
 
-        for cols in (slice(0, 256), slice(256, 512), halves[1]):
+        for cols in (slice(0, 384), slice(384, TOKENS)):
             scale_add(new_m[3][:, cols], partial_3[:, cols], DECAY, pb_win[3][:, cols])
             store(out_0, 3, new_m[3], cols)
-        for cols in (halves[0], slice(512, 768), slice(768, TOKENS)):
+        for cols in (slice(0, 384), slice(384, 768), slice(768, TOKENS)):
             scale_add(new_w[3][:, cols], new_m[3][:, cols], -RATE, w_rows[3][:, cols])
             store(out_1, 3, new_w[3], cols)

from contextlib import ExitStack

import concourse.mybir as mybir
from concourse.masks import make_identity

F32 = mybir.dt.float32
BF16 = mybir.dt.bfloat16
I32 = mybir.dt.int32
U32 = mybir.dt.uint32
U16 = mybir.dt.uint16
U8 = mybir.dt.uint8
E4M3 = mybir.dt.float8_e4m3fn_x4
E5M2 = mybir.dt.float8_e5m2_x4
COPY = mybir.ActivationFunctionType.Copy
MULT = mybir.AluOpType.mult
ADD = mybir.AluOpType.add
SUBTRACT = mybir.AluOpType.subtract

P = 128
PACK = 4
K = 512
D = 512
SLOTS = 512
TOKENS = 1024
HALF = 256
BLOCKS = D // P
DECAY = 0.9
RATE = 0.1
SHARE = 640

FLOPS = 2 * 2 * K * D * SLOTS


def tile_attend_gtied_mom_kernel(tc, V, dz, xT, G, mT, wT, offs, joffs, out_0, out_1):
    nc = tc.nc
    with ExitStack() as ctx:
        keep = ctx.enter_context(tc.tile_pool(name="keep", bufs=1))
        reuse = ctx.enter_context(tc.tile_pool(name="reuse", bufs=1))
        psum = ctx.enter_context(tc.psum_pool(name="psum", bufs=1))

        def tile(shape, dtype, name, at=None):
            if at is None:
                return keep.tile(shape, dtype, name=name, align_bytes=64)
            return reuse.tile(shape, dtype, name=name, offset=at, align_bytes=64)

        def load_k_first(src, c0, c1, name, at=None):
            raw = tile([P, PACK, c1 - c0], F32, name, at)
            nc.sync.dma_start(out=raw[:], in_=src.rearrange("(p j) n -> p j n", j=PACK)[:, :, c0:c1])
            return raw

        def load_rows(src, b, name, at=None):
            raw = tile([P, TOKENS], F32, name, at)
            nc.sync.dma_start(out=raw[:], in_=src[b * P:(b + 1) * P, :])
            return raw

        def load_x(pair):
            raw = tile([P, 2, K], F32, "x_%d" % pair)
            rows = xT[pair * HALF:(pair + 1) * HALF, :]
            nc.sync.dma_start(out=raw[:], in_=rows.rearrange("(n d) r -> d n r", n=2))
            return raw

        def load_list(src, name):
            lst = keep.tile([P, SLOTS // 16], U16, name=name)
            nc.sync.dma_start(lst[:], src)
            return lst

        def window(name, at=None):
            win = tile([P, TOKENS], F32, name, at)
            nc.vector.memset(win[:].bitcast(I32), 0)
            return win

        def mx_operand(name, width, at=None):
            return tile([P, width], U32, name + "_codes", at), tile([P, width], U8, name + "_scales")

        def weave_into(woven, raw, engine):
            dst = woven.rearrange("p (c i) t -> p c t i", i=4)
            src = raw.rearrange("p t (c i) -> p c t i", i=4)
            if engine == "vector":
                nc.vector.tensor_copy(out=dst, in_=src)
            else:
                nc.scalar.activation(out=dst, in_=src, func=COPY)

        def weave(raw, engine, name, at=None):
            woven = tile([P, raw.shape[2], PACK], BF16, name, at)
            weave_into(woven[:], raw, engine)
            return woven

        def quantise(woven, operand, c0, fmt):
            codes, scales = operand
            cols = slice(c0, c0 + woven.shape[1])
            nc.vector.quantize_mx(
                out=codes[:, cols].bitcast(fmt),
                scales=scales[:, cols],
                in_=woven[:].rearrange("p n t -> p (n t)"),
            )

        def bank(n):
            return psum.tile([P, SLOTS], F32, name="bank_%d" % n, tag="bank_%d" % n)

        def round_x(raw, name, at=None):
            pairs = tile([P, 2, 2, P, 2], BF16, name, at)
            nc.vector.tensor_copy(out=pairs[:], in_=raw[:].rearrange("d n (p u e) -> d n u p e", u=2, e=2))
            return pairs

        def turn_x(pairs, turned):
            words = pairs[:].rearrange("d n u p e -> d (n u p e)").bitcast(F32)
            for q in range(4):
                nc.tensor.transpose(turned[:, q * P:(q + 1) * P], words[:, q * P:(q + 1) * P], ident[:])

        def weave_x(turned, name, at=None):
            woven = tile([P, HALF, PACK], BF16, name, at)
            dst = woven[:].rearrange("p d t -> p (d t)").bitcast(F32).rearrange("p (n d u) -> p n d u", n=2, u=2)
            nc.vector.tensor_copy(out=dst, in_=turned[:].rearrange("p (n u d) -> p n d u", n=2, u=2))
            return woven

        def multiply(stationary, n, moving, c0, c1, sums):
            cols = slice(n * P, (n + 1) * P)
            nc.tensor.matmul_mx(
                out=sums,
                lhsT=stationary[0][:, cols].bitcast(E4M3),
                lhsT_scale=stationary[1][:, cols],
                rhs=moving[0][:, c0:c1].bitcast(E5M2),
                rhs_scale=moving[1][:, c0:c1],
                start=True,
                stop=True,
            )

        def drain(engine, sums, width, scale, name, at=None):
            grad = tile([P, width], F32, name, at)
            if engine == "vector":
                nc.vector.tensor_scalar(out=grad[:], in0=sums[:, 0:width], scalar1=scale, scalar2=None, op0=MULT)
            else:
                nc.scalar.activation(out=grad[:], in_=sums[:, 0:width], func=COPY, scale=scale)
            return grad

        def scatter_scalar(win, lst, s0, s1, grad, scale=1.0):
            nc.scalar.activation(out=win[:].indirect(lst[:, s0 // 16:s1 // 16]), in_=grad, func=COPY, scale=scale)

        def scale_add(dst, src, factor, other):
            nc.vector.scalar_tensor_tensor(out=dst, in0=src, scalar=factor, in1=other, op0=MULT, op1=ADD)

        def store(dst, b, src, cols):
            nc.sync.dma_start(out=dst[b * P:(b + 1) * P, cols], in_=src[:, cols])

        v_01 = load_k_first(V, 0, HALF, "v_01", 90112)
        dz_parts = [(0, P), (P, HALF), (HALF, SLOTS)]
        dz_raw = [load_k_first(dz, 0, P, "dz_0")]
        j_list = load_list(joffs, "j_list")
        dz_raw.extend(load_k_first(dz, c0, c1, "dz_%d" % c0) for c0, c1 in dz_parts[1:])
        v_23 = load_k_first(V, HALF, D, "v_23")
        x_raw = [load_x(0), load_x(1)]
        g_raw = load_k_first(G, 0, SLOTS, "g", 28672 + 64 - 8192)
        i_list = load_list(offs, "i_list")
        m_rows, w_rows = {}, {}
        for rows, src, name, b in ((m_rows, mT, "m", 1), (m_rows, mT, "m", 0), (w_rows, wT, "w", 1), (m_rows, mT, "m", 2),
                                   (m_rows, mT, "m", 3), (w_rows, wT, "w", 0), (w_rows, wT, "w", 2), (w_rows, wT, "w", 3)):
            rows[b] = load_rows(src, b, "%s_%d" % (name, b), {("w", 1): 32768, ("m", 2): 65536 + 2048}.get((name, b)))

        ident = keep.tile([P, P], F32, name="ident")
        make_identity(nc, ident[:])

        pa_win = [window("pa_win_%d" % n) for n in range(3)]
        pb_win = [window("pb_win_0")]
        pa_win.append(pa_win[0])

        dz_mx = mx_operand("dz", SLOTS, 90112 + 4032)
        v_01_mx, x_01_mx, x_23_mx = [mx_operand(n, HALF) for n in ("v_01", "x_01", "x_23")]
        v_23_mx = mx_operand("v_23", HALF)
        g_mx = mx_operand("g", SLOTS, 8192)
        first, second = slice(0, HALF), slice(HALF, SLOTS)
        halves = [slice(0, 512), slice(512, TOKENS)]

        def pair_products(part, n_bank):
            c0, c1 = dz_parts[part]
            sums = bank(n_bank)
            for b in range(2):
                multiply(v_01_mx, b, dz_mx, c0, c1, sums[:, b * (c1 - c0):(b + 1) * (c1 - c0)])
            return sums

        def pair_scatters(part, sums):
            c0, c1 = dz_parts[part]
            width = c1 - c0
            grads = drain("vector", sums, 2 * width, 1.0 / DECAY, "da_01_%d" % part)
            for b in range(2):
                scatter_scalar(pa_win[b], j_list, c0, c1, grads[:, b * width:(b + 1) * width])

        def pieces(n_bank, parts):
            sums = bank(n_bank)
            at = 0
            for stationary, n, moving, c0, c1 in parts:
                multiply(stationary, n, moving, c0, c1, sums[:, at:at + c1 - c0])
                at = at + c1 - c0
            return sums

        def add_turned(addend, unit, opens, closes):
            for h in range(2):
                for q in range(4):
                    c = (4 * h + q) * P
                    nc.tensor.matmul(turned[h][:, q * P:(q + 1) * P], lhsT=addend[:, c:c + P], rhs=unit[:],
                                     start=(opens and q == 0), stop=(closes and q == 3), is_transpose=True)

        v_01_woven = tile([P, HALF, PACK], BF16, "v_01_woven", 49152)
        weave_into(v_01_woven[:, 0:64, :], v_01[:, :, 0:64], "vector")
        weave_into(v_01_woven[:, 64:, :], v_01[:, :, 64:], "scalar")
        dz_woven = [weave(dz_raw[0][:], "vector", "dz_0_woven", 81920)]
        quantise(v_01_woven, v_01_mx, 0, E4M3)
        quantise(dz_woven[0], dz_mx, 0, E5M2)
        dz_woven.append(weave(dz_raw[1][:], "scalar", "dz_1_woven", 90112 + 64 - 1024))
        opening = [pieces((0, 7)[b], [(v_01_mx, b, dz_mx, 0, P)]) for b in range(2)]
        opening = [drain("scalar", opening[b], P, 1.0 / DECAY, "da_0_%d" % b) for b in range(2)]
        for b in range(2):
            scatter_scalar(pa_win[b], j_list, 0, P, opening[b][:])
        pb_win.append(window("pb_win_1", 49152 + 1984))
        pb_win.extend([pb_win[1], pb_win[0]])
        quantise(dz_woven[1], dz_mx, P, E5M2)
        sums_1 = pair_products(1, 1)
        dz_woven.append(weave(dz_raw[2][:], "vector", "dz_2_woven", 49152 + 64 - 2048))
        pair_scatters(1, sums_1)
        quantise(dz_woven[2], dz_mx, HALF, E5M2)
        sums_2 = pair_products(2, 2)
        v_23_woven = weave(v_23[:], "vector", "v_23_woven", 87168)
        x_01_pairs = round_x(x_raw[0], "x_01_pairs", 49152 + 64 - 2048 + 64 - 2048)
        turned_01 = bank(3)
        turn_x(x_01_pairs, turned_01)
        pair_scatters(2, sums_2)
        quantise(v_23_woven, v_23_mx, 0, E4M3)
        sums_a = pieces(1, [(v_23_mx, 0, dz_mx, 0, HALF), (v_23_mx, 1, dz_mx, 0, HALF)])
        x_23_pairs = round_x(x_raw[1], "x_23_pairs", 87168 + 1984)
        turned_23 = bank(4)
        turn_x(x_23_pairs, turned_23)
        x_01_woven = weave_x(turned_01, "x_01_woven")
        da_first = drain("vector", sums_a, SLOTS, 1.0 / DECAY, "da_first")
        turned = [bank(3), bank(1)]
        add_turned(pa_win[0], ident, True, False)
        scatter_scalar(pa_win[2], j_list, 0, HALF, da_first[:, first])
        scatter_scalar(pa_win[3], j_list, 0, HALF, da_first[:, second])
        g_woven = [
            weave(g_raw[:, :, cols], "vector", "g_woven_%d" % cols.start, at)
            for cols, at in ((first, 45184 + 64 - 2048), (second, 81152))
        ]
        quantise(x_01_woven, x_01_mx, 0, E4M3)
        quantise(g_woven[0], g_mx, 0, E5M2)
        quantise(g_woven[1], g_mx, HALF, E5M2)
        sums_x = pieces(0, [(v_23_mx, 0, dz_mx, HALF, SLOTS), (x_01_mx, 0, g_mx, 0, HALF)])
        sums_u = pieces(2, [(v_23_mx, 1, dz_mx, HALF, SLOTS), (x_01_mx, 0, g_mx, HALF, SLOTS)])
        sums_b1 = pieces(5, [(x_01_mx, 1, g_mx, 0, SLOTS)])
        partial_1 = tile([P, TOKENS], F32, "partial_1", 45184 + 64 - 2048 + 64 - 4096)
        nc.gpsimd.tensor_tensor(out=partial_1[:], in0=m_rows[1][:], in1=pa_win[1][:], op=ADD)
        x_23_woven = weave_x(turned_23, "x_23_woven", 28672)
        grads_x = drain("vector", sums_x, SLOTS, 1.0 / DECAY, "grads_x")
        grads_u = drain("vector", sums_u, SLOTS, 1.0 / DECAY, "grads_u")
        db_1 = drain("vector", sums_b1, SLOTS, 1.0, "db_1", 16384)
        quantise(x_23_woven, x_23_mx, 0, E4M3)
        nc.vector.tensor_copy(pb_win[1][:].indirect(i_list[:]), db_1[:])
        sums_y = pieces(4, [(x_23_mx, 0, g_mx, 0, HALF), (x_23_mx, 1, g_mx, 0, P)])
        sums_z = pieces(6, [(x_23_mx, 0, g_mx, HALF, SLOTS)])
        sums_w = pieces(7, [(x_23_mx, 1, g_mx, P, HALF), (x_23_mx, 1, g_mx, HALF, SLOTS)])
        ident_late = tile([P, P], F32, "ident_late", 28672)
        nc.vector.tensor_copy(out=ident_late[:], in_=ident[:])
        add_turned(m_rows[0], ident_late, False, False)
        for cols, grads, win in ((first, grads_x, pa_win[2]), (second, grads_u, pa_win[3])):
            scatter_scalar(pb_win[0], i_list, cols.start, cols.stop, grads[:, second])
            scatter_scalar(win, j_list, HALF, SLOTS, grads[:, first])
        add_turned(pb_win[0], ident_late, False, True)

        places = (None, None, 57344 + 1984, None)
        new_m = [tile([P, TOKENS], F32, "new_m_%d" % b, places[b]) for b in range(BLOCKS)]
        new_w = [tile([P, TOKENS], F32, "new_w_%d" % b) for b in range(BLOCKS)]
        whole = slice(0, TOKENS)
        by_gpsimd, by_vector = slice(0, SHARE), slice(SHARE, TOKENS)

        def finish(b, parts):
            for cols, partial in parts:
                scale_add(new_m[b][:, cols], partial, DECAY, pb_win[b][:, cols])
            store(out_0, b, new_m[b], whole)
            for cols, partial in parts:
                scale_add(new_w[b][:, cols], new_m[b][:, cols], -RATE, w_rows[b][:, cols])
            store(out_1, b, new_w[b], whole)

        db_y = drain("vector", sums_y, HALF + P, 1.0, "db_y", 8192 + 1984)
        finish(1, [(cols, partial_1[:, cols]) for cols in halves])

        partial_2v = tile([P, TOKENS - SHARE], F32, "partial_2v", 39168 + 64 - 4 * (TOKENS - SHARE))
        nc.vector.tensor_tensor(out=partial_2v[:], in0=m_rows[2][:, by_vector], in1=pa_win[2][:, by_vector], op=ADD)
        partial_2g = tile([P, SHARE], F32, "partial_2g", 32768 + 64 - 4 * SHARE)
        nc.gpsimd.tensor_tensor(out=partial_2g[:], in0=m_rows[2][:, by_gpsimd], in1=pa_win[2][:, by_gpsimd], op=ADD)
        partial_3 = tile([P, TOKENS], F32, "partial_3", 65536 + 2048 + 4032)
        nc.gpsimd.tensor_tensor(out=partial_3[:], in0=m_rows[3][:], in1=pa_win[3][:], op=ADD)

        new_m_t = [
            drain("vector", turned[h], SLOTS, DECAY * RATE, "new_m_t_%d" % h, (None, 57344)[h]) for h in range(2)
        ]
        db_z = drain("vector", sums_z, HALF, 1.0, "db_z", 28672 + 448)
        db_w = drain("vector", sums_w, P + HALF, 1.0, "db_w", 28672 + 64 - 4 * (P + HALF))
        scatter_scalar(pb_win[2], i_list, 0, HALF, db_y[:, first])
        scatter_scalar(pb_win[3], i_list, 0, P, db_y[:, HALF:])
        scatter_scalar(pb_win[2], i_list, HALF, SLOTS, db_z[:])
        scatter_scalar(pb_win[3], i_list, P, SLOTS, db_w[:])

        for h in range(2):
            back = bank(2 * h)
            for q in range(4):
                nc.tensor.transpose(back[:, q * P:(q + 1) * P], new_m_t[h][:, q * P:(q + 1) * P], ident[:])
            nc.vector.tensor_scalar(
                out=new_m[0][:, halves[h]], in0=back[:], scalar1=1.0 / RATE, scalar2=None, op0=MULT
            )
            store(out_0, 0, new_m[0], halves[h])
            nc.vector.tensor_tensor(
                out=new_w[0][:, halves[h]], in0=w_rows[0][:, halves[h]], in1=back[:], op=SUBTRACT
            )
            store(out_1, 0, new_w[0], halves[h])

        finish(2, [(by_vector, partial_2v[:]), (by_gpsimd, partial_2g[:])])

        for cols in (slice(0, 384), slice(384, TOKENS)):
            scale_add(new_m[3][:, cols], partial_3[:, cols], DECAY, pb_win[3][:, cols])
            store(out_0, 3, new_m[3], cols)
        for cols in (slice(0, 384), slice(384, 768), slice(768, TOKENS)):
            scale_add(new_w[3][:, cols], new_m[3][:, cols], -RATE, w_rows[3][:, cols])
            store(out_1, 3, new_w[3], cols)
